import numpy as np, ml_dtypes
CORES = [48,51,52,55]
N = 4
BF = ml_dtypes.bfloat16
def gentries(a):
    return np.ascontiguousarray(a.reshape(8, 16, -1).transpose(0, 2, 1)).reshape(8, -1)
def gtable(e):
    e = np.asarray(e); return np.ascontiguousarray(e.reshape(8, -1, 16).transpose(0, 2, 1)).reshape(128, -1).astype(np.int32)
V, C, L, R = 1536, 8192, 128, 4
F, MX, TOP = 16 * N, 31248 * N, 2 ** 22 - 1
def parents(rng):
    p = np.zeros((8, V), np.int64); o = rng.permutation(8)
    for g in range(8):
        m = (V >> 4, V >> 3, V >> 2, V >> 1)[int(o[g]) % 4]; pool = rng.permutation(V)[:m]
        p[g] = pool[rng.integers(0, m, V)]; p[g, pool[0]] = pool[0]
    return p
def parts(rng):
    x = rng.integers(-31, 32, (8, F, V)); k = rng.integers(-63, 64, (8, F, C))
    b = np.where(rng.random((8, C)) < 0.2, rng.integers(-MX, MX + 1, (8, C)), rng.integers(-4096, 4097, (8, C)))
    w = np.where(rng.random((8, C)) < 0.25, 1000 * rng.integers(0, 4, (8, C)), rng.integers(0, TOP + 1, (8, C)))
    d = rng.integers(0, C, (8, 16, V)); one = rng.random((8, 1, V)) < 0.15
    return x, k, b, w, np.where(one, d[:, :1], d), parents(rng)
def pack(x, k, b, w, d, p):
    def deal(a): return np.ascontiguousarray(a.reshape(8, N, 16, -1).transpose(1, 0, 2, 3)).reshape(N, 128, -1).astype(np.float32).astype(BF)
    def same(a): return np.stack([np.ascontiguousarray(a).astype(np.int32)] * N)
    return {"xv": deal(x), "kc": deal(k), "bt": same(b), "co": same(w), "cd": same(d.reshape(128, V)), "pa": same(gtable(p))}
def sides(x, k, b, g, c, plus, minus):
    k[g, 0, c] = 63; b[g, c] = 0
    for s, v in ((1, plus), (-1, minus)):
        a = x[g][:, v]; r = np.add.reduce(k[g, 1:, c][:, None] * a[1:], axis=0)
        a = np.where(r * s < 0, -a, a); a[0] = s * np.maximum(np.abs(a[0]), 1); x[g][:, v] = a
def setup_inputs(rng):
    return pack(*parts(rng))
def setup_inputs_corners(rng):
    x, k, b, w, d, p = parts(rng); v = np.arange(V)
    b[:, 0] = MX; b[:, C - 1] = -MX; w[:, 0] = 0; w[:, C - 1] = 0
    u = rng.integers(0, 5, (8, 1, V)); dead = (C - 1) * rng.integers(0, 2, (8, 16, V)); n = np.arange(16)[None, :, None]
    d = np.where(((u == 0) & (n < 15)) | ((u == 1) & (n > 0)) | ((u == 2) & (n >= 0)), dead, d)
    d[:, :, 0] = rng.integers(1, C - 1, (8, 16)); d[:, :, V - 1] = rng.integers(1, C - 1, (8, 16))
    t = L * np.arange(R); edge = np.unique(np.maximum(np.concatenate([t - 1, t, t + L - 1, t + L]), 0))
    shapes = [np.where(rng.random(V) < 0.5, v, p[0]), (v + L) % V, np.maximum(v - 1, 0), np.full(V, V - 1), np.where(v == V - 1, v, 0), edge[rng.integers(0, len(edge), V)], V - 1 - v, (v + 1) % V]
    o = rng.permutation(8); cut = rng.integers(1, C - 1, 8)
    for g, a in zip(o, shapes): p[g] = a
    g, c = int(o[0]), int(cut[0]); m = np.arange(16); i = L * (R - 2) + m; s = V - 17 + m; e = R * L + m
    p[g] = np.where(np.isin(p[g], np.concatenate([i, s, e])), V - 1, p[g])
    p[g, L * (R - 1):L * R] = v[L * (R - 1):L * R]; p[g, i] = s; p[g, s] = e
    sides(x, k, b, g, c, np.concatenate([i, e]), s); d[g, 0, s] = c; w[g, c] = 0
    g, c = int(o[3]), int(cut[3]); sides(x, k, b, g, c, v[:V - 1], v[V - 1:]); d[g, 0, V - 1] = c; w[g, c] = 0
    g, c = int(o[6]), int(cut[6]); i = np.arange(R * L); sides(x, k, b, g, c, i, V - 1 - i); d[g, rng.integers(0, 16, R * L), V - 1 - i] = c
    for r in range(1, R, 2):
        q = L * r + int(rng.integers(0, L)); p[g, q] = q
    g, c = int(o[7]), int(cut[7]); q = L * np.arange(1, R); sides(x, k, b, g, c, np.concatenate([q - 1, q + 1]), q)
    d[g, 0, q] = c; d[g, 0, q - 1] = c; d[g, :, q - 2] = 0; w[g, c] = 0
    return pack(x, k, b, w, d, p)
def setup_inputs_crowd(rng):
    x, k, b, w, d, p = parts(rng); o = rng.permutation(8)
    for n in range(8):
        g = int(o[n]); big = V - 1 - n
        p[g, :R * L] = big; rest = rng.random(V - R * L) < 0.5; p[g, R * L:] = np.where(rest, big, p[g, R * L:])
        if n % 4 == 2: p[g, 1:R * L:2] = V - 10
        if n % 2 == 1:
            for t in range(R): p[g, L * t + (0, L - 1, int(rng.integers(1, L - 1)))[(n // 2 + t) % 3]] = V - 20 - t
        if n < 2: b[g, 0] = MX; d[g, :, big] = 0
        elif n < 4: d[g, :, big] = d[g, 0, big]
    return pack(x, k, b, w, d, p)
def setup_inputs_ends(rng):
    x, k, b, w, d, p = parts(rng); h = 2 * rng.integers(0, 2, (8, F, 1)) - 1; h0 = h[:, :, 0]
    def signs(n):
        u = rng.integers(0, 3, (8, 1, n)); z = 2 * rng.integers(0, 2, (8, F, n)) - 1
        return np.where(u == 0, h, np.where(u == 1, -h, z))
    a, q = signs(V), signs(C); q[:, :, C - 1] = h0; q[:, :, 0] = -h0
    q[:, :, [C - 3, C - 2]] = h; q[:, :, [1, 2]] = -h
    a[:, :, V - 1] = h0 * (1 - 2 * (np.arange(8)[:, None] & 1)); a[:, :, 0] = -a[:, :, V - 1]
    b = np.where(rng.random((8, C)) < 0.7, MX * (2 * rng.integers(0, 2, (8, C)) - 1), rng.integers(-6000, 6001, (8, C))); b[:, 0] = -MX; b[:, C - 1] = -MX
    b[:, 1] = -MX; b[:, 2] = 1 - MX; b[:, C - 3] = MX - 32; b[:, C - 2] = MX - 1
    share = np.where(np.arange(8) % 2 == 1, 0.92, 0.5)[:, None]; w = np.where(rng.random((8, C)) < share, TOP, 0)
    w = np.where(rng.random((8, C)) < 0.15, np.abs(w - rng.integers(0, 4, (8, C))), w); w[1::2, 0] = TOP; w[::2, 0] = 0; w[:, C - 1] = TOP
    d = np.where(rng.random(d.shape) < 0.7, (C - 1) * rng.integers(0, 2, d.shape), d)
    p = np.where(rng.random(p.shape) < 0.68, (V - 1) * rng.integers(0, 2, p.shape), p)
    p = np.where((p >= V - 1 - 4 * R) & (p < V - 1), V - 1, p)
    for t in range(R):
        i, s = L * t + L - 1, V - 2 - t; p[:, i] = s; a[:, :, i] = h0; a[:, :, s] = -h0
    x = 31 * a
    for t in range(R):
        for n, c in enumerate(([C - 2], [1, 2], [1, 2, C - 3, C - 2])):
            i, s, f = L * t + L - 2 - n, V - 2 - R - 3 * t - n, int(rng.integers(0, F)); p[:, i] = s
            x[:, :, i] = 31 * h0; x[:, f, i] = 30 * h0[:, f]; x[:, :, s] = 31 * h0
            d[:, :, s] = np.array(c)[rng.integers(0, len(c), (8, 16))]
    return pack(x, 63 * q, b, w, d, p)
def setup_inputs_spread(rng):
    x, k, b, w, d, p = parts(rng)
    x = np.rint(x * np.exp2(-rng.integers(0, 5, (8, 1, V)).astype(np.float64))) * (rng.random((8, 1, V)) > 0.0625)
    k = np.rint(k * np.exp2(-rng.integers(0, 6, (8, 1, C)).astype(np.float64)))
    b = np.clip((np.exp2(17 * rng.random((8, C)))).astype(np.int64) * (2 * rng.integers(0, 2, (8, C)) - 1), -MX, MX)
    w = np.exp2(22 * rng.random((8, C))).astype(np.int64) - 1
    d = np.minimum((C * rng.random(d.shape) ** 2).astype(np.int64), C - 1)
    for g in range(8): p[g] = rng.permutation(V)[np.minimum((V * rng.random(V) ** 3).astype(np.int64), V - 1)]
    return pack(x, k, b, w, d, p)
def setup_inputs_ties(rng):
    x, k, b, w, d, p = parts(rng); i = np.arange(R * L)
    x[::2] = rng.integers(-1, 2, (4, F, V)); k[::2] = rng.integers(-1, 2, (4, F, C)); b[::2] = rng.integers(-3, 4, (4, C))
    w = np.array([0, 1, TOP - 1, TOP])[rng.integers(0, 4, (8, C))]; w[1::4] = TOP - rng.integers(0, 2, (2, C)); w[2::4] = TOP - rng.integers(0, 2, (2, C))
    for g in (1, 3, 5, 7):
        s = p[g, i]; c = d[g][:, s]; own = np.where(rng.random(c.shape) < 0.5, i[None, :], s[None, :])
        z = np.einsum("fkl,fkl->kl", k[g][:, c], x[g][:, own])
        b[g, c] = np.clip(z + rng.integers(-1, 2, c.shape), -MX, MX)
    return pack(x, k, b, w, d, p)
def check_inputs(d):
    bad = []
    for k, lo, hi in (("xv", -31, 31), ("kc", -63, 63), ("bt", -MX, MX), ("co", 0, TOP), ("cd", 0, C - 1), ("pa", 0, V - 1)):
        a = np.asarray(d[k]).astype(np.float64)
        if not (np.min(a) >= lo and np.max(a) <= hi): bad.append("range of " + k)
        if k in ("xv", "kc") and not np.all(a == np.floor(a)): bad.append("whole numbers in " + k)
        if k not in ("xv", "kc") and not np.all(a == a[:1]): bad.append(k + " alike on all ranks")
    return bad
def reference(xv, kc, bt, co, cd, pa):
    x = np.ascontiguousarray(xv.astype(np.float32).reshape(N, 8, 16, V).transpose(1, 0, 2, 3)).reshape(8, F, V)
    k = np.ascontiguousarray(kc.astype(np.float32).reshape(N, 8, 16, C).transpose(1, 0, 2, 3)).reshape(8, F, C)
    b = bt[0].astype(np.int64); w = co[0].astype(np.int64); d = cd[0].astype(np.int64).reshape(8, 16, V); p = gentries(pa[0]).astype(np.int64)
    yc = np.full((8, R * L), -1, np.int64)
    for rnd in range(R):
        lane = np.arange(L * rnd, L * rnd + L); new = np.array(p)
        for g in range(8):
            s = p[g, lane]; c = d[g][:, s]; kp = k[g][:, c]
            si = np.einsum("fkl,fl->kl", kp, x[g][:, lane]) > b[g][c]; ss = np.einsum("fkl,fl->kl", kp, x[g][:, s]) > b[g][c]
            apart = si != ss
            first = np.zeros(L, bool); first[np.unique(s, return_index=True)[1]] = True
            act = first & ((s < lane[0]) | (s > lane[-1])) & np.any(apart, axis=0)
            best = np.argmin(np.where(apart, w[g][c], 2 ** 24), axis=0)
            a = np.nonzero(act)[0]; i = lane[a]; sa = s[a]; ca = c[best[a], a]; side = si[best[a], a]
            yc[g, i] = w[g][ca]
            who = np.full(V, -1, np.int64); who[sa] = np.arange(len(a))
            u = who[p[g]]; j = np.nonzero(u >= 0)[0]; u = u[j]; cj = ca[u]
            sj = np.einsum("fj,fj->j", k[g][:, cj], x[g][:, j]) > b[g][cj]
            m = (sj == side[u]) & (j != i[u]); new[g, j[m]] = i[u[m]]
            up = p[g, sa]; o = (np.einsum("fj,fj->j", k[g][:, ca], x[g][:, up]) > b[g][ca]) == side
            new[g, i[o]] = up[o]; new[g, sa[o]] = i[o]
        p = new
    return {"yp": np.stack([gtable(p)] * N).astype(np.float32), "yc": np.stack([gtable(yc)] * N).astype(np.float32)}

@@ -1,0 +1,619 @@
+from concourse.bass import DstId, RemoteDMATransfer
+from concourse.mybir import AluOpType, AxisListType, ActivationFunctionType
+
+V, C, L, R = 1536, 8192, 128, 4
+BF, F32, F16, I32, U16 = "bfloat16", "float32", "float16", "int32", "uint16"
+WID = {
+    "kcs": (C, BF), "dig": (C, BF), "xs": (V, BF), "cds": (V, I32), "btc": (1024, I32), "dg5": (2560, BF),
+    "pa32": (96, I32), "io256": (V, F32), "lo": (256, BF), "pi": (8, I32), "pj": (8, I32), "cf": (24, F32),
+    "Z": (144, BF), "Z2": (144, BF), "Z3": (144, BF), "Sel": (24, BF), "M16": (16, BF), "M16x": (V, BF),
+    "fst": (16, F32), "idt": (128, BF), "m3": (8, F32), "D1b": (32, F32),
+    "tiny": (48, BF), "hic": (32, F32), "Perm": (128, F32), "laneW": (8, F32), "dumpW": (8, F32), "lane1": (8, F32),
+    "XM": (4 * 2048, BF), "Kg": (2048, BF), "Dg": (512, BF), "xsg": (128, BF), "cU": (128, U16),
+    "sU": (32, U16), "sF": (8, F32), "pU": (4 * 96, U16), "pF": (96, F32),
+    "SA": (4 * 192, U16), "LA": (4 * 192, U16), "fA": (192, F32), "uA": (64, F32), "rest": (64, F32),
+    "side": (64, F32), "kp": (96, F32), "kpT": (96, F32), "negc": (32, F32), "pay": (32, F32), "s8": (32, F32),
+    "mn": (4, F32), "ee": (32, F32), "ep": (32, F32), "DC": (64, F32), "ci": (8, I32), "cc32": (16, I32), "cx": (16, U16),
+    "Kc": (528, BF), "DS": (528, BF), "sgR": (128, BF), "Psm": (384, F16), "Xsm": (384, BF), "Lsm": (24, U16),
+    "KS": (1664, BF), "Pb": (V, F16), "DJ": (128 + V, BF), "LS": (4 * 96, U16), "fS": (96, F32),
+    "sg": (128, F32), "tm": (128, F32), "thr": (128, F32), "th2": (128, F32), "t1": (96, F32), "t2": (96, F32),
+    "sd": (96, F32), "n3": (8, F32), "d0s": (24, F32), "d1s": (24, F32), "sos": (24, F32),
+    "d0b": (288, F32), "d1b": (288, F32), "sob": (288, F32), "SB": (3 * 96, U16), "LB": (3 * 72, U16), "fB": (384, F32),
+    "LF": (4 * 96, U16), "keyR": (128, F32), "kb": (16, F32), "junk": (2048, BF), "acc": (16, F32),
+    "nl": (24, F32), "cond": (32, F32), "D1": (16, F32), "of": (16, F32), "og": (8, F32), "offU": (32, U16),
+    "who": (4 * 1664, BF), "ov": (4 * 1664, BF), "val": (8, F32), "valU": (8, U16), "ovR": (128, BF), "ovt": (192, F32),
+    "s32": (8, I32), "sb32": (16, I32), "sbU": (16, U16), "mk": (128, BF), "RB": (768, F16), "L1R": (V, BF),
+    "LFf": (48, F32), "l1v": (96, F32), "L1F": (96, F32), "L1U": (96, U16), "upU": (8, U16), "upF": (32, F32),
+    "act": (32, F32), "xa": (8, F32), "yc1": (32, F32), "yc2": (32, F32), "yc3": (32, F32), "ypo": (96, F32),
+}
+SCRATCH = dict((k, ("sbuf", [128, w], d)) for k, (w, d) in WID.items())
+SCRATCH["DC"] = ("sbuf", [128, 16, 4], F32)
+for _k in range(8):
+    SCRATCH["ps%d" % _k] = ("psum", [128, 512], F32)
+DMAS = ["pa", "bt", "co", "xv", "cd", "k0", "k1", "g0", "g1", "g2", "g3", "g4", "yp", "yc"]
+SEMAPHORES = (["cv", "cs", "ct", "cg", "ls", "fin", "f0"] + ["d" + n for n in DMAS] + ["a%d%d" % (t, c) for t in range(R) for c in range(2)]
+              + ["e%d" % t for t in range(R)] + ["s%d" % t for t in range(R)] + ["b%d" % t for t in range(R - 1)] + ["p%d" % t for t in range(R - 1)])
+OP, AF = AluOpType, ActivationFunctionType
+
+
+def A(name, c0=0, c1=None, st=1, p0=0, p1=128, ps=1):
+    if c1 is None:
+        c1 = WID[name][0] if name in WID else 512
+    return (name, c0, c1, st, p0, p1, ps)
+
+
+def IND(win, off):
+    return ("ind", win, off)
+
+
+def rank_program(g, core, T, topo):
+    r = T.rank_of(core)
+    if r is None:
+        return
+    N = len(T.cores)
+    Q = {"v": g.vector, "s": g.scalar, "t": g.tensor, "g": g, "y": g.sync}
+    CS = {"v": "cv", "s": "cs", "t": "ct", "g": "cg"}
+    ops, acc, know, snap, nloc = [], {}, dict((e, {}) for e in Q), {}, [0]
+    cnt = dict((e, 0) for e in Q)
+
+    def M(a):
+        if not isinstance(a, tuple):
+            return a
+        if a[0] == "ind":
+            return M(a[1]).indirect(M(a[2]))
+        n, c0, c1, st, p0, p1, ps = a
+        if n == "DC":
+            return T[n][:, c0 // 4:c1 // 4, 0:2] if st < 0 else T[n][:, c0 // 4, c0 % 4:c0 % 4 + c1 - c0]
+        sp = slice(p0, p1, ps) if ps != 1 else slice(p0, p1)
+        return T[n][sp, c0:c1:st] if st != 1 else T[n][sp, c0:c1]
+
+    def flat(l):
+        o = []
+        for a in l:
+            if isinstance(a, tuple):
+                o += [a[1], a[2]] if a[0] == "ind" else [a]
+        return o
+
+    def note(ev, eng, rd, wr):
+        for w, l in ((False, rd), (True, wr)):
+            for a in l:
+                acc.setdefault(a[0], []).append((ev, eng, w, a[1], a[2], a[4], a[5], a[3]))
+
+    def op(eng, fn, rd, wr, dma=None, send=0):
+        rd, wr = flat(rd), flat(wr)
+        need = {}
+        for w, l in ((False, rd), (True, wr)):
+            for a in l:
+                psum = a[0] not in WID
+                for ev, e2, w2, c0, c1, p0, p1, st in acc.get(a[0], []):
+                    hit = (w or w2) and c0 < a[2] and a[1] < c1 and p0 < a[5] and a[4] < p1
+                    if st > 1 and st == a[3] and (c0 - a[1]) % st:
+                        hit = False
+                    if (e2 == eng and eng == "t") or (a[6] > 1 and ev[0][:2] == "dg"):
+                        continue
+                    if hit or (psum and e2 != eng):
+                        if know[eng].get(ev[0], -1) < ev[1] and need.get(ev[0], -1) < ev[1]:
+                            need[ev[0]] = ev[1]
+        waits = []
+        for k in sorted(need, key=lambda k: -snap[(k, need[k])][1]):
+            if know[eng].get(k, -1) < need[k]:
+                waits.append((k, need[k]))
+                for k2, v2 in snap[(k, need[k])][0].items():
+                    if know[eng].get(k2, -1) < v2:
+                        know[eng][k2] = v2
+        if dma is not None:
+            ev = ("d" + dma, 16)
+        elif send:
+            ev = None
+            nloc[0] += send
+        else:
+            ev = (eng, cnt[eng])
+            cnt[eng] += 1
+        ops.append((eng, fn, waits, ev))
+        if ev is not None:
+            s = dict(know[eng])
+            s[ev[0]] = ev[1]
+            snap[ev] = (s, len(ops))
+            note(ev, None if dma is not None else eng, rd, wr)
+
+    def lands(sem, val, regions):
+        snap[(sem, val)] = ({sem: val}, len(ops))
+        note((sem, val), None, [], regions)
+
+    def cp(o, i, e="v"):
+        if e == "s":
+            return act(o, i, AF.Copy)
+        if o[0] == "ind":
+            return op("v", lambda: g.vector.tensor_copy(M(o), M(i)), [i, o[2]], [o[1]])
+        op("v", lambda: g.vector.tensor_copy(M(o), M(i)), [i], [o])
+
+    def tt(o, a, b, f):
+        op("v", lambda: g.vector.tensor_tensor(M(o), M(a), M(b), f), [a, b], [o])
+
+    def ts(o, a, s1, f1, s2=None, f2=None):
+        if f2 is None:
+            op("v", lambda: g.vector.tensor_scalar(M(o), M(a), M(s1), None, f1), [a, s1], [o])
+        else:
+            op("v", lambda: g.vector.tensor_scalar(M(o), M(a), M(s1), M(s2), f1, f2), [a, s1, s2], [o])
+
+    def ms(o, c):
+        op("v", lambda: g.vector.memset(M(o), c), [], [o])
+
+    def red(o, a, f):
+        op("v", lambda: g.vector.tensor_reduce(M(o), M(a), AxisListType.X, f), [a], [o])
+
+    def act(o, i, f, bias=None, scale=None, accum=None):
+        kw = {}
+        if bias is not None:
+            kw["bias"] = bias
+        if scale is not None:
+            kw["scale"] = scale
+        if accum is not None:
+            kw["accum_out"] = accum
+        op("s", lambda: g.scalar.activation(M(o), M(i), f, **dict((k, M(v)) for k, v in kw.items())), [i, bias, scale], [o, accum])
+
+    def mm(o, l, rh, st=True, sp=True):
+        op("t", lambda: g.tensor.matmul(M(o), M(l), M(rh), st, sp), [l, rh], [o])
+
+    def toW(o, z, name, c0, c1):
+        for a in range(16):
+            mm(o, A(z, 15 - a, 143 - a), A(name, c0 + a, c1, 16), a == 0, a == 15)
+
+    def scan(o, d0, d1):
+        op("v", lambda: g.vector.tensor_tensor_scan(M(o), M(d0), M(d1), 0.0, OP.mult, OP.add), [d0, d1], [o])
+
+    def dma(e, name, o, i):
+        op(e, lambda: Q[e].dma_start(M(o), M(i)), [i], [o], dma=name)
+
+    def iota(o, pat, cm):
+        if WID[o[0]][1] == I32:
+            op("g", lambda: g.iota(M(o), pat, 0, cm), [], [o])
+        else:
+            op("g", lambda: g.iota(M(o), pat, 0, cm, allow_small_or_imprecise_dtypes=True), [], [o])
+
+    peer = [T.cores[(r + 1 + c) % N] for c in range(N - 1)]
+    did = [DstId(rid=topo.addr(p)[0], pnc=topo.addr(p)[1]) for p in peer]
+    eng = [e for e in topo.engines(core, peer[0]) if all(e in topo.engines(core, p) for p in peer)]
+    ne = len(eng)
+
+    def mask_of(l):
+        return sum(1 << e for e in l)
+
+    def send1(c, dst, src, sem):
+        ad = topo.addr(peer[c])
+        op("g", lambda: g.remote_dma(M(dst), M(src), T.sem[sem], T.sem.ls, ad[1], ad[0], mask_of(eng)), [src], [], send=ne)
+
+    def send2(dsts, srcs, sem):
+        parts = [eng[:ne // 2], eng[ne // 2:]]
+        op("g", lambda: g.remote_dma_fused([RemoteDMATransfer(dst_ids=[did[c]], dma_engine_mask=mask_of(parts[c]), remote_sem=T.sem[sem],
+                                                              src=M(srcs[c]), dst=M(dsts[c])) for c in range(2)], local_sem=T.sem.ls), srcs, [], send=ne)
+        lands(sem, ne, dsts)
+
+    def send_all(a, sem, regions):
+        op("g", lambda: g.remote_dma_fused([RemoteDMATransfer(dst_ids=did, dma_engine_mask=mask_of(eng), remote_sem=T.sem[sem],
+                                                              srcs=[M(a)], dsts=[M(a)] * (N - 1))], local_sem=T.sem.ls), [a], [], send=ne)
+        lands(sem, ne * (N - 1), regions)
+
+    def send3(dsts, srcs, sem):
+        parts = [eng[:ne // 4], eng[ne // 4:ne // 2], eng[ne // 2:]]
+        op("g", lambda: g.remote_dma_fused([RemoteDMATransfer(dst_ids=[did[c]], dma_engine_mask=mask_of(parts[c]), remote_sem=T.sem[sem],
+                                                              src=M(srcs[c]), dst=M(dsts[c])) for c in range(3)], local_sem=T.sem.ls), srcs, [], send=ne)
+        lands(sem, ne, dsts)
+
+    others = [(r + 1 + c) % N for c in range(3)]
+    col = lambda n, j: A(n, j, j + 1)
+
+    dma("y", "pa", A("pa32"), T.pa[:])
+    dma("y", "bt", A("btc", 0, 512), T.bt[:])
+    dma("y", "co", A("btc", 512, 1024), T.co[:])
+    dma("s", "xv", A("xs"), T.xv[:])
+    dma("s", "cd", A("cds"), T.cd[:])
+    dma("y", "k0", A("kcs", 0, C // 2), T.kc[:, 0:C // 2])
+    dma("s", "k1", A("kcs", C // 2, C), T.kc[:, C // 2:C])
+    iota(col("pi", 0), [[1, 1]], 1)
+    iota(A("lo"), [[1, 256]], 0)
+    iota(col("pi", 1), [[1, 1]], 4)
+    iota(A("io256"), [[256, V]], 0)
+    ts(col("pj", 0), col("pi", 0), 15, OP.bitwise_and)
+    ts(col("pj", 1), col("pi", 0), 112, OP.bitwise_and)
+    cp(A("cf", 0, 2), A("pj", 0, 2))
+    ts(A("M16"), A("lo", 0, 16), col("cf", 0), OP.is_equal)
+    ts(A("Z"), A("lo", 0, 144), -15.0, OP.add, col("cf", 1), OP.is_equal)
+    cp(col("cf", 5), col("M16", 6))
+    ts(A("hic"), A("lo", 0, 32), 256.0, OP.mult, col("M16", 7), OP.mult)
+    for m in range(32):
+        if m % 2:
+            act(A("dig", 256 * m, 256 * m + 256), A("lo"), AF.Identity, bias=col("hic", m), scale=col("cf", 5))
+        else:
+            ts(A("dig", 256 * m, 256 * m + 256), A("lo"), col("cf", 5), OP.mult, col("hic", m), OP.add)
+
+    def xmask(t, ty, src):
+        for gg in range(8):
+            c0 = 2048 * t + 1024 * ty + 128 * gg
+            ts(A("XM", c0, c0 + 128), src, col("Z", 15 + 16 * gg), OP.mult)
+
+    def keys(sU, sF):
+        tt(A("keyR"), IND(A("io256"), sU), A("lo", 0, 128), OP.add)
+        act(A("kb", 8, 16), sF, AF.Identity, bias=-0.5, scale=256.0)
+        tt(A("kb", 0, 8), A("kb", 8, 16), A("laneW"), OP.add)
+
+    def counts(bs):
+        for b in [b + 8 for b in bs] + bs:
+            act(A("junk", 128 * b, 128 * b + 128), A("keyR"), AF.Sign, bias=col("kb", b), scale=-1.0, accum=col("acc", b))
+
+    ts(A("laneW"), A("lo", 0, 8), 16.0, OP.mult, col("cf", 0), OP.add)
+    cp(A("pU", 0, 96), A("pa32"))
+    cp(A("pF"), A("pa32"))
+    for j, lim in enumerate((3.0, 6.0, 8.0)):
+        ts(col("cf", 6 + j), col("cf", 0), lim, OP.is_lt)
+    ts(col("pj", 2), col("pi", 0), 3, OP.logical_shift_right, 12, OP.bitwise_and)
+    ts(col("pj", 3), col("pi", 1), 112, OP.bitwise_and)
+    ts(col("pj", 4), col("pi", 0), 3, OP.bitwise_and)
+    tt(A("cf", 9, 11), A("cf", 7, 9), A("cf", 6, 8), OP.subtract)
+    ts(col("cf", 11), col("cf", 0), -16384.0, OP.mult, 262144.0, OP.add)
+    cp(A("cf", 2, 5), A("pj", 2, 5))
+    for j, m in enumerate((6, 9, 10)):
+        ts(A("Sel", 8 * j, 8 * j + 8), A("Z", 15, 128, 16), col("cf", m), OP.mult)
+    keys(A("pU", 0, 8), A("pF", 0, 8))
+    counts([2 * r, 2 * r + 1])
+    cp(A("ps0"), A("btc", 0, 512))
+    tt(A("fst", 4 * r, 4 * r + 2), A("acc", 2 * r, 2 * r + 2), A("acc", 8 + 2 * r, 10 + 2 * r), OP.is_equal)
+    send_all(A("fst", 4 * r, 4 * r + 2), "f0", [A("fst", 4 * o, 4 * o + 2) for o in others])
+    iota(A("M16x"), [[0, 96], [1, 16]], 0)
+    cp(A("ps1"), A("btc", 512, 1024))
+    cp(A("dg5", 0, 512), A("ps0"), "s")
+    cp(A("dg5", 1024, 1536), A("ps1"), "s")
+    tt(A("dg5", 512, 1024), A("ps0"), A("dg5", 0, 512), OP.subtract)
+    tt(A("ps2"), A("ps1"), A("dg5", 1024, 1536), OP.subtract)
+    cp(A("dg5", 1536, 2048), A("ps2"), "s")
+    xmask(0, 0, A("xs", 0, 128))
+    tt(A("dg5", 2048, 2560), A("ps2"), A("dg5", 1536, 2048), OP.subtract)
+    for d, row in enumerate((0, 1, 3, 4, 5)):
+        dma("y", "g%d" % d, A("dig", 0, C, 1, row, 128, 16), A("dg5", 512 * d, 512 * d + 512))
+    for name, c in (("who", 512.0), ("KS", 0.0)):
+        act(A(name, 0, V), A("xs"), AF.Identity, bias=c, scale=0.0)
+        act(A(name, V, 1664), A("lo", 0, 128), AF.Identity, bias=c, scale=0.0)
+    ts(col("cf", 12), col("cf", 2), col("cf", 3), OP.add, col("cf", 4), OP.add)
+    ts(col("cf", 13), col("M16", 2), 524288.0, OP.mult)
+    ms(A("tiny"), 0.0)
+    ts(A("dumpW"), A("laneW"), float(V), OP.add)
+    ts(A("Perm"), A("lo", 0, 128), col("cf", 12), OP.is_equal)
+    ts(A("tiny", 1, 48, 2), A("lo", 0, 24), 0.0, OP.mult, col("cf", 13), OP.add)
+    ts(col("tiny", 0), col("cf", 13), 1.5, OP.mult)
+    ts(A("Z2"), A("Z"), col("cf", 6), OP.mult)
+    ts(A("Z3"), A("Z"), col("cf", 9), OP.mult)
+    cp(A("cf", 16, 24), A("Z", 15, 128, 16))
+    ms(A("d0s"), 0.0)
+    cp(A("DS", 512, 528), A("tiny", 0, 16))
+    for t in range(R):
+        ts(A("D1b", 8 * t, 8 * t + 8), A("laneW"), 128.0 * t - 512, OP.add)
+
+    def late_constants():
+        ts(A("M16x"), A("M16x"), col("cf", 0), OP.is_equal, 16.0, OP.mult)
+        ms(A("Kc"), 0.0)
+        ms(A("DS", 0, 512), 0.0)
+        ms(A("d0b"), 0.0)
+        ts(A("idt"), A("lo", 0, 128), 1.0, OP.add)
+
+    def sfill(name, t, c):
+        act(A(name, 1664 * t, 1664 * t + 1664), A("kcs", 0, 1664), AF.Identity, bias=c, scale=0.0)
+
+    def spare_work(t):
+        for gg in range(8):
+            c0 = 2048 * (t + 1) + 128 * gg
+            act(A("XM", c0, c0 + 128), A("xs", 128 * t + 128, 128 * t + 256), AF.Identity, scale=col("cf", 16 + gg))
+        sfill("who", t + 1, 512.0 - 128 * (t + 1))
+
+    def parts(f, land, w, n):
+        for o0, o1 in ((0, r), (r + 1, N)) if n == w else [(o, o + 1) for o in others]:
+            if o0 < o1:
+                ts(A(f, w * o0, w * (o1 - 1) + n), A(land[0], land[1] + w * o0, land[1] + w * (o1 - 1) + n), -32768.0, OP.add)
+
+    def decode(n, ps="ps7"):
+        ts(A("tm", 0, n), A(ps, 0, n), 262144.0, OP.is_gt, -524288.0, OP.mult)
+        ts(A("sg", 0, n), A(ps, 0, n), 262144.0, OP.is_gt)
+        tt(A("thr", 0, n), A(ps, 0, n), A("tm", 0, n), OP.add)
+
+    def route1(t):
+        cp(A("valU"), A("m3"))
+        tt(A("ovR"), IND(A("lo"), A("valU")), A("idt"), OP.mult)
+
+    def route2(t):
+        cp(IND(A("ov", 1664 * t, 1664 * t + 1664), A("offU", 8 * t, 8 * t + 8)), A("ovR"))
+
+    def route3(t, b0, n, ps):
+        lanes = b0 <= 8 * t < b0 + n
+        for c0, c1 in ((0, 8 * t - b0), (8 * t - b0 + 8, n)) if lanes else ((0, n),):
+            if c0 < c1:
+                ts(A("d0b", 3 * c0 + 2, 3 * c1, 3), A(ps, c0, c1), 0.5, OP.is_lt)
+                ts(A("d1b", 3 * c0 + 2, 3 * c1, 3), A(ps, c0, c1), 1.0 / 16, OP.mult, 128.0 * t - 1, OP.add)
+
+    def route_lanes(t, b0, n):
+        if b0 <= 8 * t < b0 + n:
+            j = 3 * (8 * t - b0) + 2
+            ts(A("d0b", j, j + 22, 3), A("m3"), -1.0, OP.mult, 1.0, OP.add)
+            tt(A("val"), A("upF", 8 * t, 8 * t + 8), A("m3"), OP.mult)
+            ts(A("d1b", j, j + 22, 3), A("val"), 128.0 * t - 1, OP.add)
+
+    def first_step(t, n, l1, p):
+        ts(A("d1b", 1, 3 * n, 3), l1, 1.0, OP.add)
+        ts(A("ovt", 0, n), p, 1.0 - 128 * t, OP.add)
+        tt(A("d1b", 0, 3 * n, 3), A("ovt", 0, n), A("d1b", 1, 3 * n, 3), OP.subtract)
+
+    def sides(n, f, o, m0):
+        tt(A("t1", 0, n), A(f, o[0], o[0] + n), A(f, o[1], o[1] + n), OP.add)
+        tt(A("t2", 0, n), A("th2", m0, m0 + n), A(f, o[2], o[2] + n), OP.subtract)
+        tt(A("sd", 0, n), A("t1", 0, n), A("t2", 0, n), OP.is_gt)
+
+    for t in range(R):
+        last, u = t == R - 1, t - 1
+        sU = A("pU", 0, 8) if t == 0 else A("sU", 8 * t, 8 * t + 8)
+        pU = lambda b0, b1: A("pU", 96 * t + b0, 96 * t + b1)
+        who = A("who", 1664 * t, 1664 * t + 1664)
+        dummy = 512.0 - 128 * t
+        cp(A("cU"), IND(A("cds"), sU))
+        cp(A("xsg"), IND(A("xs"), sU), "s")
+        xmask(t, 1, A("xsg"))
+        own = [(r + 1 + c) % N for c in range(N)]
+
+        def kg(c, e, l0=0, l1=32):
+            o = own[c]
+            cp(A("Kg", 512 * o + 16 * l0, 512 * o + 16 * l1), IND(A("kcs"), A("cU", 32 * o + l0, 32 * o + l1)), e)
+
+        def lanes_mm(ps, name, l00, rhs, n):
+            for h in (1, 0):
+                for a in range(16):
+                    l, q, B = l00 + 16 * h + a, a // 4, a % 4
+                    mm(A(ps, B, 4 * n, 4, 32 * q, 32 * q + 16 + 16 * h), A(name, 16 * (l - h), 16 * l + 16), rhs(l))
+
+        def pe(c):
+            lanes_mm("ps%d" % c, "Kg", 32 * own[c], lambda l: A("XM", 2048 * t + l, 2048 * t + 2048, 128), 16)
+
+        def out_a(c):
+            a0 = 192 * t + 64 * c
+            ts(A("SA", a0, a0 + 64), A("ps%d" % c, 0, 64), 32768.0, OP.add)
+            if c == 1:
+                send2([A("LA", a0 - 64, a0), A("LA", a0, a0 + 64)], [A("SA", a0 - 64, a0), A("SA", a0, a0 + 64)], "a%d0" % t)
+            if c == 2:
+                send1(c, A("LA", a0, a0 + 64), A("SA", a0, a0 + 64), "a%d1" % t)
+                lands("a%d1" % t, ne, [A("LA", a0, a0 + 64)])
+
+        sF = A("pF", 0, 8) if t == 0 else A("sos", 2, 24, 3)
+        kg(0, "s", 14, 32)
+        kg(0, "s", 0, 14)
+        pe(0)
+        kg(1, "v")
+        kg(2, "s")
+        out_a(0)
+        if t:
+            route1(u)
+        pe(1)
+        kg(3, "s")
+        out_a(1)
+        pe(2)
+        if t:
+            route2(u)
+        out_a(2)
+        if t:
+            toW(A("ps5", 0, 24), "Z", "ov", 1664 * u + 384 * r, 1664 * u + 384 * r + 384)
+            keys(sU, sF)
+        pe(3)
+        cp(A("Dg"), IND(A("dig"), A("cU", 32 * r, 32 * r + 32)), "s")
+        lanes_mm("ps4", "Dg", 0, lambda l: A("Sel"), 24)
+        if t:
+            route_lanes(u, 24 * r, 24)
+            ts(A("fB", 0, 72), A("LB", 72 * u, 72 * u + 72), -32768.0, OP.add)
+            sides(24, "fB", (0, 24, 48), 24)
+            tt(A("d0b", 1, 72, 3), A("sd", 0, 24), A("sg", 24, 48), OP.not_equal)
+            route3(u, 24 * r, 24, "ps5")
+            scan(A("sob", 0, 72), A("d0b", 0, 72), A("d1b", 0, 72))
+            cp(pU(24 * r, 24 * r + 24), A("sob", 2, 72, 3))
+            send_all(pU(24 * r, 24 * r + 24), "p%d" % u, [pU(24 * o, 24 * o + 24) for o in others])
+        else:
+            late_constants()
+        act(A("nl", 0, 8), sF, AF.Abs, bias=-128.0 * t - 63.5)
+        if t:
+            counts(list(range(8)))
+        cp(A("uA"), A("ps3", 0, 64))
+        ts(A("sbU", 0, 8), sF, 1.0 / 16, OP.mult, -0.46875, OP.add)
+        tt(A("D1", 0, 8), sF, A("dumpW"), OP.subtract)
+        ts(A("nl", 8, 16), A("nl", 0, 8), 64.0, OP.is_gt)
+        cond = A("cond", 8 * t, 8 * t + 8)
+        if t:
+            tt(A("og"), A("acc", 0, 8), A("acc", 8, 16), OP.is_equal)
+        tt(A("fA", 0, 32), A("ps4", 0, 32), A("uA", 0, 32), OP.subtract)
+        tt(A("fA", 32, 64), A("ps4", 0, 32), A("uA", 32, 64), OP.subtract)
+        act(A("negc"), A("ps4", 32, 64), AF.Identity, bias=-8388608.0)
+        act(A("pay"), A("ps4", 64, 96), AF.Identity, bias=col("cf", 11))
+        if t:
+            tt(cond, A("og"), A("nl", 8, 16), OP.mult)
+        else:
+            for h in range(2):
+                tt(A("cond", h, 8, 2), A("fst", h, 16, 4), A("nl", 8 + h, 16, 2), OP.mult)
+        ts(A("ps5", 128, 256), A("LA", 192 * t, 192 * t + 128), -32768.0, OP.add)
+        tt(A("fA", 64, 128), A("fA", 0, 64), A("ps5", 128, 192), OP.subtract)
+        cp(A("mk"), IND(A("M16x"), sU), "s")
+        sfill("ov", t, 0.0)
+        tt(A("rest"), A("fA", 64, 128), A("ps5", 192, 256), OP.subtract)
+        ts(A("ps5", 256, 320), A("LA", 192 * t + 128, 192 * t + 192), -32768.0, OP.add)
+        tt(A("side"), A("ps5", 256, 320), A("rest"), OP.is_gt)
+        tt(A("kp", 64, 96), A("side", 0, 32), A("side", 32, 64), OP.not_equal)
+        ts(A("s8"), A("side", 0, 32), 8192.0, OP.mult)
+        tt(A("kp", 0, 32), A("kp", 64, 96), A("negc"), OP.mult)
+        tt(A("kp", 32, 64), A("s8"), A("pay"), OP.add)
+        op("v", lambda: g.vector.transpose(M(A("kpT")), M(A("kp"))), [A("kp")], [A("kpT")])
+        for h in range(2):
+            red(col("mn", h), A("kpT", 16 * h, 16 * h + 16), OP.min)
+            red(col("mn", 2 + h), A("kpT", 64 + 16 * h, 80 + 16 * h), OP.max)
+        for h in range(2):
+            ts(A("ee", 16 * h, 16 * h + 16), A("kpT", 16 * h, 16 * h + 16), col("mn", h), OP.is_equal, col("mn", 2 + h), OP.mult)
+        tt(A("ep"), A("ee"), A("kpT", 32, 64), OP.mult)
+        d0 = 16 * t + 4 * r
+        for h in range(2):
+            red(col("DC", d0 + h), A("ep", 16 * h, 16 * h + 16), OP.max)
+        send_all(A("DC", d0, d0 + 2), "e%d" % t, [A("DC", 16 * t + 4 * o, 16 * t + 4 * o + 2) for o in others])
+        tt(A("of", 0, 8), cond, A("D1", 0, 8), OP.mult)
+        tt(A("of", 8, 16), cond, A("D1b", 8 * t, 8 * t + 8), OP.mult)
+        tt(A("og"), A("of", 0, 8), A("dumpW"), OP.add)
+        ts(A("Lsm", 16, 24), A("of", 8, 16), dummy, OP.add)
+        offU = A("offU", 8 * t, 8 * t + 8)
+        cp(offU, A("og"))
+        cp(IND(who, offU), A("lo", 0, 128))
+        if t:
+            cp(A("pF"), pU(0, 96))
+        g0 = 0 if last else 256
+        tt(A("RB", g0, g0 + 128), IND(A("pF"), A("sbU", 0, 8)), A("mk"), OP.mult)
+        nb = 8 * t + 8
+        if not last:
+            cp(A("RB", 0, 128), IND(who, pU(nb, nb + 8)))
+            cp(A("RB", 128, 256), A("who", 1664 * t + 16 * nb, 1664 * t + 16 * nb + 128))
+            cp(A("Xsm", 0, 128), A("xs", 16 * nb, 16 * nb + 128), "s")
+            cp(A("Xsm", 128, 256), IND(A("xs"), pU(nb, nb + 8)), "s")
+            cp(A("L1R", 0, 384), IND(who, pU(24 * r, 24 * r + 24)), "s")
+            toW(A("ps5", 64, 88), "Z", "RB", 0, 384)
+            ts(A("upU"), A("ps5", 80, 88), 1.0 / 16, OP.mult)
+            ts(A("Lsm", 0, 16), A("ps5", 64, 80), 1.0 / 16, OP.mult)
+            ts(A("LFf", 0, 24), A("ps5", 64, 88), 1.0 / 16, OP.mult)
+            cp(A("Xsm", 256, 384), IND(A("xs"), A("upU")), "s")
+            act(A("l1v", 0, 8), A("LFf", 0, 8), AF.Identity, bias=128.0 * t)
+            act(A("d1s", 2, 24, 3), A("LFf", 8, 16), AF.Identity, bias=128.0 * t)
+            act(A("ovt", 0, 24), A("pF", 24 * r, 24 * r + 24), AF.Identity, bias=1.0 - 128 * t)
+            if r == 0:
+                act(A("upF", 8 * t, 8 * t + 8), A("LFf", 16, 24), AF.Identity, bias=1.0 - 128 * t)
+        else:
+            cp(A("L1R", 640, V), IND(who, pU(40, 96)), "s")
+            cp(A("RB", 128, 768), IND(who, pU(0, 40)))
+            toW(A("ps5", 64, 112), "Z", "RB", 0, 768)
+            ts(A("upU"), A("ps5", 64, 72), 1.0 / 16, OP.mult)
+            ts(A("L1F", 0, 40), A("ps5", 72, 112), 1.0 / 16, OP.mult)
+            ts(A("upF", 8 * t, 8 * t + 8), A("ps5", 64, 72), 1.0 / 16, OP.mult, 1.0 - 128 * t, OP.add)
+            cp(A("Xsm", 256, 384), IND(A("xs"), A("upU")), "s")
+            tt(A("L1F", 8 * t, nb), A("L1F", 8 * t, nb), A("of", 8, 16), OP.subtract)
+            cp(A("L1U", 0, 40), A("L1F", 0, 40))
+        mm(A("ps4", 0, 8), A("Perm"), A("DC", 16 * t, 16 * t + 16, -1))
+        if last:
+            toW(A("ps1", 40, 96), "Z", "L1R", 640, V)
+        else:
+            toW(A("ps1", 0, 24), "Z", "L1R", 0, 384)
+        cp(A("ci"), A("ps4", 0, 8))
+        act(A("act", 8 * t, 8 * t + 8), A("ps4", 0, 8), AF.Sign)
+        ts(A("cc32", 0, 8), A("ci"), 8191, OP.bitwise_and)
+        ts(A("cc32", 8, 16), A("ci"), 13, OP.logical_shift_right)
+        cp(A("cx"), A("cc32"))
+        Kc, DS = A("Kc", 128 * t, 128 * t + 128), A("DS", 128 * t, 128 * t + 128)
+        cp(Kc, IND(A("kcs"), A("cx", 0, 8)))
+        cp(A("sgR"), IND(A("tiny"), A("cx", 8, 16)), "s")
+        DSw = A("DS", 128 * t, 528)
+        s0 = 16 if last else 0
+        ns = 24 - s0
+        tt(A("Psm", 16 * s0, 384), IND(A("Kc", 128 * t, 528), A("Lsm", s0, 24)), A("Xsm", 16 * s0, 384), OP.mult)
+        toW(A("ps6", 0, ns), "Z", "Psm", 16 * s0, 384)
+
+        def big(b0, b1):
+            tt(A("Pb", 16 * b0, 16 * b1), IND(A("KS"), pU(b0, b1)), A("xs", 16 * b0, 16 * b1), OP.mult)
+
+        if last:
+            cp(IND(A("KS"), offU), Kc)
+            tt(DS, IND(A("dig"), A("cx", 0, 8)), A("sgR"), OP.add)
+            ts(A("L1U", 40, 96), A("ps1", 40, 96), 1.0 / 16, OP.mult)
+            cp(A("DJ", 0, 128), IND(DSw, A("Lsm", 16, 24)), "s")
+            toW(A("ps7", 0, 8), "Z2", "DJ", 0, 128)
+            cp(A("DJ", 128, 128 + V), IND(DSw, A("L1U")), "s")
+            big(0, 16)
+        else:
+            tt(DS, IND(A("dig"), A("cx", 0, 8)), A("sgR"), OP.add)
+            if r == 0:
+                ts(A("LFf", 24, 48), A("ps1", 0, 24), 1.0 / 16, OP.mult)
+                tt(A("LFf", 24 + 8 * t, 32 + 8 * t), A("LFf", 24 + 8 * t, 32 + 8 * t), A("of", 8, 16), OP.subtract)
+                cp(A("L1U", 0, 24), A("LFf", 24, 48))
+            else:
+                ts(A("L1U", 0, 24), A("ps1", 0, 24), 1.0 / 16, OP.mult)
+            cp(IND(A("KS"), offU), Kc)
+        slot = lambda o: A("LS", 96 * t + 24 * o, 96 * t + 24 * o + ns)
+        ts(slot(r), A("ps6", 0, ns), 32768.0, OP.add)
+        send_all(slot(r), "s%d" % t, [slot(o) for o in others])
+        if not last:
+            cp(A("DJ", 0, 384), IND(DSw, A("Lsm")), "s")
+            cp(A("DJ", 384, 768), IND(DSw, A("L1U", 0, 24)), "s")
+            toW(A("ps7", 0, 48), "Z2", "DJ", 0, 768)
+            spare_work(t)
+            big(0, 48)
+            toW(A("ps3", 0, 48), "Z", "Pb", 0, V // 2)
+            big(48, 96)
+            toW(A("ps3", 48, 96), "Z", "Pb", V // 2, V)
+            decode(48)
+            tt(A("th2", 0, 24), A("thr", 0, 24), A("ps6", 0, 24), OP.subtract)
+            ts(A("d1b", 1, 72, 3), A("L1U", 0, 24), 1.0, OP.add)
+            tt(A("d1s", 1, 24, 3), A("LFf", 0, 8), A("LFf", 8, 16), OP.subtract)
+            tt(A("d1s", 0, 24, 3), A("pF", nb, nb + 8), A("l1v", 0, 8), OP.subtract)
+            tt(A("d1b", 0, 72, 3), A("ovt", 0, 24), A("d1b", 1, 72, 3), OP.subtract)
+            ts(A("SB", 96 * t, 96 * t + 96), A("ps3", 0, 96), 32768.0, OP.add)
+            send3([A("LB", 72 * t + 24 * c, 72 * t + 24 * c + 24) for c in range(3)], [A("SB", 96 * t + 24 * o, 96 * t + 24 * o + 24) for o in others], "b%d" % t)
+            tt(A("th2", 24, 48), A("thr", 24, 48), A("ps3", 24 * r, 24 * r + 24), OP.subtract)
+            parts("fS", ("LS", 96 * t), 24, 24)
+            sides(24, "fS", [24 * o for o in others], 0)
+            tt(A("d0s", 1, 24, 3), A("sd", 0, 8), A("sg", 0, 8), OP.not_equal)
+            tt(A("d0s", 2, 24, 3), A("sd", 8, 16), A("sg", 8, 16), OP.not_equal)
+            scan(A("sos"), A("d0s"), A("d1s"))
+            tt(A("m3"), A("sd", 16, 24), A("sg", 16, 24), OP.is_equal)
+            cp(A("sU", nb, nb + 8), A("sos", 2, 24, 3))
+        else:
+            big(16, 48)
+            toW(A("ps3", 0, 48), "Z", "Pb", 0, V // 2)
+            big(48, 96)
+            toW(A("ps3", 48, 96), "Z", "Pb", V // 2, V)
+            toW(A("ps0", 0, 96), "Z2", "DJ", 128, 128 + V)
+            toW(A("ps4", 0, 32), "Z3", "DS", 0, 512)
+            decode(8)
+            ts(A("L1F", 40, 96), A("ps1", 40, 96), 1.0 / 16, OP.mult)
+            tt(A("th2", 0, 8), A("thr", 0, 8), A("ps6", 0, 8), OP.subtract)
+            tt(A("yc2"), A("act"), A("cond"), OP.mult)
+            fl = lambda o: A("LF", 96 * o, 96 * o + 96)
+            ts(fl(r), A("ps3", 0, 96), 32768.0, OP.add)
+            send_all(fl(r), "fin", [fl(o) for o in others])
+            first_step(t, 96, A("L1F"), A("pF"))
+            parts("fS", ("LS", 96 * t), 24, 8)
+            sides(8, "fS", [24 * o for o in others], 0)
+            tt(A("m3"), A("sd", 0, 8), A("sg", 0, 8), OP.is_equal)
+            route1(t)
+            route2(t)
+            toW(A("ps2", 0, 96), "Z", "ov", 1664 * t, 1664 * t + V)
+            decode(96, "ps0")
+            route_lanes(t, 0, 96)
+            tt(A("th2", 0, 96), A("thr", 0, 96), A("ps3", 0, 96), OP.subtract)
+            ts(A("yc1"), A("ps4", 0, 32), 1.0, OP.add)
+            tt(A("yc3"), A("yc1"), A("yc2"), OP.mult)
+            act(A("yc1"), A("yc3"), AF.Identity, bias=-1.0)
+            dma("s", "yc", T.yc[:], A("yc1"))
+            ts(A("ps1", 0, 96), fl(others[0]), -32768.0, OP.add)
+            ts(A("fB", 0, 96), fl(others[1]), -32768.0, OP.add)
+            ts(A("ps1", 96, 192), fl(others[2]), -32768.0, OP.add)
+            tt(A("ps1", 192, 288), A("ps1", 0, 96), A("fB", 0, 96), OP.add)
+            tt(A("t2"), A("th2", 0, 96), A("ps1", 96, 192), OP.subtract)
+            tt(A("ps1", 288, 384), A("ps1", 192, 288), A("t2"), OP.is_gt)
+            tt(A("d0b", 1, 288, 3), A("ps1", 288, 384), A("sg", 0, 96), OP.not_equal)
+            route3(t, 0, 96, "ps2")
+            scan(A("sob"), A("d0b"), A("d1b"))
+            cp(A("ypo"), A("sob", 2, 288, 3))
+            dma("y", "yp", T.yp[:], A("ypo"))
+
+    wanted = set(w for o in ops for w in o[2] if w[0] in CS)
+    num, tot = {}, dict((e, 0) for e in CS)
+    for e, fn, waits, ev in ops:
+        if ev in wanted:
+            tot[e] += 1
+            num[ev] = tot[e]
+    for e, fn, waits, ev in ops:
+        for w in waits:
+            if w[0] in CS:
+                Q[e].wait_ge(T.sem[CS[w[0]]], num[w])
+            else:
+                Q[e].wait_ge(T.sem[w[0]], w[1])
+        ins = fn()
+        if ev in wanted:
+            ins.then_inc(T.sem[CS[e]], 1)
+        elif ev is not None and ev[0] not in CS:
+            ins.then_inc(T.sem[ev[0]], 16)
+    g.wait_ge(T.sem.ls, nloc[0])
+    g.sync.wait_ge(T.sem.dyp, 16)
+    g.scalar.wait_ge(T.sem.dyc, 16)

@@ -1,49 +1,151 @@
+import numpy as np
 from concourse.bass import DstId, RemoteDMATransfer
 from concourse.mybir import AluOpType, AxisListType, ActivationFunctionType
 
 V, C, L, R = 1536, 8192, 128, 4
 BF, F32, F16, I32, U16 = "bfloat16", "float32", "float16", "int32", "uint16"
+CX, VX, LX = C + 32, V + L, L + 16
+BIG = 2.0 ** 22
 WID = {
-    "kcs": (C, BF), "dig": (C, BF), "xs": (V, BF), "cds": (V, I32), "btc": (1024, I32), "dg5": (2560, BF),
-    "pa32": (96, I32), "io256": (V, F32), "lo": (256, BF), "pi": (8, I32), "pj": (8, I32), "cf": (24, F32),
-    "Z": (144, BF), "Z2": (144, BF), "Z3": (144, BF), "Sel": (24, BF), "M16": (16, BF), "M16x": (V, BF),
-    "fst": (16, F32), "idt": (128, BF), "m3": (8, F32), "D1b": (32, F32),
-    "tiny": (48, BF), "hic": (32, F32), "Perm": (128, F32), "laneW": (8, F32), "dumpW": (8, F32), "lane1": (8, F32),
+    "kcs": (CX, BF), "dig": (CX, BF), "xs": (V, BF), "xsP": ((4, 352), BF), "cds": (V, I32), "btc": (1024, I32), "dg5": (2560, BF),
+    "pa32": (96, I32), "io256": (VX, F32), "lo": (256, BF), "pi": (8, I32), "pj": (8, I32), "cf": (32, F32),
+    "Z": (144, BF), "Z1": (144, BF), "Z2": (144, BF), "Z3": (144, BF), "Sel": (32, BF), "M16": (16, BF), "M16x": (V, BF),
+    "Y": (128, BF), "Q": (512, BF), "Q1": (512, BF), "Q2": (512, BF), "hq": (128, F32), "hq2": (128, F32), "MQ": (128, F32), "TG": (4 * L, BF),
+    "fst": (16, F32), "w0": (16, F32), "wg": (16, F32), "c18": (32, F32), "hic": (32, F32), "Perm": (128, F32),
+    "laneW": (32, F32), "lane16": (8, F32),
     "XM": (4 * 2048, BF), "Kg": (2048, BF), "Dg": (512, BF), "xsg": (128, BF), "cU": (128, U16),
-    "sU": (32, U16), "sF": (8, F32), "pU": (4 * 96, U16), "pF": (96, F32),
-    "SA": (4 * 192, U16), "LA": (4 * 192, U16), "fA": (192, F32), "uA": (64, F32), "rest": (64, F32),
-    "side": (64, F32), "kp": (96, F32), "kpT": (96, F32), "negc": (32, F32), "pay": (32, F32), "s8": (32, F32),
-    "mn": (4, F32), "ee": (32, F32), "ep": (32, F32), "DC": (64, F32), "ci": (8, I32), "cc32": (16, I32), "cx": (16, U16),
-    "Kc": (528, BF), "DS": (528, BF), "sgR": (128, BF), "Psm": (384, F16), "Xsm": (384, BF), "Lsm": (24, U16),
-    "KS": (1664, BF), "Pb": (V, F16), "DJ": (128 + V, BF), "LS": (4 * 96, U16), "fS": (96, F32),
-    "sg": (128, F32), "tm": (128, F32), "thr": (128, F32), "th2": (128, F32), "t1": (96, F32), "t2": (96, F32),
-    "sd": (96, F32), "n3": (8, F32), "d0s": (24, F32), "d1s": (24, F32), "sos": (24, F32),
-    "d0b": (288, F32), "d1b": (288, F32), "sob": (288, F32), "SB": (3 * 96, U16), "LB": (3 * 72, U16), "fB": (384, F32),
-    "LF": (4 * 96, U16), "keyR": (128, F32), "kb": (16, F32), "junk": (2048, BF), "acc": (16, F32),
-    "nl": (24, F32), "cond": (32, F32), "D1": (16, F32), "of": (16, F32), "og": (8, F32), "offU": (32, U16),
-    "who": (4 * 1664, BF), "ov": (4 * 1664, BF), "val": (8, F32), "valU": (8, U16), "ovR": (128, BF), "ovt": (192, F32),
-    "s32": (8, I32), "sb32": (16, I32), "sbU": (16, U16), "mk": (128, BF), "RB": (768, F16), "L1R": (V, BF),
-    "LFf": (48, F32), "l1v": (96, F32), "L1F": (96, F32), "L1U": (96, U16), "upU": (8, U16), "upF": (32, F32),
-    "act": (32, F32), "xa": (8, F32), "yc1": (32, F32), "yc2": (32, F32), "yc3": (32, F32), "ypo": (96, F32),
+    "sU": (32, U16), "pS": ((16, 24), U16), "pN": (96, U16), "pF": (4 * 96, F32), "sqP": (32, F32), "sqW": (128, F32),
+    "TR": ((12, 32), F32), "TO": ((8, 32), F32), "SA": (4 * 192, U16), "LA": (4 * 192, U16), "r1": (64, F32), "rest": (64, F32),
+    "side": ((4, 19), F32), "cutp": ((2, 19), F32), "d1c": (36, F32), "d1e": (36, F32), "ne": (36, F32), "negc": ((2, 18), F32),
+    "key": (36, F32), "pm": (36, F32), "M18": (36, F32), "nfl": (36, F32), "yq": (72, F32),
+    "DL": ((16, 8), U16), "cx": (16, U16), "Kc": (LX, BF), "DS": (4 * LX, BF), "sgR": (128, BF),
+    "WL": (96, U16), "XL": (48, U16), "RB": (512, BF), "sqL": (128, F32), "LL": (32, U16), "Lf": (32, F32), "Xsm": (256, BF),
+    "Psm": (256, F16), "sqO": (64, F32), "sqT": (64, F32), "SS": (48, U16), "LS": (3 * 48, U16), "fS": (48, F32),
+    "DJ": (512, BF), "tm": (16, F32), "uu": (16, F32), "th2": (16, F32),
+    "t1": (16, F32), "t2": (16, F32), "sd": ((8, 3), F32), "sg3": ((8, 3), F32), "d0s": (24, F32), "d1s": (24, F32), "sos": (24, F32),
+    "sbU": (8, U16), "mk": (128, BF), "RU": (128, F16), "upU": (8, U16), "upF": (8, F32), "X3": (128, BF), "Pu": (384, F16),
+    "sqU": (96, F32), "sqV": (96, F32), "SU": (96, U16), "LU": (4 * 72, U16), "fU": (72, F32),
+    "u0": (24, F32), "u1": (24, F32), "u2": (24, F32), "ud": (24, F32), "uw": (24, F32), "d0u": (48, F32), "d1u": (48, F32), "sou": (48, F32),
+    "KS": (VX, BF), "who": (VX, BF), "ov": (VX, BF), "Pb": (V, F16), "L1R": (V, BF), "DB": (V, BF), "L1U": (96, U16), "L1F": (8, F32),
+    "tb": (96, F32), "b0": (96, F32), "b1": (96, F32), "b2": (96, F32), "bd": (96, F32), "bw": (96, F32),
+    "d0b": (288, F32), "d1b": (288, F32), "sob": (288, F32), "SB": (4 * 96, U16), "LB": (3 * 72, U16), "LF": (288, U16), "fB": (288, F32),
+    "keyR": (128, F32), "kb": (16, F32), "junk": (2048, BF), "acc": (16, F32), "nl": (16, F32), "ap": (8, F32), "cond": (36, F32),
+    "o0": (16, F32), "o1": (64, F32), "og": (16, F32), "cl": (32, F32), "offU": (32, U16), "val": (8, F32), "vam": (8, F32), "offV": (8, U16),
+    "ovt": (96, F32), "yc1": (36, F32), "ycq": ((4, 9), F32), "yco": (32, F32), "ypo": (96, F32),
 }
-SCRATCH = dict((k, ("sbuf", [128, w], d)) for k, (w, d) in WID.items())
-SCRATCH["DC"] = ("sbuf", [128, 16, 4], F32)
+SMALL, _at = {}, 0
+for _k, (_w, _d) in list(WID.items()):
+    if _d == F32 and not isinstance(_w, tuple) and _w <= 128 and _k not in ("fst", "ypo", "yco"):
+        SMALL[_k] = (_at, _w)
+        _at += (_w + 7) // 8 * 8
+        del WID[_k]
+WID["small"] = (_at, F32)
+SHAPE = dict((k, [128] + (list(w) if isinstance(w, tuple) else [w])) for k, (w, d) in WID.items())
+SCRATCH = dict((k, ("sbuf", SHAPE[k], d)) for k, (w, d) in WID.items())
 for _k in range(8):
     SCRATCH["ps%d" % _k] = ("psum", [128, 512], F32)
-DMAS = ["pa", "bt", "co", "xv", "cd", "k0", "k1", "g0", "g1", "g2", "g3", "g4", "yp", "yc"]
-SEMAPHORES = (["cv", "cs", "ct", "cg", "ls", "fin", "f0"] + ["d" + n for n in DMAS] + ["a%d%d" % (t, c) for t in range(R) for c in range(2)]
-              + ["e%d" % t for t in range(R)] + ["s%d" % t for t in range(R)] + ["b%d" % t for t in range(R - 1)] + ["p%d" % t for t in range(R - 1)])
+    SHAPE["ps%d" % _k] = [128, 512]
+DMAS = ["pa", "bt", "co", "xv", "cd", "k0", "k1", "g0", "g1", "g2", "g3", "g4", "y0", "y1", "yc"]
+SEMAPHORES = (["cv", "cs", "ct", "cg", "ls", "f0", "z0", "z1"] + ["d" + n for n in DMAS] + ["a%d%d" % (t, c) for t in range(R) for c in range(2)]
+              + [n + "%d" % t for n in "eu" for t in range(R)] + [n + "%d" % t for n in "sbp" for t in range(R - 1)])
 OP, AF = AluOpType, ActivationFunctionType
+ALL = slice(None)
+CY, WAKE, GATHER, SCATTER = 0.00083, 0.24, 1.56, 3.8
+SAME = 0.15
+ISSUE, START, ROW, LAND, LOAD, RATE = 0.3, 0.7, 0.035, 0.05, 1.0, 500e3
+TRIES = 4000
 
 
-def A(name, c0=0, c1=None, st=1, p0=0, p1=128, ps=1):
-    if c1 is None:
-        c1 = WID[name][0] if name in WID else 512
-    return (name, c0, c1, st, p0, p1, ps)
+def A(name, c0=0, c1=None, st=1, p=ALL):
+    if name in SMALL:
+        at, w = SMALL[name]
+        return ("small", (p, slice(at + c0, at + (w if c1 is None else c1), st)))
+    return (name, (p, slice(c0, c1, st)))
+
+
+def B(name, i=ALL, j=ALL):
+    return (name, (ALL, i, j))
+
+
+def S(a, b=None, c=1):
+    return slice(a, b, c)
 
 
 def IND(win, off):
     return ("ind", win, off)
+
+
+FOOT, PLAN = {}, []
+
+
+def foot(a):
+    k = repr(a)
+    if k not in FOOT:
+        sh = SHAPE[a[0]]
+        cols = np.arange(int(np.prod(sh[1:]))).reshape(sh[1:])[a[1][1:]].reshape(-1)
+        m = np.zeros(int(np.prod(sh[1:])), np.uint8)
+        m[cols] = 1
+        q = np.zeros(128, np.uint8)
+        q[a[1][0]] = 1
+        FOOT[k] = (int.from_bytes(np.packbits(q).tobytes(), "big"), int.from_bytes(np.packbits(m).tobytes(), "big"), len(cols))
+    return FOOT[k]
+
+
+def planned(ops):
+    n = len(ops)
+    que, dur = [o[0] for o in ops], [o[3] for o in ops]
+    before, after = [list(o[2].items()) for o in ops], [[] for o in ops]
+    for i in range(n):
+        for m, lat in before[i]:
+            after[m].append((i, lat))
+
+    def place(urgency, links, ids):
+        u = list(urgency)
+        for i in ids:
+            for m, _ in links[i]:
+                if u[m] > u[i]:
+                    u[i] = u[m]
+        end, slots = [0.0] * n, dict((e, ([], [])) for e in que)
+        for i in sorted(ids, key=lambda i: u[i]):
+            s, d = 0.0, dur[i]
+            for m, lat in links[i]:
+                if end[m] + lat > s:
+                    s = end[m] + lat
+            if que[i] != "l":
+                a, b = slots[que[i]]
+                k = len(a)
+                while k and b[k - 1] > s + 1e-12:
+                    k -= 1
+                while k < len(a) and s + d > a[k] + 1e-9:
+                    s = b[k]
+                    k += 1
+                a.insert(k, s)
+                b.insert(k, s + d)
+            end[i] = s + d
+        return end
+
+    up, down = list(range(n)), list(range(n - 1, -1, -1))
+
+    def both(urgency):
+        end = place([-x for x in place([-x for x in place(urgency, before, up)], after, down)], before, up)
+        return max(end), np.array(end) - dur
+
+    if not PLAN:
+        way = list(dur)
+        for i in down:
+            for m, lat in before[i]:
+                way[m] = max(way[m], dur[m] + lat + way[i])
+        best = now = both([-x for x in way])
+        rng = np.random.default_rng(0)
+        for _ in range(TRIES):
+            near = np.abs(now[1] - rng.uniform(0.25, 1.0) * now[0]) < rng.uniform(1, 6)
+            x = both((now[1] + near * rng.normal(0, rng.choice([0.1, 0.3, 0.6, 1.0]), n)).tolist())
+            if x[0] <= now[0] + 0.05:
+                now = x
+            if x[0] < best[0]:
+                best = x
+        PLAN.append(best[1].tolist())
+    return [e - d for e, d in zip(place(PLAN[0], before, up), dur)]
 
 
 def rank_program(g, core, T, topo):
@@ -53,19 +155,14 @@ def rank_program(g, core, T, topo):
     N = len(T.cores)
     Q = {"v": g.vector, "s": g.scalar, "t": g.tensor, "g": g, "y": g.sync}
     CS = {"v": "cv", "s": "cs", "t": "ct", "g": "cg"}
-    ops, acc, know, snap, nloc = [], {}, dict((e, {}) for e in Q), {}, [0]
-    cnt = dict((e, 0) for e in Q)
+    ops, acc, nloc, fifo = [], {}, [0], [[], []]
 
     def M(a):
         if not isinstance(a, tuple):
             return a
         if a[0] == "ind":
             return M(a[1]).indirect(M(a[2]))
-        n, c0, c1, st, p0, p1, ps = a
-        if n == "DC":
-            return T[n][:, c0 // 4:c1 // 4, 0:2] if st < 0 else T[n][:, c0 // 4, c0 % 4:c0 % 4 + c1 - c0]
-        sp = slice(p0, p1, ps) if ps != 1 else slice(p0, p1)
-        return T[n][sp, c0:c1:st] if st != 1 else T[n][sp, c0:c1]
+        return T[a[0]][a[1]]
 
     def flat(l):
         o = []
@@ -74,102 +171,82 @@ def rank_program(g, core, T, topo):
                 o += [a[1], a[2]] if a[0] == "ind" else [a]
         return o
 
-    def note(ev, eng, rd, wr):
-        for w, l in ((False, rd), (True, wr)):
+    def node(eng, fns, rd, wr, dur, ev=None, after=None):
+        n, deps = len(ops), dict(after or {})
+        for w, l in ((False, flat(rd)), (True, flat(wr))):
             for a in l:
-                acc.setdefault(a[0], []).append((ev, eng, w, a[1], a[2], a[4], a[5], a[3]))
+                p, c, _ = foot(a)
+                keep = []
+                for e in acc.get(a[0], []):
+                    m, e2, w2, p2, c2 = e
+                    if m != n and (((w or w2) and p & p2 and c & c2) or (a[0] not in WID and (e2 != eng or eng == "t"))):
+                        deps.setdefault(m, WAKE if e2 != eng else 0.0 if eng == "t" else SAME)
+                    if not (w and m != n and p2 & ~p == 0 and c2 & ~c == 0 and (a[0] in WID or e2 == eng)):
+                        keep.append(e)
+                acc[a[0]] = keep + [(n, eng, w, p, c)]
+        ops.append((eng, fns, deps, dur, ev))
+        return n
 
-    def op(eng, fn, rd, wr, dma=None, send=0):
-        rd, wr = flat(rd), flat(wr)
-        need = {}
-        for w, l in ((False, rd), (True, wr)):
-            for a in l:
-                psum = a[0] not in WID
-                for ev, e2, w2, c0, c1, p0, p1, st in acc.get(a[0], []):
-                    hit = (w or w2) and c0 < a[2] and a[1] < c1 and p0 < a[5] and a[4] < p1
-                    if st > 1 and st == a[3] and (c0 - a[1]) % st:
-                        hit = False
-                    if (e2 == eng and eng == "t") or (a[6] > 1 and ev[0][:2] == "dg"):
-                        continue
-                    if hit or (psum and e2 != eng):
-                        if know[eng].get(ev[0], -1) < ev[1] and need.get(ev[0], -1) < ev[1]:
-                            need[ev[0]] = ev[1]
-        waits = []
-        for k in sorted(need, key=lambda k: -snap[(k, need[k])][1]):
-            if know[eng].get(k, -1) < need[k]:
-                waits.append((k, need[k]))
-                for k2, v2 in snap[(k, need[k])][0].items():
-                    if know[eng].get(k2, -1) < v2:
-                        know[eng][k2] = v2
-        if dma is not None:
-            ev = ("d" + dma, 16)
-        elif send:
-            ev = None
-            nloc[0] += send
-        else:
-            ev = (eng, cnt[eng])
-            cnt[eng] += 1
-        ops.append((eng, fn, waits, ev))
-        if ev is not None:
-            s = dict(know[eng])
-            s[ev[0]] = ev[1]
-            snap[ev] = (s, len(ops))
-            note(ev, None if dma is not None else eng, rd, wr)
+    def two(l):
+        return all(WID.get(a[0], (0, F32))[1] in (BF, F16, U16) for a in l)
 
-    def lands(sem, val, regions):
-        snap[(sem, val)] = ({sem: val}, len(ops))
-        note((sem, val), None, [], regions)
+    def vdur(o, ins, per=None):
+        for a in [o] + ins:
+            if a[0] == "ind":
+                return 0.05 + 16 * foot(a[2])[2] * (SCATTER if a is o else GATHER) * CY
+        return max(64, foot(o)[2] * (per or (0.5 if two([o] + ins) else 1))) * CY
 
-    def cp(o, i, e="v"):
+    def cp(o, i, e="v", also=()):
         if e == "s":
             return act(o, i, AF.Copy)
-        if o[0] == "ind":
-            return op("v", lambda: g.vector.tensor_copy(M(o), M(i)), [i, o[2]], [o[1]])
-        op("v", lambda: g.vector.tensor_copy(M(o), M(i)), [i], [o])
+        node("v", [lambda: g.vector.tensor_copy(M(o), M(i))], [i] + ([o[2]] if o[0] == "ind" else []) + list(also), [o[1] if o[0] == "ind" else o], vdur(o, [i]))
 
     def tt(o, a, b, f):
-        op("v", lambda: g.vector.tensor_tensor(M(o), M(a), M(b), f), [a, b], [o])
+        node("v", [lambda: g.vector.tensor_tensor(M(o), M(a), M(b), f)], [a, b], [o], vdur(o, [a, b], 2 if a[0] in WID and b[0] in WID else 1))
 
     def ts(o, a, s1, f1, s2=None, f2=None):
-        if f2 is None:
-            op("v", lambda: g.vector.tensor_scalar(M(o), M(a), M(s1), None, f1), [a, s1], [o])
-        else:
-            op("v", lambda: g.vector.tensor_scalar(M(o), M(a), M(s1), M(s2), f1, f2), [a, s1, s2], [o])
+        more = () if f2 is None else (f2,)
+        node("v", [lambda: g.vector.tensor_scalar(M(o), M(a), M(s1), M(s2), f1, *more)], [a, s1, s2], [o], vdur(o, [a]))
 
     def ms(o, c):
-        op("v", lambda: g.vector.memset(M(o), c), [], [o])
+        node("v", [lambda: g.vector.memset(M(o), c)], [], [o], vdur(o, []))
 
-    def red(o, a, f):
-        op("v", lambda: g.vector.tensor_reduce(M(o), M(a), AxisListType.X, f), [a], [o])
+    def turn(o, a):
+        node("v", [lambda: g.vector.transpose(M(o), M(a))], [a], [o], vdur(o, [a]))
 
-    def act(o, i, f, bias=None, scale=None, accum=None):
-        kw = {}
-        if bias is not None:
-            kw["bias"] = bias
-        if scale is not None:
-            kw["scale"] = scale
-        if accum is not None:
-            kw["accum_out"] = accum
-        op("s", lambda: g.scalar.activation(M(o), M(i), f, **dict((k, M(v)) for k, v in kw.items())), [i, bias, scale], [o, accum])
+    def scan(o, d0, d1, f0=OP.mult, f1=OP.add):
+        node("v", [lambda: g.vector.tensor_tensor_scan(M(o), M(d0), M(d1), 0.0, f0, f1)], [d0, d1], [o], vdur(o, [d0, d1]))
 
-    def mm(o, l, rh, st=True, sp=True):
-        op("t", lambda: g.tensor.matmul(M(o), M(l), M(rh), st, sp), [l, rh], [o])
+    def act(o, i, f=AF.Identity, bias=None, scale=None, accum=None):
+        kw = dict((k, v) for k, v in (("bias", bias), ("scale", scale), ("accum_out", accum)) if v is not None)
+        node("s", [lambda: g.scalar.activation(M(o), M(i), f, **dict((k, M(v)) for k, v in kw.items()))], [i, bias, scale], [o, accum],
+             0.065 + foot(o)[2] * CY * (GATHER if i[0] == "ind" else 1) + (0.02 if accum else 0))
+
+    def mms(l):
+        node("t", [(lambda x: lambda: g.tensor.matmul(M(x[0]), M(x[1]), M(x[2]), x[3], x[4]))(x) for x in l], [a for x in l for a in x[1:3]], [x[0] for x in l],
+             sum(max(min(64, foot(x[1])[2]), foot(x[2])[2]) * (4 if WID[x[1][0]][1] == F32 else 1) for x in l) * CY)
 
     def toW(o, z, name, c0, c1):
-        for a in range(16):
-            mm(o, A(z, 15 - a, 143 - a), A(name, c0 + a, c1, 16), a == 0, a == 15)
+        for a0 in range(0, 16, 4):
+            mms([(o, A(z, 15 - a, 143 - a), A(name, c0 + a, c1, 16), a == 0, a == 15) for a in range(a0, a0 + 4)])
 
-    def scan(o, d0, d1):
-        op("v", lambda: g.vector.tensor_tensor_scan(M(o), M(d0), M(d1), 0.0, OP.mult, OP.add), [d0, d1], [o])
+    def quad(o, ps, z, srcs):
+        at = 0
+        for name, c0, c1 in srcs:
+            mms([(A(ps, at, at + (c1 - c0) // 4), A(z, 128 * a, 128 * a + 128), A(name, c0 + a, c1, 4), a == 0, a == 3) for a in range(4)])
+            at += (c1 - c0) // 4
+        scan(A(o, 0, at), A("MQ", 0, at), A(ps, 0, at), OP.add, OP.max)
+        return lambda b0, b1, st=1: A(o, 4 * b0 + 3, 4 * b1, 4 * st)
 
-    def dma(e, name, o, i):
-        op(e, lambda: Q[e].dma_start(M(o), M(i)), [i], [o], dma=name)
+    def dma(e, name, o, i, nbytes):
+        n = node(e, [lambda: Q[e].dma_start(M(o), M(i))], [i, o], [], 0.05, ("d" + name, 16), dict((m, 0.0) for m in fifo[0]))
+        x = node("d", [], [], [], nbytes / RATE + 8 * ROW, None, dict([(n, LOAD)] + [(m, 0.0) for m in fifo[1]]))
+        node("l", [], [], [i, o], 0.0, ("d" + name, 16), {x: 0.0})
+        fifo[0], fifo[1] = ([], []) if name[0] == "y" or name == "g4" else ([n], [x])
 
-    def iota(o, pat, cm):
-        if WID[o[0]][1] == I32:
-            op("g", lambda: g.iota(M(o), pat, 0, cm), [], [o])
-        else:
-            op("g", lambda: g.iota(M(o), pat, 0, cm, allow_small_or_imprecise_dtypes=True), [], [o])
+    def iota(o, pat, cm, base=0):
+        kw = {} if WID[o[0]][1] == I32 else {"allow_small_or_imprecise_dtypes": True}
+        node("g", [lambda: g.iota(M(o), pat, base, cm, **kw)], [], [o], 0.13 + 2 * CY * foot(o)[2])
 
     peer = [T.cores[(r + 1 + c) % N] for c in range(N - 1)]
     did = [DstId(rid=topo.addr(p)[0], pnc=topo.addr(p)[1]) for p in peer]
@@ -179,53 +256,86 @@ def rank_program(g, core, T, topo):
     def mask_of(l):
         return sum(1 << e for e in l)
 
-    def send1(c, dst, src, sem):
-        ad = topo.addr(peer[c])
-        op("g", lambda: g.remote_dma(M(dst), M(src), T.sem[sem], T.sem.ls, ad[1], ad[0], mask_of(eng)), [src], [], send=ne)
+    def send(sem, trs, lands, count):
+        nloc[0] += sum(len(x[1]) for x in trs)
+        n = node("g", [lambda: g.remote_dma_fused([RemoteDMATransfer(dst_ids=[did[c] for c in x[0]], dma_engine_mask=mask_of(x[1]), remote_sem=T.sem[sem],
+                                                                     srcs=[M(x[2])], dsts=[M(d) for d in x[3]]) for x in trs], local_sem=T.sem.ls)],
+                 [x[2] for x in trs], [], ISSUE, "send")
+        x = node("d", [], [], [], ROW * max(128 * len(x[0]) // len(x[1]) for x in trs), None, {n: START})
+        node("l", [], [], lands, 0.0, (sem, count), {x: LAND})
 
-    def send2(dsts, srcs, sem):
-        parts = [eng[:ne // 2], eng[ne // 2:]]
-        op("g", lambda: g.remote_dma_fused([RemoteDMATransfer(dst_ids=[did[c]], dma_engine_mask=mask_of(parts[c]), remote_sem=T.sem[sem],
-                                                              src=M(srcs[c]), dst=M(dsts[c])) for c in range(2)], local_sem=T.sem.ls), srcs, [], send=ne)
-        lands(sem, ne, dsts)
+    def send_all(sem, src, dsts, lands):
+        send(sem, [([0, 1, 2], eng, src, dsts)], lands, ne * (N - 1))
 
-    def send_all(a, sem, regions):
-        op("g", lambda: g.remote_dma_fused([RemoteDMATransfer(dst_ids=did, dma_engine_mask=mask_of(eng), remote_sem=T.sem[sem],
-                                                              srcs=[M(a)], dsts=[M(a)] * (N - 1))], local_sem=T.sem.ls), [a], [], send=ne)
-        lands(sem, ne * (N - 1), regions)
-
-    def send3(dsts, srcs, sem):
-        parts = [eng[:ne // 4], eng[ne // 4:ne // 2], eng[ne // 2:]]
-        op("g", lambda: g.remote_dma_fused([RemoteDMATransfer(dst_ids=[did[c]], dma_engine_mask=mask_of(parts[c]), remote_sem=T.sem[sem],
-                                                              src=M(srcs[c]), dst=M(dsts[c])) for c in range(3)], local_sem=T.sem.ls), srcs, [], send=ne)
-        lands(sem, ne, dsts)
+    def send_slots(sem, src, name, c0, w):
+        send_all(sem, src, [A(name, c0 + w * (2 - c), c0 + w * (3 - c)) for c in range(3)], [A(name, c0, c0 + 3 * w)])
 
     others = [(r + 1 + c) % N for c in range(3)]
+    own = others + [r]
     col = lambda n, j: A(n, j, j + 1)
 
-    dma("y", "pa", A("pa32"), T.pa[:])
-    dma("y", "bt", A("btc", 0, 512), T.bt[:])
-    dma("y", "co", A("btc", 512, 1024), T.co[:])
-    dma("s", "xv", A("xs"), T.xv[:])
-    dma("s", "cd", A("cds"), T.cd[:])
-    dma("y", "k0", A("kcs", 0, C // 2), T.kc[:, 0:C // 2])
-    dma("s", "k1", A("kcs", C // 2, C), T.kc[:, C // 2:C])
+    dma("y", "pa", A("pa32"), T.pa[:], 49152)
+    dma("s", "bt", A("btc", 0, 512), T.bt[:], 262144)
+    dma("y", "co", A("btc", 512, 1024), T.co[:], 262144)
+    dma("s", "xv", A("xs"), T.xv[:], 393216)
+    dma("y", "cd", A("cds"), T.cd[:], 786432)
+    dma("y", "k0", A("kcs", 0, C // 2), T.kc[:, 0:C // 2], 1048576)
+    dma("s", "k1", A("kcs", C // 2, C), T.kc[:, C // 2:C], 1048576)
     iota(col("pi", 0), [[1, 1]], 1)
-    iota(A("lo"), [[1, 256]], 0)
     iota(col("pi", 1), [[1, 1]], 4)
-    iota(A("io256"), [[256, V]], 0)
+    iota(A("lo"), [[1, 256]], 0)
+    iota(A("io256"), [[256, VX]], 0)
+    iota(A("Y"), [[4, 8], [0, 4], [1, 4]], 0)
+    iota(A("hq"), [[0, 32], [1, 4]], 0)
+    iota(A("TG"), [[1, 4 * L]], 0, -256)
+    iota(A("M16x"), [[0, 96], [1, 16]], 0)
     ts(col("pj", 0), col("pi", 0), 15, OP.bitwise_and)
     ts(col("pj", 1), col("pi", 0), 112, OP.bitwise_and)
-    cp(A("cf", 0, 2), A("pj", 0, 2))
+    ts(col("pj", 2), col("pi", 0), 3, OP.logical_shift_right, 12, OP.bitwise_and)
+    ts(col("pj", 3), col("pi", 1), 112, OP.bitwise_and)
+    ts(col("pj", 4), col("pi", 0), 3, OP.bitwise_and)
+    ts(col("pj", 5), col("pi", 0), 2, OP.logical_shift_right, 3, OP.bitwise_and)
+    cp(A("cf", 0, 6), A("pj", 0, 6))
     ts(A("M16"), A("lo", 0, 16), col("cf", 0), OP.is_equal)
     ts(A("Z"), A("lo", 0, 144), -15.0, OP.add, col("cf", 1), OP.is_equal)
-    cp(col("cf", 5), col("M16", 6))
+    for j, lim in enumerate((3.0, 6.0, 8.0)):
+        ts(col("cf", 6 + j), col("cf", 0), lim, OP.is_lt)
+    tt(A("cf", 9, 11), A("cf", 7, 9), A("cf", 6, 8), OP.subtract)
+    cp(col("cf", 11), col("M16", 6))
+    ts(col("cf", 12), col("cf", 2), col("cf", 3), OP.add, col("cf", 4), OP.add)
+    ts(col("cf", 13), col("cf", 5), 3.0, OP.is_lt, -BIG, OP.mult)
+    ts(col("cf", 14), col("cf", 1), 0.25, OP.mult)
+    ts(col("cf", 21), col("M16", 0), -262144.0, OP.mult)
+    tt(col("cf", 15), col("cf", 21), col("M16", 3), OP.subtract)
+    ts(col("cf", 16), col("cf", 13), 32768.0, OP.add)
+    ts(col("cf", 17), col("cf", 13), 1.0 / 16, OP.mult, 256.0, OP.add)
+    for t in range(R - 1):
+        ts(col("cf", 18 + t), col("cf", 13), 16.0 * (272 - 128 * t), OP.add)
+    for t in range(R):
+        ts(col("cf", 22 + t), col("cf", 13), 1.0 / 16, OP.mult, 1.0 - 128 * t, OP.add)
+    ts(col("cf", 26), col("cf", 13), 256.0, OP.add)
     ts(A("hic"), A("lo", 0, 32), 256.0, OP.mult, col("M16", 7), OP.mult)
     for m in range(32):
-        if m % 2:
-            act(A("dig", 256 * m, 256 * m + 256), A("lo"), AF.Identity, bias=col("hic", m), scale=col("cf", 5))
+        if m % 3 == 2:
+            act(A("dig", 256 * m, 256 * m + 256), A("lo"), bias=col("hic", m), scale=col("cf", 11))
         else:
-            ts(A("dig", 256 * m, 256 * m + 256), A("lo"), col("cf", 5), OP.mult, col("hic", m), OP.add)
+            ts(A("dig", 256 * m, 256 * m + 256), A("lo"), col("cf", 11), OP.mult, col("hic", m), OP.add)
+    ms(A("dig", C, CX), 0.0)
+    cp(col("dig", C), col("cf", 15))
+    ts(col("dig", C + 17), col("M16", 2), 524288.0, OP.mult)
+    ms(A("kcs", C, CX), 0.0)
+    ts(A("laneW"), A("lo", 0, 32), 16.0, OP.mult, col("cf", 0), OP.add)
+    cp(A("sU", 0, 8), A("pa32", 0, 8))
+    cp(A("pF", 0, 96), A("pa32"))
+    cp(B("pS", S(0, 4), S(0, 16)), A("pa32", 32, 96))
+    cp(B("pS", S(0, 4), S(16, 18)), A("pa32", 0, 8))
+    cp(B("xsP", ALL, S(0, 256)), A("xs", 512, V), "s")
+    for t in range(R - 1):
+        cp(B("xsP", ALL, S(256 + 32 * t, 288 + 32 * t)), A("xs", 128 * t, 128 * t + 128), "s")
+    ts(A("Sel", 0, 8), A("Z", 15, 128, 16), col("cf", 6), OP.mult, -1.0, OP.mult)
+    cp(A("Sel", 8, 16), A("Sel", 0, 8))
+    for j in range(2):
+        ts(A("Sel", 16 + 8 * j, 24 + 8 * j), A("Z", 15, 128, 16), col("cf", 9 + j), OP.mult)
 
     def xmask(t, ty, src):
         for gg in range(8):
@@ -234,386 +344,361 @@ def rank_program(g, core, T, topo):
 
     def keys(sU, sF):
         tt(A("keyR"), IND(A("io256"), sU), A("lo", 0, 128), OP.add)
-        act(A("kb", 8, 16), sF, AF.Identity, bias=-0.5, scale=256.0)
-        tt(A("kb", 0, 8), A("kb", 8, 16), A("laneW"), OP.add)
+        act(A("kb", 8, 16), sF, bias=-0.5, scale=256.0)
+        tt(A("kb", 0, 8), A("kb", 8, 16), A("laneW", 0, 8), OP.add)
 
-    def counts(bs):
-        for b in [b + 8 for b in bs] + bs:
-            act(A("junk", 128 * b, 128 * b + 128), A("keyR"), AF.Sign, bias=col("kb", b), scale=-1.0, accum=col("acc", b))
+    def counts(bs, whole=False):
+        for b in bs:
+            w = 128 if whole else 16 * b + 16
+            for j in (b + 8, b):
+                act(A("junk", 128 * j, 128 * j + w), A("keyR", 0, w), AF.Sign, bias=col("kb", j), scale=-1.0, accum=col("acc", j))
 
-    ts(A("laneW"), A("lo", 0, 8), 16.0, OP.mult, col("cf", 0), OP.add)
-    cp(A("pU", 0, 96), A("pa32"))
-    cp(A("pF"), A("pa32"))
-    for j, lim in enumerate((3.0, 6.0, 8.0)):
-        ts(col("cf", 6 + j), col("cf", 0), lim, OP.is_lt)
-    ts(col("pj", 2), col("pi", 0), 3, OP.logical_shift_right, 12, OP.bitwise_and)
-    ts(col("pj", 3), col("pi", 1), 112, OP.bitwise_and)
-    ts(col("pj", 4), col("pi", 0), 3, OP.bitwise_and)
-    tt(A("cf", 9, 11), A("cf", 7, 9), A("cf", 6, 8), OP.subtract)
-    ts(col("cf", 11), col("cf", 0), -16384.0, OP.mult, 262144.0, OP.add)
-    cp(A("cf", 2, 5), A("pj", 2, 5))
-    for j, m in enumerate((6, 9, 10)):
-        ts(A("Sel", 8 * j, 8 * j + 8), A("Z", 15, 128, 16), col("cf", m), OP.mult)
-    keys(A("pU", 0, 8), A("pF", 0, 8))
-    counts([2 * r, 2 * r + 1])
-    cp(A("ps0"), A("btc", 0, 512))
+    def lists(t, src, c0, st):
+        cp(A("WL", 32 * t, 32 * t + 16, 2), A(src, c0, c0 + 8 * st, st))
+        cp(A("XL", 16 * t + 1, 16 * t + 16, 2), A(src, c0, c0 + 8 * st, st))
+        if t < 2:
+            cp(A("WL", 32 * t + 16, 32 * t + 32 - 8 * t), A(src, c0 + 8 * st, c0 + (24 - 8 * t) * st, st))
+
+    keys(A("sU", 0, 8), A("pF", 0, 8))
+    counts([2 * r, 2 * r + 1], True)
     tt(A("fst", 4 * r, 4 * r + 2), A("acc", 2 * r, 2 * r + 2), A("acc", 8 + 2 * r, 10 + 2 * r), OP.is_equal)
-    send_all(A("fst", 4 * r, 4 * r + 2), "f0", [A("fst", 4 * o, 4 * o + 2) for o in others])
-    iota(A("M16x"), [[0, 96], [1, 16]], 0)
-    cp(A("ps1"), A("btc", 512, 1024))
-    cp(A("dg5", 0, 512), A("ps0"), "s")
-    cp(A("dg5", 1024, 1536), A("ps1"), "s")
-    tt(A("dg5", 512, 1024), A("ps0"), A("dg5", 0, 512), OP.subtract)
-    tt(A("ps2"), A("ps1"), A("dg5", 1024, 1536), OP.subtract)
-    cp(A("dg5", 1536, 2048), A("ps2"), "s")
-    xmask(0, 0, A("xs", 0, 128))
-    tt(A("dg5", 2048, 2560), A("ps2"), A("dg5", 1536, 2048), OP.subtract)
+    send_all("f0", A("fst", 4 * r, 4 * r + 2), [A("fst", 4 * r, 4 * r + 2)] * 3, [A("fst", 4 * o, 4 * o + 2) for o in others])
+    lists(0, "pF", 8, 1)
+    cp(A("ps5"), A("btc", 0, 512))
+    cp(A("ps6"), A("btc", 512, 1024))
+    cp(A("dg5", 0, 512), A("ps5"), "s")
+    cp(A("dg5", 1024, 1536), A("ps6"), "s")
+    tt(A("dg5", 512, 1024), A("ps5"), A("dg5", 0, 512), OP.subtract)
+    tt(A("ps7"), A("ps6"), A("dg5", 1024, 1536), OP.subtract)
+    cp(A("dg5", 1536, 2048), A("ps7"), "s")
+    tt(A("dg5", 2048, 2560), A("ps7"), A("dg5", 1536, 2048), OP.subtract)
     for d, row in enumerate((0, 1, 3, 4, 5)):
-        dma("y", "g%d" % d, A("dig", 0, C, 1, row, 128, 16), A("dg5", 512 * d, 512 * d + 512))
-    for name, c in (("who", 512.0), ("KS", 0.0)):
-        act(A(name, 0, V), A("xs"), AF.Identity, bias=c, scale=0.0)
-        act(A(name, V, 1664), A("lo", 0, 128), AF.Identity, bias=c, scale=0.0)
-    ts(col("cf", 12), col("cf", 2), col("cf", 3), OP.add, col("cf", 4), OP.add)
-    ts(col("cf", 13), col("M16", 2), 524288.0, OP.mult)
-    ms(A("tiny"), 0.0)
-    ts(A("dumpW"), A("laneW"), float(V), OP.add)
+        dma("y", "g%d" % d, A("dig", 0, C, 1, S(row, 128, 16)), A("dg5", 512 * d, 512 * d + 512), 131072)
+    for t in range(R):
+        xmask(t, 0, A("xs", 128 * t, 128 * t + 128))
+        ms(A("ps%d" % t, 0, 256 if t == 3 else 128), 0.0)
+        ts(A("o1", 16 * t + 1, 16 * t + 16, 2), A("laneW", 0, 8), float(V), OP.add)
+    for name in ("who", "ov"):
+        act(A(name), A("io256"), bias=-512.0, scale=0.0)
+    ms(A("KS"), 0.0)
+    act(A("DS"), A("io256", 0, 4 * LX), bias=col("cf", 15), scale=0.0)
+    ms(A("Kc", 0, 16), 0.0)
+    ms(A("o0"), 0.0)
+    ms(A("w0"), 0.0)
+    ts(A("lane16"), A("laneW", 0, 8), 16.0, OP.add)
+    for t in range(R - 1):
+        ts(A("WL", 32 * t + 1, 32 * t + 16, 2), A("laneW", 8 * t + 8, 8 * t + 16), 0.0, OP.add)
+    ts(A("XL", 0, 48, 2), A("laneW", 8, 32), 0.0, OP.add)
     ts(A("Perm"), A("lo", 0, 128), col("cf", 12), OP.is_equal)
-    ts(A("tiny", 1, 48, 2), A("lo", 0, 24), 0.0, OP.mult, col("cf", 13), OP.add)
-    ts(col("tiny", 0), col("cf", 13), 1.5, OP.mult)
-    ts(A("Z2"), A("Z"), col("cf", 6), OP.mult)
-    ts(A("Z3"), A("Z"), col("cf", 9), OP.mult)
-    cp(A("cf", 16, 24), A("Z", 15, 128, 16))
-    ms(A("d0s"), 0.0)
-    cp(A("DS", 512, 528), A("tiny", 0, 16))
-    for t in range(R):
-        ts(A("D1b", 8 * t, 8 * t + 8), A("laneW"), 128.0 * t - 512, OP.add)
+    for z, c in (("Z1", col("M16", 0)), ("Z2", col("cf", 6)), ("Z3", col("cf", 9))):
+        ts(A(z), A("Z"), c, OP.mult)
+    for a in range(4):
+        ts(A("Q", 128 * a, 128 * a + 128), A("Y"), -float(a), OP.add, col("cf", 14), OP.is_equal)
+    ts(A("Q1"), A("Q"), col("M16", 0), OP.mult)
+    ts(A("Q2"), A("Q"), col("cf", 6), OP.mult)
+    ts(A("hq2"), A("hq"), -1.0, OP.add, col("cf", 5), OP.is_equal)
+    ts(A("MQ"), A("hq"), col("cf", 5), OP.is_equal, -4.0, OP.mult)
+    tt(A("hq"), A("hq2"), A("MQ"), OP.add)
+    ts(A("MQ"), A("hq"), BIG, OP.mult)
+    ts(A("M16x"), A("M16x"), col("cf", 0), OP.is_equal, 16.0, OP.mult)
+    for name in ("side", "cutp", "sd", "sg3"):
+        ms(B(name), 0.0)
+    ms(B("negc"), 1.0)
+    ms(A("nfl"), 0.0)
+    ms(A("M18"), 0.0)
+    ms(A("M18", 17, 19), 4 * BIG)
+    ms(B("side", S(0, 4, 2), S(17, 19)), -16.0)
+    ms(B("cutp", ALL, 0), float(C))
+    ms(A("d0b"), 0.0)
+    ms(A("d0u"), 0.0)
+    ms(A("cond"), 0.0)
 
-    def late_constants():
-        ts(A("M16x"), A("M16x"), col("cf", 0), OP.is_equal, 16.0, OP.mult)
-        ms(A("Kc"), 0.0)
-        ms(A("DS", 0, 512), 0.0)
-        ms(A("d0b"), 0.0)
-        ts(A("idt"), A("lo", 0, 128), 1.0, OP.add)
+    def sums(f, f0, land, th, x1, x2, out, n, op):
+        ts(A(f, f0, f0 + 3 * n), land, -32768.0, OP.add)
+        tt(x1, A(f, f0, f0 + n), A(f, f0 + n, f0 + 2 * n), OP.add)
+        tt(x2, th, A(f, f0 + 2 * n, f0 + 3 * n), OP.subtract)
+        tt(out, x1, x2, op)
 
-    def sfill(name, t, c):
-        act(A(name, 1664 * t, 1664 * t + 1664), A("kcs", 0, 1664), AF.Identity, bias=c, scale=0.0)
+    def band(w, d):
+        act(w, d, AF.Abs, bias=262143.5)
 
-    def spare_work(t):
-        for gg in range(8):
-            c0 = 2048 * (t + 1) + 128 * gg
-            act(A("XM", c0, c0 + 128), A("xs", 128 * t + 128, 128 * t + 256), AF.Identity, scale=col("cf", 16 + gg))
-        sfill("who", t + 1, 512.0 - 128 * (t + 1))
-
-    def parts(f, land, w, n):
-        for o0, o1 in ((0, r), (r + 1, N)) if n == w else [(o, o + 1) for o in others]:
-            if o0 < o1:
-                ts(A(f, w * o0, w * (o1 - 1) + n), A(land[0], land[1] + w * o0, land[1] + w * (o1 - 1) + n), -32768.0, OP.add)
-
-    def decode(n, ps="ps7"):
-        ts(A("tm", 0, n), A(ps, 0, n), 262144.0, OP.is_gt, -524288.0, OP.mult)
-        ts(A("sg", 0, n), A(ps, 0, n), 262144.0, OP.is_gt)
-        tt(A("thr", 0, n), A(ps, 0, n), A("tm", 0, n), OP.add)
-
-    def route1(t):
-        cp(A("valU"), A("m3"))
-        tt(A("ovR"), IND(A("lo"), A("valU")), A("idt"), OP.mult)
-
-    def route2(t):
-        cp(IND(A("ov", 1664 * t, 1664 * t + 1664), A("offU", 8 * t, 8 * t + 8)), A("ovR"))
-
-    def route3(t, b0, n, ps):
-        lanes = b0 <= 8 * t < b0 + n
-        for c0, c1 in ((0, 8 * t - b0), (8 * t - b0 + 8, n)) if lanes else ((0, n),):
-            if c0 < c1:
-                ts(A("d0b", 3 * c0 + 2, 3 * c1, 3), A(ps, c0, c1), 0.5, OP.is_lt)
-                ts(A("d1b", 3 * c0 + 2, 3 * c1, 3), A(ps, c0, c1), 1.0 / 16, OP.mult, 128.0 * t - 1, OP.add)
-
-    def route_lanes(t, b0, n):
-        if b0 <= 8 * t < b0 + n:
-            j = 3 * (8 * t - b0) + 2
-            ts(A("d0b", j, j + 22, 3), A("m3"), -1.0, OP.mult, 1.0, OP.add)
-            tt(A("val"), A("upF", 8 * t, 8 * t + 8), A("m3"), OP.mult)
-            ts(A("d1b", j, j + 22, 3), A("val"), 128.0 * t - 1, OP.add)
-
-    def first_step(t, n, l1, p):
-        ts(A("d1b", 1, 3 * n, 3), l1, 1.0, OP.add)
-        ts(A("ovt", 0, n), p, 1.0 - 128 * t, OP.add)
-        tt(A("d1b", 0, 3 * n, 3), A("ovt", 0, n), A("d1b", 1, 3 * n, 3), OP.subtract)
-
-    def sides(n, f, o, m0):
-        tt(A("t1", 0, n), A(f, o[0], o[0] + n), A(f, o[1], o[1] + n), OP.add)
-        tt(A("t2", 0, n), A("th2", m0, m0 + n), A(f, o[2], o[2] + n), OP.subtract)
-        tt(A("sd", 0, n), A("t1", 0, n), A("t2", 0, n), OP.is_gt)
+    def swaps(d0, d1, j0, ps, cc):
+        n = foot(ps)[2]
+        if ps[0] in WID:
+            ts(A(d0, 3 * j0 + 2, 3 * (j0 + n), 3), ps, col("cf", 13), OP.add, cc - 255.5, OP.is_lt)
+        else:
+            ts(A(d0, 3 * j0 + 2, 3 * (j0 + n), 3), ps, cc - 255.5, OP.is_lt)
+        ts(A(d1, 3 * j0 + 2, 3 * (j0 + n), 3), ps, col("cf", 26) if ps[0] in WID else 256.0, OP.add, cc, OP.max)
 
     for t in range(R):
-        last, u = t == R - 1, t - 1
-        sU = A("pU", 0, 8) if t == 0 else A("sU", 8 * t, 8 * t + 8)
-        pU = lambda b0, b1: A("pU", 96 * t + b0, 96 * t + b1)
-        who = A("who", 1664 * t, 1664 * t + 1664)
-        dummy = 512.0 - 128 * t
+        last = t == R - 1
+        pS = lambda o, n, u=t: B("pS", 4 * u + o, S(0, n))
+        pF = lambda b0, b1, u=t: A("pF", 96 * u + b0, 96 * u + b1)
+        nb, cc, halves = 8 * t + 8, 128.0 * t - 1, ((0, 64), (64, 96))
+        nf, m = max(16 - 8 * t, 0), 18 + 2 * t
+        sU = A("sU", 8 * t, nb)
+        sF = pF(0, 8) if t == 0 else A("sos", 2, 24, 3)
+        tags = A("TG", L * t, L * t + L)
         cp(A("cU"), IND(A("cds"), sU))
         cp(A("xsg"), IND(A("xs"), sU), "s")
         xmask(t, 1, A("xsg"))
-        own = [(r + 1 + c) % N for c in range(N)]
 
         def kg(c, e, l0=0, l1=32):
             o = own[c]
             cp(A("Kg", 512 * o + 16 * l0, 512 * o + 16 * l1), IND(A("kcs"), A("cU", 32 * o + l0, 32 * o + l1)), e)
 
-        def lanes_mm(ps, name, l00, rhs, n):
-            for h in (1, 0):
-                for a in range(16):
-                    l, q, B = l00 + 16 * h + a, a // 4, a % 4
-                    mm(A(ps, B, 4 * n, 4, 32 * q, 32 * q + 16 + 16 * h), A(name, 16 * (l - h), 16 * l + 16), rhs(l))
+        def spot(ps, c0, l):
+            bb, q, b = l // 16, l % 16 // 4, l % 4
+            return A(ps, c0 + 64 * bb + b, c0 + 64 * bb + 64, 4, S(32 * q, 32 * q + 16))
 
-        def pe(c):
-            lanes_mm("ps%d" % c, "Kg", 32 * own[c], lambda l: A("XM", 2048 * t + l, 2048 * t + 2048, 128), 16)
+        def lane_mm(ps, l, stop=True):
+            return (spot(ps, 0, l % 32), A("Kg", 16 * l, 16 * l + 16), A("XM", 2048 * t + l, 2048 * t + 2048, 128), True, stop)
 
         def out_a(c):
             a0 = 192 * t + 64 * c
-            ts(A("SA", a0, a0 + 64), A("ps%d" % c, 0, 64), 32768.0, OP.add)
-            if c == 1:
-                send2([A("LA", a0 - 64, a0), A("LA", a0, a0 + 64)], [A("SA", a0 - 64, a0), A("SA", a0, a0 + 64)], "a%d0" % t)
-            if c == 2:
-                send1(c, A("LA", a0, a0 + 64), A("SA", a0, a0 + 64), "a%d1" % t)
-                lands("a%d1" % t, ne, [A("LA", a0, a0 + 64)])
+            turn(B("TR", S(4 * c, 4 * c + 4)), A("ps%d" % c, 0, 128))
+            ts(A("SA", a0, a0 + 64), B("TR", S(4 * c, 4 * c + 4), S(0, 16)), 32768.0, OP.add)
 
-        sF = A("pF", 0, 8) if t == 0 else A("sos", 2, 24, 3)
-        kg(0, "s", 14, 32)
-        kg(0, "s", 0, 14)
-        pe(0)
-        kg(1, "v")
-        kg(2, "s")
-        out_a(0)
-        if t:
-            route1(u)
-        pe(1)
-        kg(3, "s")
-        out_a(1)
-        pe(2)
-        if t:
-            route2(u)
-        out_a(2)
-        if t:
-            toW(A("ps5", 0, 24), "Z", "ov", 1664 * u + 384 * r, 1664 * u + 384 * r + 384)
-            keys(sU, sF)
-        pe(3)
+        piece = lambda n, c: A(n, 192 * t + 64 * c, 192 * t + 64 * c + 64)
+        for c, parts in enumerate(((("s", 0, 16), ("s", 16, 32)), (("v", 0, 32),), (("s", 0, 32),))):
+            for e, l0, l1 in parts:
+                kg(c, e, l0, l1)
+                mms([lane_mm("ps%d" % c, 32 * own[c] + l) for l in range(l0, l1)])
+            out_a(c)
+            if c == 1:
+                send("a%d0" % t, [([k], eng[k * ne // 2:(k + 1) * ne // 2], piece("SA", k), [piece("LA", k)]) for k in range(2)], [piece("LA", 0), piece("LA", 1)], ne)
+            if c == 2:
+                send("a%d1" % t, [([2], eng, piece("SA", 2), [piece("LA", 2)])], [piece("LA", 2)], ne)
         cp(A("Dg"), IND(A("dig"), A("cU", 32 * r, 32 * r + 32)), "s")
-        lanes_mm("ps4", "Dg", 0, lambda l: A("Sel"), 24)
-        if t:
-            route_lanes(u, 24 * r, 24)
-            ts(A("fB", 0, 72), A("LB", 72 * u, 72 * u + 72), -32768.0, OP.add)
-            sides(24, "fB", (0, 24, 48), 24)
-            tt(A("d0b", 1, 72, 3), A("sd", 0, 24), A("sg", 24, 48), OP.not_equal)
-            route3(u, 24 * r, 24, "ps5")
-            scan(A("sob", 0, 72), A("d0b", 0, 72), A("d1b", 0, 72))
-            cp(pU(24 * r, 24 * r + 24), A("sob", 2, 72, 3))
-            send_all(pU(24 * r, 24 * r + 24), "p%d" % u, [pU(24 * o, 24 * o + 24) for o in others])
-        else:
-            late_constants()
+        mms([(spot("ps3", 128, l), A("Dg", 16 * l, 16 * l + 16), A("Sel", 16, 32), True, True) for l in range(32)])
+        for e, l0, l1 in (("v", 0, 16), ("s", 16, 32)):
+            kg(3, e, l0, l1)
+            mms([x for l in range(l0, l1) for x in (lane_mm("ps3", 32 * r + l, False), (spot("ps3", 0, l), A("Dg", 16 * l, 16 * l + 16), A("Sel", 0, 16), False, True))])
+        turn(B("TO"), A("ps3", 0, 256))
+        act(B("negc", ALL, S(1, 17)), B("TO", S(4, 8, 2), S(0, 16)), bias=-8388608.0)
+        cp(B("cutp", ALL, S(1, 17)), B("TO", S(5, 8, 2), S(0, 16)), "s")
+        tt(A("d1c"), B("cutp", ALL, S(0, 18)), B("cutp", ALL, S(1, 19)), OP.subtract)
+        ts(A("ps3", 256, 384), A("LA", 192 * t, 192 * t + 128), -32768.0, OP.add)
+        tt(A("r1"), B("TO", S(0, 4), S(0, 16)), A("ps3", 256, 320), OP.add)
+        tt(A("rest"), A("r1"), A("ps3", 320, 384), OP.add)
+        ts(A("ps3", 384, 448), piece("LA", 2), -1.0, OP.mult, 32768.0, OP.add)
+        tt(B("side", ALL, S(1, 17)), A("rest"), A("ps3", 384, 448), OP.is_gt)
+        tt(A("ne"), B("side", S(0, 4, 2), S(0, 18)), B("side", S(1, 4, 2), S(0, 18)), OP.not_equal)
+        tt(A("d1e"), B("side", S(0, 4, 2), S(0, 18)), B("side", S(0, 4, 2), S(1, 19)), OP.subtract)
+        tt(A("key"), A("ne"), B("negc"), OP.mult)
+        scan(A("pm"), A("M18"), A("key"), OP.add, OP.min)
+        tt(A("nfl", 1, 36), A("key", 1, 36), A("pm", 0, 35), OP.is_ge)
+        scan(A("yq", 0, 36), A("nfl"), A("d1c"))
+        scan(A("yq", 36, 72), A("nfl"), A("d1e"))
+        mms([(A("ps2", 0, 4), A("Perm"), A("yq", 17, 72, 18), True, True)])
+        dl = lambda o, n=4: B("DL", 4 * t + o, S(0, n))
+        cp(dl(r), A("ps2", 0, 4))
+        send_all("e%d" % t, dl(r), [dl(r)] * 3, [dl(o) for o in others])
+        cond = A("cond", 9 * t + 1, 9 * t + 9)
         act(A("nl", 0, 8), sF, AF.Abs, bias=-128.0 * t - 63.5)
         if t:
-            counts(list(range(8)))
-        cp(A("uA"), A("ps3", 0, 64))
-        ts(A("sbU", 0, 8), sF, 1.0 / 16, OP.mult, -0.46875, OP.add)
-        tt(A("D1", 0, 8), sF, A("dumpW"), OP.subtract)
-        ts(A("nl", 8, 16), A("nl", 0, 8), 64.0, OP.is_gt)
-        cond = A("cond", 8 * t, 8 * t + 8)
-        if t:
-            tt(A("og"), A("acc", 0, 8), A("acc", 8, 16), OP.is_equal)
-        tt(A("fA", 0, 32), A("ps4", 0, 32), A("uA", 0, 32), OP.subtract)
-        tt(A("fA", 32, 64), A("ps4", 0, 32), A("uA", 32, 64), OP.subtract)
-        act(A("negc"), A("ps4", 32, 64), AF.Identity, bias=-8388608.0)
-        act(A("pay"), A("ps4", 64, 96), AF.Identity, bias=col("cf", 11))
-        if t:
-            tt(cond, A("og"), A("nl", 8, 16), OP.mult)
+            keys(sU, sF)
+            counts(range(8))
+            act(A("nl", 8, 16), A("nl", 0, 8), AF.Relu, bias=64.0, scale=-1.0)
+            tt(A("ap"), A("acc", 0, 8), A("nl", 8, 16), OP.add)
+            tt(A("o0", 1, 16, 2), A("ap"), A("acc", 8, 16), OP.is_le)
         else:
+            ts(A("nl", 8, 16), A("nl", 0, 8), 64.0, OP.is_gt)
             for h in range(2):
-                tt(A("cond", h, 8, 2), A("fst", h, 16, 4), A("nl", 8 + h, 16, 2), OP.mult)
-        ts(A("ps5", 128, 256), A("LA", 192 * t, 192 * t + 128), -32768.0, OP.add)
-        tt(A("fA", 64, 128), A("fA", 0, 64), A("ps5", 128, 192), OP.subtract)
+                tt(A("o0", 1 + 2 * h, 16, 4), A("fst", h, 16, 4), A("nl", 8 + h, 16, 2), OP.mult)
+        o1 = A("o1", 16 * t, 16 * t + 16)
+        tt(A("o1", 16 * t, 16 * t + 16, 2), sF, A("o1", 16 * t + 1, 16 * t + 16, 2), OP.subtract)
+        scan(A("og"), A("o0"), o1)
+        act(A("c18", 8 * t, nb), A("o0", 1, 16, 2), scale=262144.0)
+        offU = A("offU", 8 * t, nb)
+        cp(offU, A("og", 1, 16, 2))
+        cp(IND(A("who"), offU), tags)
+        cp(cond, A("o0", 1, 16, 2), "s")
+        if not last:
+            cp(A("Xsm"), IND(A("xs"), A("XL", 16 * t, 16 * t + 16)), "s")
+            cp(A("RB", 0, 256 + 16 * nf), IND(A("who"), A("WL", 32 * t, 32 * t + 16 + nf)), "s")
+            sq = quad("sqL", "ps1", "Q", [("RB", 0, 256 + 16 * nf)])
+            ts(A("LL", 0, 16 + nf), sq(0, 16 + nf), col("cf", 18 + t), OP.add, 1.0 / 16, OP.mult)
+            act(A("Lf", 0, 16 + nf), sq(0, 16 + nf), bias=col("cf", 17), scale=1.0 / 16)
+            cp(A("d1s", 2, 24, 3), A("Lf", 1, 16, 2), "s")
+            tt(A("d1s", 1, 24, 3), A("Lf", 0, 16, 2), A("Lf", 1, 16, 2), OP.subtract)
+            tt(A("d1s", 0, 24, 3), pF(nb, nb + 8), A("Lf", 0, 16, 2), OP.subtract)
+        if nf:
+            act(A("d1u", 1, 3 * nf, 3), A("Lf", 16, 16 + nf), bias=-cc)
+            tt(A("d1u", 0, 3 * nf, 3), pF(32 - nf, 32), A("Lf", 16, 16 + nf), OP.subtract)
+        ts(A("sbU"), sF, 1.0 / 16, OP.mult, -0.46875, OP.add)
         cp(A("mk"), IND(A("M16x"), sU), "s")
-        sfill("ov", t, 0.0)
-        tt(A("rest"), A("fA", 64, 128), A("ps5", 192, 256), OP.subtract)
-        ts(A("ps5", 256, 320), A("LA", 192 * t + 128, 192 * t + 192), -32768.0, OP.add)
-        tt(A("side"), A("ps5", 256, 320), A("rest"), OP.is_gt)
-        tt(A("kp", 64, 96), A("side", 0, 32), A("side", 32, 64), OP.not_equal)
-        ts(A("s8"), A("side", 0, 32), 8192.0, OP.mult)
-        tt(A("kp", 0, 32), A("kp", 64, 96), A("negc"), OP.mult)
-        tt(A("kp", 32, 64), A("s8"), A("pay"), OP.add)
-        op("v", lambda: g.vector.transpose(M(A("kpT")), M(A("kp"))), [A("kp")], [A("kpT")])
-        for h in range(2):
-            red(col("mn", h), A("kpT", 16 * h, 16 * h + 16), OP.min)
-            red(col("mn", 2 + h), A("kpT", 64 + 16 * h, 80 + 16 * h), OP.max)
-        for h in range(2):
-            ts(A("ee", 16 * h, 16 * h + 16), A("kpT", 16 * h, 16 * h + 16), col("mn", h), OP.is_equal, col("mn", 2 + h), OP.mult)
-        tt(A("ep"), A("ee"), A("kpT", 32, 64), OP.mult)
-        d0 = 16 * t + 4 * r
-        for h in range(2):
-            red(col("DC", d0 + h), A("ep", 16 * h, 16 * h + 16), OP.max)
-        send_all(A("DC", d0, d0 + 2), "e%d" % t, [A("DC", 16 * t + 4 * o, 16 * t + 4 * o + 2) for o in others])
-        tt(A("of", 0, 8), cond, A("D1", 0, 8), OP.mult)
-        tt(A("of", 8, 16), cond, A("D1b", 8 * t, 8 * t + 8), OP.mult)
-        tt(A("og"), A("of", 0, 8), A("dumpW"), OP.add)
-        ts(A("Lsm", 16, 24), A("of", 8, 16), dummy, OP.add)
-        offU = A("offU", 8 * t, 8 * t + 8)
-        cp(offU, A("og"))
-        cp(IND(who, offU), A("lo", 0, 128))
-        if t:
-            cp(A("pF"), pU(0, 96))
-        g0 = 0 if last else 256
-        tt(A("RB", g0, g0 + 128), IND(A("pF"), A("sbU", 0, 8)), A("mk"), OP.mult)
-        nb = 8 * t + 8
-        if not last:
-            cp(A("RB", 0, 128), IND(who, pU(nb, nb + 8)))
-            cp(A("RB", 128, 256), A("who", 1664 * t + 16 * nb, 1664 * t + 16 * nb + 128))
-            cp(A("Xsm", 0, 128), A("xs", 16 * nb, 16 * nb + 128), "s")
-            cp(A("Xsm", 128, 256), IND(A("xs"), pU(nb, nb + 8)), "s")
-            cp(A("L1R", 0, 384), IND(who, pU(24 * r, 24 * r + 24)), "s")
-            toW(A("ps5", 64, 88), "Z", "RB", 0, 384)
-            ts(A("upU"), A("ps5", 80, 88), 1.0 / 16, OP.mult)
-            ts(A("Lsm", 0, 16), A("ps5", 64, 80), 1.0 / 16, OP.mult)
-            ts(A("LFf", 0, 24), A("ps5", 64, 88), 1.0 / 16, OP.mult)
-            cp(A("Xsm", 256, 384), IND(A("xs"), A("upU")), "s")
-            act(A("l1v", 0, 8), A("LFf", 0, 8), AF.Identity, bias=128.0 * t)
-            act(A("d1s", 2, 24, 3), A("LFf", 8, 16), AF.Identity, bias=128.0 * t)
-            act(A("ovt", 0, 24), A("pF", 24 * r, 24 * r + 24), AF.Identity, bias=1.0 - 128 * t)
-            if r == 0:
-                act(A("upF", 8 * t, 8 * t + 8), A("LFf", 16, 24), AF.Identity, bias=1.0 - 128 * t)
-        else:
-            cp(A("L1R", 640, V), IND(who, pU(40, 96)), "s")
-            cp(A("RB", 128, 768), IND(who, pU(0, 40)))
-            toW(A("ps5", 64, 112), "Z", "RB", 0, 768)
-            ts(A("upU"), A("ps5", 64, 72), 1.0 / 16, OP.mult)
-            ts(A("L1F", 0, 40), A("ps5", 72, 112), 1.0 / 16, OP.mult)
-            ts(A("upF", 8 * t, 8 * t + 8), A("ps5", 64, 72), 1.0 / 16, OP.mult, 1.0 - 128 * t, OP.add)
-            cp(A("Xsm", 256, 384), IND(A("xs"), A("upU")), "s")
-            tt(A("L1F", 8 * t, nb), A("L1F", 8 * t, nb), A("of", 8, 16), OP.subtract)
-            cp(A("L1U", 0, 40), A("L1F", 0, 40))
-        mm(A("ps4", 0, 8), A("Perm"), A("DC", 16 * t, 16 * t + 16, -1))
+        tt(A("RU"), IND(pF(0, 96), A("sbU")), A("mk"), OP.mult)
+        sp = quad("sqP", "ps4", "Q", [("RU", 0, 128)])
+        ts(A("upU"), sp(0, 8), col("cf", 13), OP.add, 1.0 / 16, OP.mult)
+        cp(A("X3"), IND(A("xs"), A("upU")), "s")
+        n, jl, l0, l1 = (96, 24, 0, 8) if last else (m, m - 2, 2 * r, 2 * r + 2)
+        act(A("upF", l0, l1), sp(l0, l1), bias=col("cf", 22 + t), scale=1.0 / 16)
+        cl = A("cl", 8 * t + l0, 8 * t + l1)
+        tt(cl, A("cond", 9 * t + 1 + l0, 9 * t + 1 + l1), A("lane16", l0, l1), OP.mult)
+        ps = "ps1" if last else "ps7"
+        for b0, b1 in ((0, 32), (32, 64), (64, 96)) if last else ((0, n),):
+            cp(A("L1R", 16 * b0, 16 * b1), IND(A("who"), A("pN", b0, b1) if last else pS(r, m)), "s")
+        toW(A(ps, 256, 256 + n), "Z", "L1R", 0, 16 * n)
+        ts(A("L1U", 0, n), A(ps, 256, 256 + n), 1.0 / 16, OP.mult, 272.0 - 128 * t, OP.add)
+        act(A("L1F", l0, l1), A(ps, 256 + jl, 256 + jl + l1 - l0), bias=272.0 - 128 * t, scale=1.0 / 16)
+        tt(A("val", l0, l1), A("L1F", l0, l1), cl, OP.subtract)
+        cp(A("L1U", jl, jl + l1 - l0), A("val", l0, l1))
+        act(A("d1b", 1, 3 * n, 3), A(ps, 256, 256 + n), bias=256.0 - cc, scale=1.0 / 16)
         if last:
-            toW(A("ps1", 40, 96), "Z", "L1R", 640, V)
+            act(A("ovt"), pF(0, 96), bias=-cc)
         else:
-            toW(A("ps1", 0, 24), "Z", "L1R", 0, 384)
-        cp(A("ci"), A("ps4", 0, 8))
-        act(A("act", 8 * t, 8 * t + 8), A("ps4", 0, 8), AF.Sign)
-        ts(A("cc32", 0, 8), A("ci"), 8191, OP.bitwise_and)
-        ts(A("cc32", 8, 16), A("ci"), 13, OP.logical_shift_right)
-        cp(A("cx"), A("cc32"))
-        Kc, DS = A("Kc", 128 * t, 128 * t + 128), A("DS", 128 * t, 128 * t + 128)
-        cp(Kc, IND(A("kcs"), A("cx", 0, 8)))
-        cp(A("sgR"), IND(A("tiny"), A("cx", 8, 16)), "s")
-        DSw = A("DS", 128 * t, 528)
-        s0 = 16 if last else 0
-        ns = 24 - s0
-        tt(A("Psm", 16 * s0, 384), IND(A("Kc", 128 * t, 528), A("Lsm", s0, 24)), A("Xsm", 16 * s0, 384), OP.mult)
-        toW(A("ps6", 0, ns), "Z", "Psm", 16 * s0, 384)
-
-        def big(b0, b1):
-            tt(A("Pb", 16 * b0, 16 * b1), IND(A("KS"), pU(b0, b1)), A("xs", 16 * b0, 16 * b1), OP.mult)
-
-        if last:
-            cp(IND(A("KS"), offU), Kc)
-            tt(DS, IND(A("dig"), A("cx", 0, 8)), A("sgR"), OP.add)
-            ts(A("L1U", 40, 96), A("ps1", 40, 96), 1.0 / 16, OP.mult)
-            cp(A("DJ", 0, 128), IND(DSw, A("Lsm", 16, 24)), "s")
-            toW(A("ps7", 0, 8), "Z2", "DJ", 0, 128)
-            cp(A("DJ", 128, 128 + V), IND(DSw, A("L1U")), "s")
-            big(0, 16)
-        else:
-            tt(DS, IND(A("dig"), A("cx", 0, 8)), A("sgR"), OP.add)
-            if r == 0:
-                ts(A("LFf", 24, 48), A("ps1", 0, 24), 1.0 / 16, OP.mult)
-                tt(A("LFf", 24 + 8 * t, 32 + 8 * t), A("LFf", 24 + 8 * t, 32 + 8 * t), A("of", 8, 16), OP.subtract)
-                cp(A("L1U", 0, 24), A("LFf", 24, 48))
-            else:
-                ts(A("L1U", 0, 24), A("ps1", 0, 24), 1.0 / 16, OP.mult)
-            cp(IND(A("KS"), offU), Kc)
-        slot = lambda o: A("LS", 96 * t + 24 * o, 96 * t + 24 * o + ns)
-        ts(slot(r), A("ps6", 0, ns), 32768.0, OP.add)
-        send_all(slot(r), "s%d" % t, [slot(o) for o in others])
+            act(A("ovt", 0, jl), A("sob", 2, 3 * jl, 3) if t else pF(32 + 16 * r, 48 + 16 * r), bias=-cc)
+            act(A("ovt", jl, n), pF(8 * t + l0, 8 * t + l1), bias=-cc)
+        tt(A("d1b", 0, 3 * n, 3), A("ovt", 0, n), A("d1b", 1, 3 * n, 3), OP.subtract)
+        for o, e in zip(own, "vvss"):
+            cp(A("Kc", 16 + 32 * o, 48 + 32 * o), IND(A("kcs"), dl(o, 2)), e)
         if not last:
-            cp(A("DJ", 0, 384), IND(DSw, A("Lsm")), "s")
-            cp(A("DJ", 384, 768), IND(DSw, A("L1U", 0, 24)), "s")
-            toW(A("ps7", 0, 48), "Z2", "DJ", 0, 768)
-            spare_work(t)
-            big(0, 48)
-            toW(A("ps3", 0, 48), "Z", "Pb", 0, V // 2)
-            big(48, 96)
-            toW(A("ps3", 48, 96), "Z", "Pb", V // 2, V)
-            decode(48)
-            tt(A("th2", 0, 24), A("thr", 0, 24), A("ps6", 0, 24), OP.subtract)
-            ts(A("d1b", 1, 72, 3), A("L1U", 0, 24), 1.0, OP.add)
-            tt(A("d1s", 1, 24, 3), A("LFf", 0, 8), A("LFf", 8, 16), OP.subtract)
-            tt(A("d1s", 0, 24, 3), A("pF", nb, nb + 8), A("l1v", 0, 8), OP.subtract)
-            tt(A("d1b", 0, 72, 3), A("ovt", 0, 24), A("d1b", 1, 72, 3), OP.subtract)
-            ts(A("SB", 96 * t, 96 * t + 96), A("ps3", 0, 96), 32768.0, OP.add)
-            send3([A("LB", 72 * t + 24 * c, 72 * t + 24 * c + 24) for c in range(3)], [A("SB", 96 * t + 24 * o, 96 * t + 24 * o + 24) for o in others], "b%d" % t)
-            tt(A("th2", 24, 48), A("thr", 24, 48), A("ps3", 24 * r, 24 * r + 24), OP.subtract)
-            parts("fS", ("LS", 96 * t), 24, 24)
-            sides(24, "fS", [24 * o for o in others], 0)
-            tt(A("d0s", 1, 24, 3), A("sd", 0, 8), A("sg", 0, 8), OP.not_equal)
-            tt(A("d0s", 2, 24, 3), A("sd", 8, 16), A("sg", 8, 16), OP.not_equal)
+            tt(A("Psm"), IND(A("Kc"), A("LL", 0, 16)), A("Xsm"), OP.mult)
+            so = quad("sqO", "ps2", "Q", [("Psm", 0, 256)])
+            ts(A("SS", 16 * t, 16 * t + 16), so(0, 16), col("cf", 16), OP.add)
+            send_slots("s%d" % t, A("SS", 16 * t, 16 * t + 16), "LS", 48 * t, 16)
+        cp(A("cx", 0, 8), B("DL", S(4 * t, 4 * t + 4), S(0, 2)))
+        cp(A("cx", 8, 16), B("DL", S(4 * t, 4 * t + 4), S(2, 4)))
+        cp(A("sgR"), IND(A("dig", C, CX), A("cx", 8, 16)), "s")
+        tt(A("DS", LX * t + 16, LX * t + LX), IND(A("dig"), A("cx", 0, 8)), A("sgR"), OP.add)
+        DSw = A("DS", LX * t, LX * t + LX)
+        if not last:
+            cp(A("DJ", 0, 256), IND(DSw, A("LL", 0, 16)), "s")
+            st = quad("sqT", "ps0", "Q2", [("DJ", 0, 256)])
+            sg = B("sg3", ALL, S(1, 3))
+            ts(sg, st(0, 16), col("cf", 13), OP.add, 262144.0, OP.is_gt)
+            tt(A("uu"), st(0, 16), so(0, 16), OP.subtract)
+            act(A("tm"), sg, scale=-524288.0)
+            tt(A("th2"), A("uu"), A("tm"), OP.add)
+            sums("fS", 0, A("LS", 48 * t, 48 * t + 48), A("th2"), A("t1"), A("t2"), B("sd", ALL, S(1, 3)), 16, OP.is_gt)
+            tt(A("d0s"), B("sd"), B("sg3"), OP.not_equal)
             scan(A("sos"), A("d0s"), A("d1s"))
-            tt(A("m3"), A("sd", 16, 24), A("sg", 16, 24), OP.is_equal)
             cp(A("sU", nb, nb + 8), A("sos", 2, 24, 3))
+            cp(pF(nb, nb + 8, t + 1), A("sos", 2, 24, 3), "s")
+        nu = 8 + nf
+        tt(A("Pu", 0, 128), A("Kc", 16, LX), A("X3"), OP.mult)
+        if nf:
+            tt(A("Pu", 128, 16 * nu), IND(A("Kc"), A("LL", 16, 16 + nf)), A("xs", 16 * (32 - nf), 512), OP.mult)
+            cp(A("DJ", 256, 256 + 16 * nf), IND(DSw, A("LL", 16, 16 + nf)), "s")
+        su = quad("sqU", "ps4", "Q", [("Pu", 0, 16 * nu)])
+        ts(A("SU", 24 * t, 24 * t + nu), su(0, nu), col("cf", 16), OP.add)
+        send_slots("u%d" % t, A("SU", 24 * t, 24 * t + nu), "LU", 72 * t, nu)
+        sv = quad("sqV", "ps5", "Q2", [("DS", LX * t + 16, LX * t + LX)] + ([("DJ", 256, 256 + 16 * nf)] if nf else []))
+        tt(A("u0", 0, nu), sv(0, nu), su(0, nu), OP.subtract)
+        cp(IND(A("KS"), offU), A("Kc", 16, LX))
+        if last:
+            for h, (h0, h1) in enumerate(halves):
+                for b0 in range(h0, h1, 16):
+                    tt(A("Pb", 16 * b0, 16 * b0 + 256), IND(A("KS"), A("pN", b0, b0 + 16)), A("xs", 16 * b0, 16 * b0 + 256), OP.mult)
+                toW(A("ps%d" % (6 + h), 0, h1 - h0), "Z", "Pb", 16 * h0, 16 * h1)
+                sb = A("SB", 96 * t + h0, 96 * t + h1)
+                ts(sb, A("ps%d" % (6 + h), 0, h1 - h0), 32768.0, OP.add)
+                send_slots("z%d" % h, sb, "LF", 3 * h0, h1 - h0)
         else:
-            big(16, 48)
-            toW(A("ps3", 0, 48), "Z", "Pb", 0, V // 2)
-            big(48, 96)
-            toW(A("ps3", 48, 96), "Z", "Pb", V // 2, V)
-            toW(A("ps0", 0, 96), "Z2", "DJ", 128, 128 + V)
-            toW(A("ps4", 0, 32), "Z3", "DS", 0, 512)
-            decode(8)
-            ts(A("L1F", 40, 96), A("ps1", 40, 96), 1.0 / 16, OP.mult)
-            tt(A("th2", 0, 8), A("thr", 0, 8), A("ps6", 0, 8), OP.subtract)
-            tt(A("yc2"), A("act"), A("cond"), OP.mult)
-            fl = lambda o: A("LF", 96 * o, 96 * o + 96)
-            ts(fl(r), A("ps3", 0, 96), 32768.0, OP.add)
-            send_all(fl(r), "fin", [fl(o) for o in others])
-            first_step(t, 96, A("L1F"), A("pF"))
-            parts("fS", ("LS", 96 * t), 24, 8)
-            sides(8, "fS", [24 * o for o in others], 0)
-            tt(A("m3"), A("sd", 0, 8), A("sg", 0, 8), OP.is_equal)
-            route1(t)
-            route2(t)
-            toW(A("ps2", 0, 96), "Z", "ov", 1664 * t, 1664 * t + V)
-            decode(96, "ps0")
-            route_lanes(t, 0, 96)
-            tt(A("th2", 0, 96), A("thr", 0, 96), A("ps3", 0, 96), OP.subtract)
-            ts(A("yc1"), A("ps4", 0, 32), 1.0, OP.add)
-            tt(A("yc3"), A("yc1"), A("yc2"), OP.mult)
-            act(A("yc1"), A("yc3"), AF.Identity, bias=-1.0)
-            dma("s", "yc", T.yc[:], A("yc1"))
-            ts(A("ps1", 0, 96), fl(others[0]), -32768.0, OP.add)
-            ts(A("fB", 0, 96), fl(others[1]), -32768.0, OP.add)
-            ts(A("ps1", 96, 192), fl(others[2]), -32768.0, OP.add)
-            tt(A("ps1", 192, 288), A("ps1", 0, 96), A("fB", 0, 96), OP.add)
-            tt(A("t2"), A("th2", 0, 96), A("ps1", 96, 192), OP.subtract)
-            tt(A("ps1", 288, 384), A("ps1", 192, 288), A("t2"), OP.is_gt)
-            tt(A("d0b", 1, 288, 3), A("ps1", 288, 384), A("sg", 0, 96), OP.not_equal)
-            route3(t, 0, 96, "ps2")
-            scan(A("sob"), A("d0b"), A("d1b"))
-            cp(A("ypo"), A("sob", 2, 288, 3))
-            dma("y", "yp", T.yp[:], A("ypo"))
+            for o in range(N):
+                for c0, c1 in ((0, 10), (10, m)):
+                    tt(A("Pb", 16 * (m * o + c0), 16 * (m * o + c1)), IND(A("KS"), B("pS", 4 * t + o, S(c0, c1))), B("xsP", o, S(16 * c0, 16 * c1)), OP.mult)
+            toW(A("ps6", 0, 4 * m), "Z", "Pb", 0, 64 * m)
+            ts(A("SB", 96 * t, 96 * t + 4 * m), A("ps6", 0, 4 * m), 32768.0, OP.add)
+            cuts = [0, ne // 4, ne // 2, ne]
+            send("b%d" % t, [([c], eng[cuts[c]:cuts[c + 1]], A("SB", 96 * t + m * own[c], 96 * t + m * own[c] + m),
+                              [A("LB", 72 * t + m * c, 72 * t + m * c + m)]) for c in range(3)], [A("LB", 72 * t, 72 * t + 3 * m)], ne)
+        sums("fU", 0, A("LU", 72 * t, 72 * t + 3 * nu), A("u0", 0, nu), A("u1", 0, nu), A("u2", 0, nu), A("ud", 0, nu), nu, OP.subtract)
+        band(A("uw", 0, nu), A("ud", 0, nu))
+        tt(A("w0", 1, 16, 2), A("uw", 0, 8), A("c18", 8 * t, nb), OP.is_lt)
+        scan(A("wg"), A("w0"), o1)
+        cp(A("offV"), A("wg", 1, 16, 2))
+        cp(IND(A("ov"), A("offV")), tags)
+        if last:
+            toW(A("ps2", 128, 224), "Z1", "ov", 0, V)
+            swaps("d0b", "d1b", 0, A("ps2", 128, 224), cc)
+        else:
+            past = [("ov", 128 * u + 32 * r, 128 * u + 32 * r + 32) for u in range(t)]
+            sw = quad("sqW", "ps5", "Q1", [("ov", 512 + 256 * r, 768 + 256 * r)] + past + ([("ov", 512 - 16 * nf, 512)] if nf else []))
+            swaps("d0b", "d1b", 0, sw(0, jl), cc)
+        if nf:
+            swaps("d0u", "d1u", 0, sw(jl, jl + nf), cc)
+            ts(A("d0u", 1, 3 * nf, 3), A("uw", 8, nu), 262144.0, OP.is_gt)
+            scan(A("sou", 0, 3 * nf), A("d0u", 0, 3 * nf), A("d1u", 0, 3 * nf))
+            lists(t + 1, "sou", 2, 3)
+            cp(pF(32 - nf, 32, t + 1), A("sou", 2, 3 * nf, 3), "s")
+        for b0, b1 in ((0, 32), (32, 64), (64, 96)) if last else ((0, n),):
+            cp(A("DB", 16 * b0, 16 * b1), IND(DSw, A("L1U", b0, b1)), "s")
+        pt = "ps0" if last else "ps7"
+        toW(A(pt, 0, n), "Z2", "DB", 0, 16 * n)
+        cp(A("tb", 0, n), A(pt, 0, n), "s")
+        j0, j1 = 3 * jl + 2, 3 * (jl + l1 - l0)
+        m3 = A("w0", 2 * l0 + 1, 2 * l1, 2)
+        act(A("d0b", j0, j1, 3), m3, bias=1.0, scale=-1.0)
+        tt(A("vam", l0, l1), A("upF", l0, l1), m3, OP.mult)
+        act(A("d1b", j0, j1, 3), A("vam", l0, l1), bias=cc)
+        for h, (b0, b1) in enumerate(halves if last else ((0, n),)):
+            mine = A("ps%d" % (6 + h), 0, b1 - b0) if last else A("ps6", m * r, m * r + m)
+            tt(A("b0", b0, b1), A("tb", b0, b1), mine, OP.subtract)
+            land = A("LF", 3 * b0, 3 * b1) if last else A("LB", 72 * t, 72 * t + 3 * m)
+            sums("fB", 3 * b0, land, A("b0", b0, b1), A("b1", b0, b1), A("b2", b0, b1), A("bd", b0, b1), b1 - b0, OP.subtract)
+            band(A("bw", b0, b1), A("bd", b0, b1))
+            ts(A("d0b", 3 * b0 + 1, 3 * b1, 3), A("bw", b0, b1), 262144.0, OP.is_gt)
+            scan(A("sob", 3 * b0, 3 * b1), A("d0b", 3 * b0, 3 * b1), A("d1b", 3 * b0, 3 * b1))
+            if last:
+                cp(A("ypo", b0, b1), A("sob", 3 * b0 + 2, 3 * b1, 3))
+                dma("ys"[h], "y%d" % h, T.yp[:, b0:b1], A("ypo", b0, b1), 24576)
+        if not last:
+            mine, slots = pS(r, m, t + 1), S(4 * t + 4, 4 * t + 8)
+            cp(mine, A("sob", 2, 3 * m, 3))
+            send_all("p%d" % t, mine, [mine] * 3, [pS(o, m, t + 1) for o in others])
+            cp(pF(32, 96, t + 1), B("pS", slots, S(0, 16)))
+            for u in range(t + 1):
+                cp(pF(8 * u, 8 * u + 8, t + 1), B("pS", slots, S(16 + 2 * u, 18 + 2 * u)))
+            if t == R - 2:
+                cp(A("pN"), pF(0, 96, t + 1))
+            else:
+                cp(B("pS", slots, S(m, m + 2)), A("sos", 2, 24, 3), also=[pS(o, m, t + 1) for o in others])
+    toW(A("ps5", 0, 36), "Z3", "DS", 0, 4 * LX)
+    act(A("yc1"), A("ps5", 0, 36), bias=1.0)
+    tt(B("ycq"), A("yc1"), A("cond"), OP.mult)
+    act(A("yco"), B("ycq", ALL, S(1, 9)), bias=-1.0)
+    dma("y", "yc", T.yc[:], A("yco"), 16384)
 
-    wanted = set(w for o in ops for w in o[2] if w[0] in CS)
+    start = planned(ops)
+    order = sorted(range(len(ops)), key=lambda i: (start[i], i))
+
+    know, snap, cnt, plan = dict((e, {}) for e in Q), {}, dict((e, 0) for e in Q), []
+    for pos, i in enumerate(order):
+        e, fns, deps, _, ev = ops[i]
+        if e == "l":
+            snap[i] = (ev, {ev[0]: ev[1]}, pos)
+        if e not in Q:
+            continue
+        waits = []
+        for m in sorted([m for m in deps if m in snap and not (ops[m][0] == e == "t")], key=lambda m: -snap[m][2]):
+            k, v = snap[m][0]
+            if know[e].get(k, -1) < v:
+                waits.append((k, v))
+                for k2, v2 in snap[m][1].items():
+                    know[e][k2] = max(know[e].get(k2, -1), v2)
+        if ev is None:
+            ev = (e, cnt[e])
+            cnt[e] += 1
+            snap[i] = (ev, dict(know[e], **{e: ev[1]}), pos)
+        plan.append((e, fns, waits, ev))
+    wanted = set(w for o in plan for w in o[2] if w[0] in CS)
     num, tot = {}, dict((e, 0) for e in CS)
-    for e, fn, waits, ev in ops:
+    for e, fns, waits, ev in plan:
         if ev in wanted:
             tot[e] += 1
             num[ev] = tot[e]
-    for e, fn, waits, ev in ops:
+    for e, fns, waits, ev in plan:
         for w in waits:
-            if w[0] in CS:
-                Q[e].wait_ge(T.sem[CS[w[0]]], num[w])
-            else:
-                Q[e].wait_ge(T.sem[w[0]], w[1])
-        ins = fn()
+            Q[e].wait_ge(T.sem[CS[w[0]]] if w[0] in CS else T.sem[w[0]], num[w] if w[0] in CS else w[1])
+        for fn in fns:
+            ins = fn()
         if ev in wanted:
             ins.then_inc(T.sem[CS[e]], 1)
-        elif ev is not None and ev[0] not in CS:
+        elif ev != "send" and ev[0] not in CS:
             ins.then_inc(T.sem[ev[0]], 16)
     g.wait_ge(T.sem.ls, nloc[0])
-    g.sync.wait_ge(T.sem.dyp, 16)
-    g.scalar.wait_ge(T.sem.dyc, 16)
+    g.sync.wait_ge(T.sem.dy0, 16)
+    g.scalar.wait_ge(T.sem.dy1, 16)
+    g.sync.wait_ge(T.sem.dyc, 16)

@@ -1,6 +1,6 @@
 import numpy as np
 from concourse.bass import DstId, RemoteDMATransfer
-from concourse.mybir import AluOpType, AxisListType, ActivationFunctionType
+from concourse.mybir import AluOpType, ActivationFunctionType
 
 V, C, L, R = 1536, 8192, 128, 4
 BF, F32, F16, I32, U16 = "bfloat16", "float32", "float16", "int32", "uint16"
@@ -13,53 +13,52 @@ WID = {
     "Y": (128, BF), "Q": (512, BF), "Q1": (512, BF), "Q2": (512, BF), "hq": (128, F32), "hq2": (128, F32), "MQ": (128, F32), "TG": (4 * L, BF),
     "fst": (16, F32), "w0": (16, F32), "wg": (16, F32), "c18": (32, F32), "hic": (32, F32), "Perm": (128, F32),
     "laneW": (32, F32), "lane16": (8, F32),
-    "XM": (4 * 2048, BF), "Kg": (2048, BF), "Dg": (512, BF), "xsg": (128, BF), "cU": (128, U16),
-    "sU": (32, U16), "pS": ((16, 24), U16), "pN": (96, U16), "pF": (4 * 96, F32), "sqP": (32, F32), "sqW": (128, F32),
+    "XM": (2048, BF), "xo": (8, U16), "Kg": (2048, BF), "Dg": (512, BF), "xsg": (128, BF), "cU": (128, U16),
+    "sU": (32, U16), "pS": ((16, 24), U16), "pG": ((4, 24), F32), "pN": (96, U16), "pF": (4 * 96, F32), "sqP": (32, F32), "sqW": (128, F32),
     "TR": ((12, 32), F32), "TO": ((8, 32), F32), "SA": (4 * 192, U16), "LA": (4 * 192, U16), "r1": (64, F32), "rest": (64, F32),
     "side": ((4, 19), F32), "cutp": ((2, 19), F32), "d1c": (36, F32), "d1e": (36, F32), "ne": (36, F32), "negc": ((2, 18), F32),
     "key": (36, F32), "pm": (36, F32), "M18": (36, F32), "nfl": (36, F32), "yq": (72, F32),
     "DL": ((16, 8), U16), "cx": (16, U16), "Kc": (LX, BF), "DS": (4 * LX, BF), "sgR": (128, BF),
     "WL": (96, U16), "XL": (48, U16), "RB": (512, BF), "sqL": (128, F32), "LL": (32, U16), "Lf": (32, F32), "Xsm": (256, BF),
-    "Psm": (256, F16), "sqO": (64, F32), "sqT": (64, F32), "SS": (48, U16), "LS": (3 * 48, U16), "fS": (48, F32),
-    "DJ": (512, BF), "tm": (16, F32), "uu": (16, F32), "th2": (16, F32),
-    "t1": (16, F32), "t2": (16, F32), "sd": ((8, 3), F32), "sg3": ((8, 3), F32), "d0s": (24, F32), "d1s": (24, F32), "sos": (24, F32),
+    "Psm": (256, F16), "sqO": (64, F32), "sqT": (64, F32), "SS": (48, U16), "LS": (3 * 48, U16), "DJ": (512, BF),
+    "e0s": (112, F32), "e1s": (112, F32), "es": (112, F32), "e0u": (168, F32), "e1u": (168, F32), "eu": (168, F32),
+    "e0b": (672, F32), "e1b": (672, F32), "eb": (672, F32), "d0s": (24, F32), "d1s": (24, F32), "sos": (24, F32),
     "sbU": (8, U16), "mk": (128, BF), "RU": (128, F16), "upU": (8, U16), "upF": (8, F32), "X3": (128, BF), "Pu": (384, F16),
-    "sqU": (96, F32), "sqV": (96, F32), "SU": (96, U16), "LU": (4 * 72, U16), "fU": (72, F32),
-    "u0": (24, F32), "u1": (24, F32), "u2": (24, F32), "ud": (24, F32), "uw": (24, F32), "d0u": (48, F32), "d1u": (48, F32), "sou": (48, F32),
+    "sqU": (96, F32), "sqV": (96, F32), "SU": (96, U16), "LU": (4 * 72, U16), "d0u": (48, F32), "d1u": (48, F32), "sou": (48, F32),
     "KS": (VX, BF), "who": (VX, BF), "ov": (VX, BF), "Pb": (V, F16), "L1R": (V, BF), "DB": (V, BF), "L1U": (96, U16), "L1F": (8, F32),
-    "tb": (96, F32), "b0": (96, F32), "b1": (96, F32), "b2": (96, F32), "bd": (96, F32), "bw": (96, F32),
-    "d0b": (288, F32), "d1b": (288, F32), "sob": (288, F32), "SB": (4 * 96, U16), "LB": (3 * 72, U16), "LF": (288, U16), "fB": (288, F32),
+    "d0b": (288, F32), "d1b": (288, F32), "sob": (288, F32), "SB": (4 * 96, U16), "LB": (3 * 72, U16), "LF": (288, U16),
     "keyR": (128, F32), "kb": (16, F32), "junk": (2048, BF), "acc": (16, F32), "nl": (16, F32), "ap": (8, F32), "cond": (36, F32),
-    "o0": (16, F32), "o1": (64, F32), "og": (16, F32), "cl": (32, F32), "offU": (32, U16), "val": (8, F32), "vam": (8, F32), "offV": (8, U16),
+    "o0": (16, F32), "o1": (64, F32), "og": (16, F32), "cl": (32, F32), "offU": (32, U16), "val": (8, F32), "offV": (8, U16),
     "ovt": (96, F32), "yc1": (36, F32), "ycq": ((4, 9), F32), "yco": (32, F32), "ypo": (96, F32),
 }
-SMALL, _at = {}, 0
-for _k, (_w, _d) in list(WID.items()):
-    if _d == F32 and not isinstance(_w, tuple) and _w <= 128 and _k not in ("fst", "ypo", "yco"):
-        SMALL[_k] = (_at, _w)
-        _at += (_w + 7) // 8 * 8
-        del WID[_k]
-WID["small"] = (_at, F32)
+SMALL = {}
+ZERO, ONES = ["o0", "w0", "nfl", "M18", "d0s", "cond", "d0u", "e1s", "e1u", "d0b", "e1b"], ["e0s", "e0u", "e0b"]
+for _n, _l in (("zero", ZERO), ("ones", ONES),
+               ("small", [k for k, (w, d) in WID.items() if d == F32 and not isinstance(w, tuple) and w <= 128 and k not in ZERO + ONES + ["fst", "ypo", "yco"]])):
+    _at = 0
+    for _k in _l:
+        SMALL[_k] = (_at, WID[_k][0], _n)
+        _at += (WID.pop(_k)[0] + 7) // 8 * 8
+    WID[_n] = (_at, F32)
 SHAPE = dict((k, [128] + (list(w) if isinstance(w, tuple) else [w])) for k, (w, d) in WID.items())
 SCRATCH = dict((k, ("sbuf", SHAPE[k], d)) for k, (w, d) in WID.items())
 for _k in range(8):
     SCRATCH["ps%d" % _k] = ("psum", [128, 512], F32)
     SHAPE["ps%d" % _k] = [128, 512]
 DMAS = ["pa", "bt", "co", "xv", "cd", "k0", "k1", "g0", "g1", "g2", "g3", "g4", "y0", "y1", "yc"]
-SEMAPHORES = (["cv", "cs", "ct", "cg", "ls", "f0", "z0", "z1"] + ["d" + n for n in DMAS] + ["a%d%d" % (t, c) for t in range(R) for c in range(2)]
+SEMAPHORES = (["cv", "cs", "ct", "cg", "ls", "f0", "z0", "z1"] + ["d" + n for n in DMAS] + ["a%d%d" % (t, c) for t in range(R) for c in range(3)]
               + [n + "%d" % t for n in "eu" for t in range(R)] + [n + "%d" % t for n in "sbp" for t in range(R - 1)])
 OP, AF = AluOpType, ActivationFunctionType
 ALL = slice(None)
-CY, WAKE, GATHER, SCATTER = 0.00083, 0.24, 1.56, 3.8
-SAME = 0.15
-ISSUE, START, ROW, LAND, LOAD, RATE = 0.3, 0.7, 0.035, 0.05, 1.0, 500e3
-TRIES = 4000
+FIG = {"wake": 0.25, "same": 0.17, "gather": 1.45, "scatter": 3.4, "pe": 0.85, "call": 0.02, "issue": 0.2, "start": 0.7, "row": 0.032,
+       "load": 0.7, "rate": 580e3, "dma": 0.25, "first": 2.8, "tries": 7000, "seed": 0}
+CY = 0.00083
 
 
 def A(name, c0=0, c1=None, st=1, p=ALL):
     if name in SMALL:
-        at, w = SMALL[name]
-        return ("small", (p, slice(at + c0, at + (w if c1 is None else c1), st)))
+        at, w, buf = SMALL[name]
+        return (buf, (p, slice(at + c0, at + (w if c1 is None else c1), st)))
     return (name, (p, slice(c0, c1, st)))
 
 
@@ -136,11 +135,11 @@ def planned(ops):
             for m, lat in before[i]:
                 way[m] = max(way[m], dur[m] + lat + way[i])
         best = now = both([-x for x in way])
-        rng = np.random.default_rng(0)
-        for _ in range(TRIES):
-            near = np.abs(now[1] - rng.uniform(0.25, 1.0) * now[0]) < rng.uniform(1, 6)
+        rng = np.random.default_rng(FIG["seed"])
+        for _ in range(FIG["tries"]):
+            near = np.abs(now[1] - rng.uniform(0.0, 1.0) * now[0]) < rng.uniform(1, 6)
             x = both((now[1] + near * rng.normal(0, rng.choice([0.1, 0.3, 0.6, 1.0]), n)).tolist())
-            if x[0] <= now[0] + 0.05:
+            if x[0] <= now[0] + 0.04:
                 now = x
             if x[0] < best[0]:
                 best = x
@@ -155,7 +154,7 @@ def rank_program(g, core, T, topo):
     N = len(T.cores)
     Q = {"v": g.vector, "s": g.scalar, "t": g.tensor, "g": g, "y": g.sync}
     CS = {"v": "cv", "s": "cs", "t": "ct", "g": "cg"}
-    ops, acc, nloc, fifo = [], {}, [0], [[], []]
+    ops, acc, nloc, fifo, first = [], {}, [0], [[], []], []
 
     def M(a):
         if not isinstance(a, tuple):
@@ -180,7 +179,7 @@ def rank_program(g, core, T, topo):
                 for e in acc.get(a[0], []):
                     m, e2, w2, p2, c2 = e
                     if m != n and (((w or w2) and p & p2 and c & c2) or (a[0] not in WID and (e2 != eng or eng == "t"))):
-                        deps.setdefault(m, WAKE if e2 != eng else 0.0 if eng == "t" else SAME)
+                        deps.setdefault(m, FIG["wake"] if e2 != eng else 0.0 if eng == "t" else FIG["same"])
                     if not (w and m != n and p2 & ~p == 0 and c2 & ~c == 0 and (a[0] in WID or e2 == eng)):
                         keep.append(e)
                 acc[a[0]] = keep + [(n, eng, w, p, c)]
@@ -193,8 +192,8 @@ def rank_program(g, core, T, topo):
     def vdur(o, ins, per=None):
         for a in [o] + ins:
             if a[0] == "ind":
-                return 0.05 + 16 * foot(a[2])[2] * (SCATTER if a is o else GATHER) * CY
-        return max(64, foot(o)[2] * (per or (0.5 if two([o] + ins) else 1))) * CY
+                return 0.05 + 16 * foot(a[2])[2] * FIG["scatter" if a is o else "gather"] * CY
+        return max(64, foot(o)[2] * (per or (0.5 if two([o] + ins) else 1))) * CY + FIG["call"]
 
     def cp(o, i, e="v", also=()):
         if e == "s":
@@ -220,11 +219,11 @@ def rank_program(g, core, T, topo):
     def act(o, i, f=AF.Identity, bias=None, scale=None, accum=None):
         kw = dict((k, v) for k, v in (("bias", bias), ("scale", scale), ("accum_out", accum)) if v is not None)
         node("s", [lambda: g.scalar.activation(M(o), M(i), f, **dict((k, M(v)) for k, v in kw.items()))], [i, bias, scale], [o, accum],
-             0.065 + foot(o)[2] * CY * (GATHER if i[0] == "ind" else 1) + (0.02 if accum else 0))
+             0.065 + foot(o)[2] * CY * (FIG["gather"] if i[0] == "ind" else 1) + (0.02 if accum else 0))
 
     def mms(l):
         node("t", [(lambda x: lambda: g.tensor.matmul(M(x[0]), M(x[1]), M(x[2]), x[3], x[4]))(x) for x in l], [a for x in l for a in x[1:3]], [x[0] for x in l],
-             sum(max(min(64, foot(x[1])[2]), foot(x[2])[2]) * (4 if WID[x[1][0]][1] == F32 else 1) for x in l) * CY)
+             sum(max(min(64, foot(x[1])[2]), foot(x[2])[2]) * (4 if WID[x[1][0]][1] == F32 else 1) for x in l) * CY * FIG["pe"])
 
     def toW(o, z, name, c0, c1):
         for a0 in range(0, 16, 4):
@@ -239,8 +238,8 @@ def rank_program(g, core, T, topo):
         return lambda b0, b1, st=1: A(o, 4 * b0 + 3, 4 * b1, 4 * st)
 
     def dma(e, name, o, i, nbytes):
-        n = node(e, [lambda: Q[e].dma_start(M(o), M(i))], [i, o], [], 0.05, ("d" + name, 16), dict((m, 0.0) for m in fifo[0]))
-        x = node("d", [], [], [], nbytes / RATE + 8 * ROW, None, dict([(n, LOAD)] + [(m, 0.0) for m in fifo[1]]))
+        n = node(e, [lambda: Q[e].dma_start(M(o), M(i))], [i, o], [], FIG["dma"], ("d" + name, 16), dict((m, 0.0) for m in fifo[0]))
+        x = node("d", [], [], [], nbytes / FIG["rate"] + 8 * FIG["row"], None, dict([(n, FIG["load"])] + [(m, 0.0) for m in fifo[1]] + first))
         node("l", [], [], [i, o], 0.0, ("d" + name, 16), {x: 0.0})
         fifo[0], fifo[1] = ([], []) if name[0] == "y" or name == "g4" else ([n], [x])
 
@@ -260,9 +259,12 @@ def rank_program(g, core, T, topo):
         nloc[0] += sum(len(x[1]) for x in trs)
         n = node("g", [lambda: g.remote_dma_fused([RemoteDMATransfer(dst_ids=[did[c] for c in x[0]], dma_engine_mask=mask_of(x[1]), remote_sem=T.sem[sem],
                                                                      srcs=[M(x[2])], dsts=[M(d) for d in x[3]]) for x in trs], local_sem=T.sem.ls)],
-                 [x[2] for x in trs], [], ISSUE, "send")
-        x = node("d", [], [], [], ROW * max(128 * len(x[0]) // len(x[1]) for x in trs), None, {n: START})
-        node("l", [], [], lands, 0.0, (sem, count), {x: LAND})
+                 [x[2] for x in trs], [], FIG["issue"], "send")
+        x = node("d", [], [], [], FIG["row"] * max(128 * len(x[0]) // len(x[1]) for x in trs), None,
+                 dict([(n, FIG["start"] + (0.0 if first else FIG["first"]))] + first))
+        node("l", [], [], lands, 0.0, (sem, count), {x: 0.0})
+        if not first:
+            first.append((x, 0.0))
 
     def send_all(sem, src, dsts, lands):
         send(sem, [([0, 1, 2], eng, src, dsts)], lands, ne * (N - 1))
@@ -288,7 +290,12 @@ def rank_program(g, core, T, topo):
     iota(A("Y"), [[4, 8], [0, 4], [1, 4]], 0)
     iota(A("hq"), [[0, 32], [1, 4]], 0)
     iota(A("TG"), [[1, 4 * L]], 0, -256)
-    iota(A("M16x"), [[0, 96], [1, 16]], 0)
+    for h in range(3):
+        iota(A("M16x", 512 * h, 512 * h + 512), [[0, 32], [1, 16]], 0)
+    for name, step, c in (("XM", 512, 0), ("zero", 512, 0), ("ones", 476, 1)):
+        for c0 in range(0, WID[name][0], step):
+            c1 = min(c0 + step, WID[name][0])
+            iota(A(name, c0, c1), [[0, c1 - c0]], 0, c)
     ts(col("pj", 0), col("pi", 0), 15, OP.bitwise_and)
     ts(col("pj", 1), col("pi", 0), 112, OP.bitwise_and)
     ts(col("pj", 2), col("pi", 0), 3, OP.logical_shift_right, 12, OP.bitwise_and)
@@ -301,22 +308,25 @@ def rank_program(g, core, T, topo):
     for j, lim in enumerate((3.0, 6.0, 8.0)):
         ts(col("cf", 6 + j), col("cf", 0), lim, OP.is_lt)
     tt(A("cf", 9, 11), A("cf", 7, 9), A("cf", 6, 8), OP.subtract)
-    cp(col("cf", 11), col("M16", 6))
+    cp(col("cf", 11), col("M16", 6), "s")
     ts(col("cf", 12), col("cf", 2), col("cf", 3), OP.add, col("cf", 4), OP.add)
     ts(col("cf", 13), col("cf", 5), 3.0, OP.is_lt, -BIG, OP.mult)
-    ts(col("cf", 14), col("cf", 1), 0.25, OP.mult)
+    act(col("cf", 14), col("cf", 1), scale=0.25)
+    cp(col("cf", 26), col("M16", 0), "s")
+    act(col("cf", 27), col("cf", 1), scale=8.0)
     ts(col("cf", 21), col("M16", 0), -262144.0, OP.mult)
     tt(col("cf", 15), col("cf", 21), col("M16", 3), OP.subtract)
-    ts(col("cf", 16), col("cf", 13), 32768.0, OP.add)
-    ts(col("cf", 17), col("cf", 13), 1.0 / 16, OP.mult, 256.0, OP.add)
-    for t in range(R - 1):
-        ts(col("cf", 18 + t), col("cf", 13), 16.0 * (272 - 128 * t), OP.add)
+    act(col("cf", 16), col("cf", 13), bias=32768.0)
+    act(col("cf", 17), col("cf", 13), bias=256.0, scale=1.0 / 16)
+    act(col("cf", 31), col("cf", 13), bias=-262144.0)
     for t in range(R):
-        ts(col("cf", 22 + t), col("cf", 13), 1.0 / 16, OP.mult, 1.0 - 128 * t, OP.add)
-    ts(col("cf", 26), col("cf", 13), 256.0, OP.add)
+        act(col("cf", 22 + t), col("cf", 13), bias=1.0 - 128 * t, scale=1.0 / 16)
+        if t < R - 1:
+            act(col("cf", 18 + t), col("cf", 13), bias=16.0 * (272 - 128 * t))
+            act(col("cf", 28 + t), col("cf", 13), bias=257.0 - 128 * t)
     ts(A("hic"), A("lo", 0, 32), 256.0, OP.mult, col("M16", 7), OP.mult)
     for m in range(32):
-        if m % 3 == 2:
+        if m % 3 == 1:
             act(A("dig", 256 * m, 256 * m + 256), A("lo"), bias=col("hic", m), scale=col("cf", 11))
         else:
             ts(A("dig", 256 * m, 256 * m + 256), A("lo"), col("cf", 11), OP.mult, col("hic", m), OP.add)
@@ -333,14 +343,13 @@ def rank_program(g, core, T, topo):
     for t in range(R - 1):
         cp(B("xsP", ALL, S(256 + 32 * t, 288 + 32 * t)), A("xs", 128 * t, 128 * t + 128), "s")
     ts(A("Sel", 0, 8), A("Z", 15, 128, 16), col("cf", 6), OP.mult, -1.0, OP.mult)
-    cp(A("Sel", 8, 16), A("Sel", 0, 8))
+    cp(A("Sel", 8, 16), A("Sel", 0, 8), "s")
     for j in range(2):
         ts(A("Sel", 16 + 8 * j, 24 + 8 * j), A("Z", 15, 128, 16), col("cf", 9 + j), OP.mult)
+    ts(A("xo"), A("laneW", 0, 8), col("cf", 27), OP.add)
 
-    def xmask(t, ty, src):
-        for gg in range(8):
-            c0 = 2048 * t + 1024 * ty + 128 * gg
-            ts(A("XM", c0, c0 + 128), src, col("Z", 15 + 16 * gg), OP.mult)
+    def xmask(ty, src):
+        cp(IND(A("XM", 1024 * ty, 1024 * ty + 1024), A("xo")), src)
 
     def keys(sU, sF):
         tt(A("keyR"), IND(A("io256"), sU), A("lo", 0, 128), OP.add)
@@ -353,11 +362,11 @@ def rank_program(g, core, T, topo):
             for j in (b + 8, b):
                 act(A("junk", 128 * j, 128 * j + w), A("keyR", 0, w), AF.Sign, bias=col("kb", j), scale=-1.0, accum=col("acc", j))
 
-    def lists(t, src, c0, st):
-        cp(A("WL", 32 * t, 32 * t + 16, 2), A(src, c0, c0 + 8 * st, st))
-        cp(A("XL", 16 * t + 1, 16 * t + 16, 2), A(src, c0, c0 + 8 * st, st))
+    def lists(t, src, c0, st, add=0.0):
+        ts(A("WL", 32 * t, 32 * t + 16, 2), A(src, c0, c0 + 8 * st, st), add, OP.add)
+        ts(A("XL", 16 * t + 1, 16 * t + 16, 2), A(src, c0, c0 + 8 * st, st), add, OP.add)
         if t < 2:
-            cp(A("WL", 32 * t + 16, 32 * t + 32 - 8 * t), A(src, c0 + 8 * st, c0 + (24 - 8 * t) * st, st))
+            ts(A("WL", 32 * t + 16, 32 * t + 32 - 8 * t), A(src, c0 + 8 * st, c0 + (24 - 8 * t) * st, st), add, OP.add)
 
     keys(A("sU", 0, 8), A("pF", 0, 8))
     counts([2 * r, 2 * r + 1], True)
@@ -375,60 +384,61 @@ def rank_program(g, core, T, topo):
     for d, row in enumerate((0, 1, 3, 4, 5)):
         dma("y", "g%d" % d, A("dig", 0, C, 1, S(row, 128, 16)), A("dg5", 512 * d, 512 * d + 512), 131072)
     for t in range(R):
-        xmask(t, 0, A("xs", 128 * t, 128 * t + 128))
-        ms(A("ps%d" % t, 0, 256 if t == 3 else 128), 0.0)
-        ts(A("o1", 16 * t + 1, 16 * t + 16, 2), A("laneW", 0, 8), float(V), OP.add)
-    for name in ("who", "ov"):
-        act(A(name), A("io256"), bias=-512.0, scale=0.0)
-    ms(A("KS"), 0.0)
+        mms([(A("ps%d" % t, 0, 256), A("lo", 0, 128), A("lo"), True, True)])
+        act(A("o1", 16 * t + 1, 16 * t + 16, 2), A("laneW", 0, 8), bias=float(V))
+    for name, c in (("who", -512.0), ("ov", -512.0), ("KS", 0.0)):
+        for c0 in (0, VX // 2):
+            act(A(name, c0, c0 + VX // 2), A("io256", 0, VX // 2), bias=c, scale=0.0)
     act(A("DS"), A("io256", 0, 4 * LX), bias=col("cf", 15), scale=0.0)
     ms(A("Kc", 0, 16), 0.0)
-    ms(A("o0"), 0.0)
-    ms(A("w0"), 0.0)
-    ts(A("lane16"), A("laneW", 0, 8), 16.0, OP.add)
+    act(A("lane16"), A("laneW", 0, 8), bias=16.0)
     for t in range(R - 1):
         ts(A("WL", 32 * t + 1, 32 * t + 16, 2), A("laneW", 8 * t + 8, 8 * t + 16), 0.0, OP.add)
     ts(A("XL", 0, 48, 2), A("laneW", 8, 32), 0.0, OP.add)
     ts(A("Perm"), A("lo", 0, 128), col("cf", 12), OP.is_equal)
-    for z, c in (("Z1", col("M16", 0)), ("Z2", col("cf", 6)), ("Z3", col("cf", 9))):
-        ts(A(z), A("Z"), c, OP.mult)
+    for z, c in (("Z1", col("cf", 26)), ("Z2", col("cf", 6)), ("Z3", col("cf", 9))):
+        act(A(z), A("Z"), scale=c)
     for a in range(4):
         ts(A("Q", 128 * a, 128 * a + 128), A("Y"), -float(a), OP.add, col("cf", 14), OP.is_equal)
-    ts(A("Q1"), A("Q"), col("M16", 0), OP.mult)
-    ts(A("Q2"), A("Q"), col("cf", 6), OP.mult)
+    act(A("Q1"), A("Q"), scale=col("cf", 26))
+    act(A("Q2"), A("Q"), scale=col("cf", 6))
     ts(A("hq2"), A("hq"), -1.0, OP.add, col("cf", 5), OP.is_equal)
     ts(A("MQ"), A("hq"), col("cf", 5), OP.is_equal, -4.0, OP.mult)
     tt(A("hq"), A("hq2"), A("MQ"), OP.add)
-    ts(A("MQ"), A("hq"), BIG, OP.mult)
-    ts(A("M16x"), A("M16x"), col("cf", 0), OP.is_equal, 16.0, OP.mult)
-    for name in ("side", "cutp", "sd", "sg3"):
+    act(A("MQ"), A("hq"), scale=BIG)
+    for h in range(3):
+        ts(A("M16x", 512 * h, 512 * h + 512), A("M16x", 512 * h, 512 * h + 512), col("cf", 0), OP.is_equal, 16.0, OP.mult)
+    for name in ("side", "cutp"):
         ms(B(name), 0.0)
     ms(B("negc"), 1.0)
-    ms(A("nfl"), 0.0)
-    ms(A("M18"), 0.0)
     ms(A("M18", 17, 19), 4 * BIG)
     ms(B("side", S(0, 4, 2), S(17, 19)), -16.0)
     ms(B("cutp", ALL, 0), float(C))
-    ms(A("d0b"), 0.0)
-    ms(A("d0u"), 0.0)
-    ms(A("cond"), 0.0)
+    ms(A("ones", 0, None, 7), 0.0)
+    ms(A("ones", 1, None, 7), -1.0)
 
-    def sums(f, f0, land, th, x1, x2, out, n, op):
-        ts(A(f, f0, f0 + 3 * n), land, -32768.0, OP.add)
-        tt(x1, A(f, f0, f0 + n), A(f, f0 + n, f0 + 2 * n), OP.add)
-        tt(x2, th, A(f, f0 + 2 * n, f0 + 3 * n), OP.subtract)
-        tt(out, x1, x2, op)
+    def terms(x, j0, n, code, bias, part):
+        at = lambda e, k: A(e + x, 7 * j0 + k, 7 * (j0 + n), 7)
+        cp(at("e1", 0), code, "s")
+        cp(at("e1", 1), part, "s")
+        act(at("e0", 6), code, AF.Sign, bias=bias)
+        act(at("e1", 2), at("e0", 6), bias=262143.5, scale=262144.0)
 
-    def band(w, d):
-        act(w, d, AF.Abs, bias=262143.5)
+    def tally(x, j0, n, land, c0):
+        for c in range(3):
+            ts(A("e1" + x, 7 * j0 + 3 + c, 7 * (j0 + n), 7), A(land, c0 + c * n, c0 + c * n + n), -32768.0, OP.add)
+        scan(A("e" + x, 7 * j0, 7 * (j0 + n)), A("e0" + x, 7 * j0, 7 * (j0 + n)), A("e1" + x, 7 * j0, 7 * (j0 + n)))
+        return lambda b0, b1, st=1: A("e" + x, 7 * b0 + 6, 7 * b1, 7 * st)
 
-    def swaps(d0, d1, j0, ps, cc):
+    def swaps(d0, d1, j0, ps, t):
         n = foot(ps)[2]
-        if ps[0] in WID:
-            ts(A(d0, 3 * j0 + 2, 3 * (j0 + n), 3), ps, col("cf", 13), OP.add, cc - 255.5, OP.is_lt)
+        at = lambda d: A(d, 3 * j0 + 2, 3 * (j0 + n), 3)
+        if t == R - 1:
+            ts(at(d0), ps, 128.0 * t - 256.5, OP.is_lt)
+            ts(at(d1), ps, 257.0 - 128 * t, OP.add, 0.0, OP.max)
         else:
-            ts(A(d0, 3 * j0 + 2, 3 * (j0 + n), 3), ps, cc - 255.5, OP.is_lt)
-        ts(A(d1, 3 * j0 + 2, 3 * (j0 + n), 3), ps, col("cf", 26) if ps[0] in WID else 256.0, OP.add, cc, OP.max)
+            act(at(d1), ps, AF.Relu, bias=col("cf", 28 + t))
+            act(at(d0), at(d1), AF.Relu, bias=1.0, scale=-1.0)
 
     for t in range(R):
         last = t == R - 1
@@ -441,7 +451,8 @@ def rank_program(g, core, T, topo):
         tags = A("TG", L * t, L * t + L)
         cp(A("cU"), IND(A("cds"), sU))
         cp(A("xsg"), IND(A("xs"), sU), "s")
-        xmask(t, 1, A("xsg"))
+        xmask(0, A("xs", 128 * t, 128 * t + 128))
+        xmask(1, A("xsg"))
 
         def kg(c, e, l0=0, l1=32):
             o = own[c]
@@ -452,33 +463,27 @@ def rank_program(g, core, T, topo):
             return A(ps, c0 + 64 * bb + b, c0 + 64 * bb + 64, 4, S(32 * q, 32 * q + 16))
 
         def lane_mm(ps, l, stop=True):
-            return (spot(ps, 0, l % 32), A("Kg", 16 * l, 16 * l + 16), A("XM", 2048 * t + l, 2048 * t + 2048, 128), True, stop)
-
-        def out_a(c):
-            a0 = 192 * t + 64 * c
-            turn(B("TR", S(4 * c, 4 * c + 4)), A("ps%d" % c, 0, 128))
-            ts(A("SA", a0, a0 + 64), B("TR", S(4 * c, 4 * c + 4), S(0, 16)), 32768.0, OP.add)
+            return (spot(ps, 0, l % 32), A("Kg", 16 * l, 16 * l + 16), A("XM", l, 2048, 128), True, stop)
 
         piece = lambda n, c: A(n, 192 * t + 64 * c, 192 * t + 64 * c + 64)
         for c, parts in enumerate(((("s", 0, 16), ("s", 16, 32)), (("v", 0, 32),), (("s", 0, 32),))):
             for e, l0, l1 in parts:
                 kg(c, e, l0, l1)
                 mms([lane_mm("ps%d" % c, 32 * own[c] + l) for l in range(l0, l1)])
-            out_a(c)
-            if c == 1:
-                send("a%d0" % t, [([k], eng[k * ne // 2:(k + 1) * ne // 2], piece("SA", k), [piece("LA", k)]) for k in range(2)], [piece("LA", 0), piece("LA", 1)], ne)
-            if c == 2:
-                send("a%d1" % t, [([2], eng, piece("SA", 2), [piece("LA", 2)])], [piece("LA", 2)], ne)
+            turn(B("TR", S(4 * c, 4 * c + 4)), A("ps%d" % c, 0, 128))
+            ts(piece("SA", c), B("TR", S(4 * c, 4 * c + 4), S(0, 16)), 32768.0, OP.add)
+            send("a%d%d" % (t, c), [([c], eng, piece("SA", c), [piece("LA", c)])], [piece("LA", c)], ne)
         cp(A("Dg"), IND(A("dig"), A("cU", 32 * r, 32 * r + 32)), "s")
         mms([(spot("ps3", 128, l), A("Dg", 16 * l, 16 * l + 16), A("Sel", 16, 32), True, True) for l in range(32)])
-        for e, l0, l1 in (("v", 0, 16), ("s", 16, 32)):
+        for e, l0, l1 in (("s", 0, 16), ("s", 16, 32)):
             kg(3, e, l0, l1)
             mms([x for l in range(l0, l1) for x in (lane_mm("ps3", 32 * r + l, False), (spot("ps3", 0, l), A("Dg", 16 * l, 16 * l + 16), A("Sel", 0, 16), False, True))])
         turn(B("TO"), A("ps3", 0, 256))
         act(B("negc", ALL, S(1, 17)), B("TO", S(4, 8, 2), S(0, 16)), bias=-8388608.0)
         cp(B("cutp", ALL, S(1, 17)), B("TO", S(5, 8, 2), S(0, 16)), "s")
         tt(A("d1c"), B("cutp", ALL, S(0, 18)), B("cutp", ALL, S(1, 19)), OP.subtract)
-        ts(A("ps3", 256, 384), A("LA", 192 * t, 192 * t + 128), -32768.0, OP.add)
+        for c in range(2):
+            ts(A("ps3", 256 + 64 * c, 320 + 64 * c), piece("LA", c), -32768.0, OP.add)
         tt(A("r1"), B("TO", S(0, 4), S(0, 16)), A("ps3", 256, 320), OP.add)
         tt(A("rest"), A("r1"), A("ps3", 320, 384), OP.add)
         ts(A("ps3", 384, 448), piece("LA", 2), -1.0, OP.mult, 32768.0, OP.add)
@@ -509,7 +514,7 @@ def rank_program(g, core, T, topo):
         o1 = A("o1", 16 * t, 16 * t + 16)
         tt(A("o1", 16 * t, 16 * t + 16, 2), sF, A("o1", 16 * t + 1, 16 * t + 16, 2), OP.subtract)
         scan(A("og"), A("o0"), o1)
-        act(A("c18", 8 * t, nb), A("o0", 1, 16, 2), scale=262144.0)
+        act(A("c18", 8 * t, nb), A("o0", 1, 16, 2), bias=BIG, scale=-BIG)
         offU = A("offU", 8 * t, nb)
         cp(offU, A("og", 1, 16, 2))
         cp(IND(A("who"), offU), tags)
@@ -537,8 +542,9 @@ def rank_program(g, core, T, topo):
         cl = A("cl", 8 * t + l0, 8 * t + l1)
         tt(cl, A("cond", 9 * t + 1 + l0, 9 * t + 1 + l1), A("lane16", l0, l1), OP.mult)
         ps = "ps1" if last else "ps7"
-        for b0, b1 in ((0, 32), (32, 64), (64, 96)) if last else ((0, n),):
-            cp(A("L1R", 16 * b0, 16 * b1), IND(A("who"), A("pN", b0, b1) if last else pS(r, m)), "s")
+        thirds = ((0, 32, "s"), (32, 64, "s"), (64, 96, "v")) if last else ((0, n, "s"),)
+        for b0, b1, e in thirds:
+            cp(A("L1R", 16 * b0, 16 * b1), IND(A("who"), A("pN", b0, b1) if last else pS(r, m)), e)
         toW(A(ps, 256, 256 + n), "Z", "L1R", 0, 16 * n)
         ts(A("L1U", 0, n), A(ps, 256, 256 + n), 1.0 / 16, OP.mult, 272.0 - 128 * t, OP.add)
         act(A("L1F", l0, l1), A(ps, 256 + jl, 256 + jl + l1 - l0), bias=272.0 - 128 * t, scale=1.0 / 16)
@@ -548,7 +554,7 @@ def rank_program(g, core, T, topo):
         if last:
             act(A("ovt"), pF(0, 96), bias=-cc)
         else:
-            act(A("ovt", 0, jl), A("sob", 2, 3 * jl, 3) if t else pF(32 + 16 * r, 48 + 16 * r), bias=-cc)
+            act(A("ovt", 0, jl), A("sob", 2, 3 * jl, 3) if t else pF(32 + 16 * r, 48 + 16 * r), bias=-128.0 if t else -cc)
             act(A("ovt", jl, n), pF(8 * t + l0, 8 * t + l1), bias=-cc)
         tt(A("d1b", 0, 3 * n, 3), A("ovt", 0, n), A("d1b", 1, 3 * n, 3), OP.subtract)
         for o, e in zip(own, "vvss"):
@@ -566,13 +572,10 @@ def rank_program(g, core, T, topo):
         if not last:
             cp(A("DJ", 0, 256), IND(DSw, A("LL", 0, 16)), "s")
             st = quad("sqT", "ps0", "Q2", [("DJ", 0, 256)])
-            sg = B("sg3", ALL, S(1, 3))
-            ts(sg, st(0, 16), col("cf", 13), OP.add, 262144.0, OP.is_gt)
-            tt(A("uu"), st(0, 16), so(0, 16), OP.subtract)
-            act(A("tm"), sg, scale=-524288.0)
-            tt(A("th2"), A("uu"), A("tm"), OP.add)
-            sums("fS", 0, A("LS", 48 * t, 48 * t + 48), A("th2"), A("t1"), A("t2"), B("sd", ALL, S(1, 3)), 16, OP.is_gt)
-            tt(A("d0s"), B("sd"), B("sg3"), OP.not_equal)
+            terms("s", 0, 16, st(0, 16), col("cf", 31), so(0, 16))
+            es = tally("s", 0, 16, "LS", 48 * t)
+            for h in range(2):
+                ts(A("d0s", 1 + h, 24, 3), es(h, 16, 2), 0.0, OP.is_lt)
             scan(A("sos"), A("d0s"), A("d1s"))
             cp(A("sU", nb, nb + 8), A("sos", 2, 24, 3))
             cp(pF(nb, nb + 8, t + 1), A("sos", 2, 24, 3), "s")
@@ -585,7 +588,7 @@ def rank_program(g, core, T, topo):
         ts(A("SU", 24 * t, 24 * t + nu), su(0, nu), col("cf", 16), OP.add)
         send_slots("u%d" % t, A("SU", 24 * t, 24 * t + nu), "LU", 72 * t, nu)
         sv = quad("sqV", "ps5", "Q2", [("DS", LX * t + 16, LX * t + LX)] + ([("DJ", 256, 256 + 16 * nf)] if nf else []))
-        tt(A("u0", 0, nu), sv(0, nu), su(0, nu), OP.subtract)
+        terms("u", 0, nu, sv(0, nu), col("cf", 31), su(0, nu))
         cp(IND(A("KS"), offU), A("Kc", 16, LX))
         if last:
             for h, (h0, h1) in enumerate(halves):
@@ -597,60 +600,55 @@ def rank_program(g, core, T, topo):
                 send_slots("z%d" % h, sb, "LF", 3 * h0, h1 - h0)
         else:
             for o in range(N):
-                for c0, c1 in ((0, 10), (10, m)):
-                    tt(A("Pb", 16 * (m * o + c0), 16 * (m * o + c1)), IND(A("KS"), B("pS", 4 * t + o, S(c0, c1))), B("xsP", o, S(16 * c0, 16 * c1)), OP.mult)
+                tt(A("Pb", 16 * m * o, 16 * m * o + 16 * m), IND(A("KS"), pS(o, m)), B("xsP", o, S(0, 16 * m)), OP.mult)
             toW(A("ps6", 0, 4 * m), "Z", "Pb", 0, 64 * m)
             ts(A("SB", 96 * t, 96 * t + 4 * m), A("ps6", 0, 4 * m), 32768.0, OP.add)
             cuts = [0, ne // 4, ne // 2, ne]
             send("b%d" % t, [([c], eng[cuts[c]:cuts[c + 1]], A("SB", 96 * t + m * own[c], 96 * t + m * own[c] + m),
                               [A("LB", 72 * t + m * c, 72 * t + m * c + m)]) for c in range(3)], [A("LB", 72 * t, 72 * t + 3 * m)], ne)
-        sums("fU", 0, A("LU", 72 * t, 72 * t + 3 * nu), A("u0", 0, nu), A("u1", 0, nu), A("u2", 0, nu), A("ud", 0, nu), nu, OP.subtract)
-        band(A("uw", 0, nu), A("ud", 0, nu))
-        tt(A("w0", 1, 16, 2), A("uw", 0, 8), A("c18", 8 * t, nb), OP.is_lt)
+        eu = tally("u", 0, nu, "LU", 72 * t)
+        tt(A("w0", 1, 16, 2), eu(0, 8), A("c18", 8 * t, nb), OP.is_gt)
         scan(A("wg"), A("w0"), o1)
         cp(A("offV"), A("wg", 1, 16, 2))
         cp(IND(A("ov"), A("offV")), tags)
         if last:
             toW(A("ps2", 128, 224), "Z1", "ov", 0, V)
-            swaps("d0b", "d1b", 0, A("ps2", 128, 224), cc)
+            swaps("d0b", "d1b", 0, A("ps2", 128, 152), t)
+            swaps("d0b", "d1b", 32, A("ps2", 160, 224), t)
         else:
             past = [("ov", 128 * u + 32 * r, 128 * u + 32 * r + 32) for u in range(t)]
             sw = quad("sqW", "ps5", "Q1", [("ov", 512 + 256 * r, 768 + 256 * r)] + past + ([("ov", 512 - 16 * nf, 512)] if nf else []))
-            swaps("d0b", "d1b", 0, sw(0, jl), cc)
+            swaps("d0b", "d1b", 0, sw(0, jl), t)
         if nf:
-            swaps("d0u", "d1u", 0, sw(jl, jl + nf), cc)
-            ts(A("d0u", 1, 3 * nf, 3), A("uw", 8, nu), 262144.0, OP.is_gt)
+            swaps("d0u", "d1u", 0, sw(jl, jl + nf), t)
+            ts(A("d0u", 1, 3 * nf, 3), eu(8, nu), 0.0, OP.is_lt)
             scan(A("sou", 0, 3 * nf), A("d0u", 0, 3 * nf), A("d1u", 0, 3 * nf))
-            lists(t + 1, "sou", 2, 3)
-            cp(pF(32 - nf, 32, t + 1), A("sou", 2, 3 * nf, 3), "s")
-        for b0, b1 in ((0, 32), (32, 64), (64, 96)) if last else ((0, n),):
-            cp(A("DB", 16 * b0, 16 * b1), IND(DSw, A("L1U", b0, b1)), "s")
+            lists(t + 1, "sou", 2, 3, cc)
+            act(pF(32 - nf, 32, t + 1), A("sou", 2, 3 * nf, 3), bias=cc)
+        for b0, b1, e in thirds:
+            cp(A("DB", 16 * b0, 16 * b1), IND(DSw, A("L1U", b0, b1)), e)
         pt = "ps0" if last else "ps7"
         toW(A(pt, 0, n), "Z2", "DB", 0, 16 * n)
-        cp(A("tb", 0, n), A(pt, 0, n), "s")
         j0, j1 = 3 * jl + 2, 3 * (jl + l1 - l0)
         m3 = A("w0", 2 * l0 + 1, 2 * l1, 2)
         act(A("d0b", j0, j1, 3), m3, bias=1.0, scale=-1.0)
-        tt(A("vam", l0, l1), A("upF", l0, l1), m3, OP.mult)
-        act(A("d1b", j0, j1, 3), A("vam", l0, l1), bias=cc)
+        tt(A("d1b", j0, j1, 3), A("upF", l0, l1), m3, OP.mult)
         for h, (b0, b1) in enumerate(halves if last else ((0, n),)):
-            mine = A("ps%d" % (6 + h), 0, b1 - b0) if last else A("ps6", m * r, m * r + m)
-            tt(A("b0", b0, b1), A("tb", b0, b1), mine, OP.subtract)
-            land = A("LF", 3 * b0, 3 * b1) if last else A("LB", 72 * t, 72 * t + 3 * m)
-            sums("fB", 3 * b0, land, A("b0", b0, b1), A("b1", b0, b1), A("b2", b0, b1), A("bd", b0, b1), b1 - b0, OP.subtract)
-            band(A("bw", b0, b1), A("bd", b0, b1))
-            ts(A("d0b", 3 * b0 + 1, 3 * b1, 3), A("bw", b0, b1), 262144.0, OP.is_gt)
+            terms("b", b0, b1 - b0, A(pt, b0, b1), -262144.0, A("ps%d" % (6 + h), 0, b1 - b0) if last else A("ps6", m * r, m * r + m))
+            eb = tally("b", b0, b1 - b0, *(("LF", 3 * b0) if last else ("LB", 72 * t)))
+            ts(A("d0b", 3 * b0 + 1, 3 * b1, 3), eb(b0, b1), 0.0, OP.is_lt)
             scan(A("sob", 3 * b0, 3 * b1), A("d0b", 3 * b0, 3 * b1), A("d1b", 3 * b0, 3 * b1))
             if last:
-                cp(A("ypo", b0, b1), A("sob", 3 * b0 + 2, 3 * b1, 3))
+                ts(A("ypo", b0, b1), A("sob", 3 * b0 + 2, 3 * b1, 3), cc, OP.add)
                 dma("ys"[h], "y%d" % h, T.yp[:, b0:b1], A("ypo", b0, b1), 24576)
         if not last:
             mine, slots = pS(r, m, t + 1), S(4 * t + 4, 4 * t + 8)
-            cp(mine, A("sob", 2, 3 * m, 3))
+            ts(mine, A("sob", 2, 3 * m, 3), cc, OP.add)
             send_all("p%d" % t, mine, [mine] * 3, [pS(o, m, t + 1) for o in others])
-            cp(pF(32, 96, t + 1), B("pS", slots, S(0, 16)))
+            cp(B("pG", ALL, S(0, m)), B("pS", slots, S(0, m)))
+            cp(pF(32, 96, t + 1), B("pG", ALL, S(0, 16)), "s")
             for u in range(t + 1):
-                cp(pF(8 * u, 8 * u + 8, t + 1), B("pS", slots, S(16 + 2 * u, 18 + 2 * u)))
+                cp(pF(8 * u, 8 * u + 8, t + 1), B("pG", ALL, S(16 + 2 * u, 18 + 2 * u)), "s")
             if t == R - 2:
                 cp(A("pN"), pF(0, 96, t + 1))
             else:

@@ -8,10 +8,10 @@ CX, VX, LX = C + 32, V + L, L + 16
 BIG = 2.0 ** 22
 WID = {
     "kcs": (CX, BF), "dig": (CX, BF), "xs": (V, BF), "xsP": ((4, 352), BF), "cds": (V, I32), "btc": (1024, I32), "dg5": (2560, BF),
-    "pa32": (96, I32), "io256": (VX, F32), "lo": (256, BF), "pi": (8, I32), "pj": (8, I32), "cf": (32, F32),
+    "pa32": (96, I32), "io256": (V, F32), "lo": (256, BF), "pi": (8, I32), "pj": (8, I32), "cf": (32, F32),
     "Z": (144, BF), "Z1": (144, BF), "Z2": (144, BF), "Z3": (144, BF), "Sel": (32, BF), "M16": (16, BF), "M16x": (V, BF),
     "Y": (128, BF), "Q": (512, BF), "Q1": (512, BF), "Q2": (512, BF), "hq": (128, F32), "hq2": (128, F32), "MQ": (128, F32), "TG": (4 * L, BF),
-    "fst": (16, F32), "w0": (16, F32), "wg": (16, F32), "c18": (32, F32), "hic": (32, F32), "Perm": (128, F32),
+    "fst": ((16, 8), BF), "w0": (16, F32), "wg": (16, F32), "c18": (32, F32), "hic": (32, F32), "Perm": (128, F32),
     "laneW": (32, F32), "lane16": (8, F32),
     "XM": (2048, BF), "xo": (8, U16), "Kg": (2048, BF), "Dg": (512, BF), "xsg": (128, BF), "cU": (128, U16),
     "sU": (32, U16), "pS": ((16, 24), U16), "pG": ((4, 24), F32), "pN": (96, U16), "pF": (4 * 96, F32), "sqP": (32, F32), "sqW": (128, F32),
@@ -22,17 +22,17 @@ WID = {
     "WL": (96, U16), "XL": (48, U16), "RB": (512, BF), "sqL": (128, F32), "LL": (32, U16), "Lf": (32, F32), "Xsm": (256, BF),
     "Psm": (256, F16), "sqO": (64, F32), "sqT": (64, F32), "SS": (48, U16), "LS": (3 * 48, U16), "DJ": (512, BF),
     "e0s": (112, F32), "e1s": (112, F32), "es": (112, F32), "e0u": (168, F32), "e1u": (168, F32), "eu": (168, F32),
-    "e0b": (672, F32), "e1b": (672, F32), "eb": (672, F32), "d0s": (24, F32), "d1s": (24, F32), "sos": (24, F32),
+    "e0b": (672, F32), "e1b": (672, F32), "eb": (672, F32), "d0s": (40, F32), "d1s": (40, F32), "sos": (40, F32),
     "sbU": (8, U16), "mk": (128, BF), "RU": (128, F16), "upU": (8, U16), "upF": (8, F32), "X3": (128, BF), "Pu": (384, F16),
     "sqU": (96, F32), "sqV": (96, F32), "SU": (96, U16), "LU": (4 * 72, U16), "d0u": (48, F32), "d1u": (48, F32), "sou": (48, F32),
     "KS": (VX, BF), "who": (VX, BF), "ov": (VX, BF), "Pb": (V, F16), "L1R": (V, BF), "DB": (V, BF), "L1U": (96, U16), "L1F": (8, F32),
     "d0b": (288, F32), "d1b": (288, F32), "sob": (288, F32), "SB": (4 * 96, U16), "LB": (3 * 72, U16), "LF": (288, U16),
     "keyR": (128, F32), "kb": (16, F32), "junk": (2048, BF), "acc": (16, F32), "nl": (16, F32), "ap": (8, F32), "cond": (36, F32),
-    "o0": (16, F32), "o1": (64, F32), "og": (16, F32), "cl": (32, F32), "offU": (32, U16), "val": (8, F32), "offV": (8, U16),
+    "o0": (16, F32), "o1": (64, F32), "og": (16, F32), "lim": (96, F32), "offU": (32, U16), "offV": (8, U16),
     "ovt": (96, F32), "yc1": (36, F32), "ycq": ((4, 9), F32), "yco": (32, F32), "ypo": (96, F32),
 }
 SMALL = {}
-ZERO, ONES = ["o0", "w0", "nfl", "M18", "d0s", "cond", "d0u", "e1s", "e1u", "d0b", "e1b"], ["e0s", "e0u", "e0b"]
+ZERO, ONES = ["o0", "w0", "nfl", "M18", "d0s", "cond", "d0u", "e1s", "e1u", "d0b", "e1b", "lim"], ["e0s", "e0u", "e0b"]
 for _n, _l in (("zero", ZERO), ("ones", ONES),
                ("small", [k for k, (w, d) in WID.items() if d == F32 and not isinstance(w, tuple) and w <= 128 and k not in ZERO + ONES + ["fst", "ypo", "yco"]])):
     _at = 0
@@ -46,12 +46,13 @@ for _k in range(8):
     SCRATCH["ps%d" % _k] = ("psum", [128, 512], F32)
     SHAPE["ps%d" % _k] = [128, 512]
 DMAS = ["pa", "bt", "co", "xv", "cd", "k0", "k1", "g0", "g1", "g2", "g3", "g4", "y0", "y1", "yc"]
-SEMAPHORES = (["cv", "cs", "ct", "cg", "ls", "f0", "z0", "z1"] + ["d" + n for n in DMAS] + ["a%d%d" % (t, c) for t in range(R) for c in range(3)]
-              + [n + "%d" % t for n in "eu" for t in range(R)] + [n + "%d" % t for n in "sbp" for t in range(R - 1)])
+SEMAPHORES = (["cv", "cs", "ct", "cg", "ls", "z0", "z1"] + ["d" + n for n in DMAS] + ["a%d%d" % (t, c) for t in range(R) for c in range(3)]
+              + [n + "%d" % t for n in "euf" for t in range(R)] + [n + "%d" % t for n in "sbp" for t in range(R - 1)])
 OP, AF = AluOpType, ActivationFunctionType
 ALL = slice(None)
-FIG = {"wake": 0.25, "same": 0.17, "gather": 1.45, "scatter": 3.4, "pe": 0.85, "call": 0.02, "issue": 0.2, "start": 0.7, "row": 0.032,
-       "load": 0.7, "rate": 580e3, "dma": 0.25, "first": 2.8, "tries": 7000, "seed": 0}
+FIG = {"wake": 0.25, "same": 0.17, "gather": 1.45, "scatter": 3.4, "pe": 0.85, "call": 0.02, "issue": 0.2, "start": 0.7, "row": 0.029,
+       "load": 0.7, "rate": 660e3, "dma": 0.25, "first": 2.8, "tries": 8000, "seed": 0}
+LATE = {"pa": 1.0, "bt": 2.4, "co": 1.8, "xv": 1.8, "cd": 2.0}
 CY = 0.00083
 
 
@@ -127,8 +128,9 @@ def planned(ops):
 
     def both(urgency):
         end = place([-x for x in place([-x for x in place(urgency, before, up)], after, down)], before, up)
-        return max(end), np.array(end) - dur
+        return max(end) + 2.0 * sum(end[i] for i in marks) / len(marks), np.array(end) - dur, max(end)
 
+    marks = [i for i in up if que[i] == "l"]
     if not PLAN:
         way = list(dur)
         for i in down:
@@ -136,10 +138,10 @@ def planned(ops):
                 way[m] = max(way[m], dur[m] + lat + way[i])
         best = now = both([-x for x in way])
         rng = np.random.default_rng(FIG["seed"])
-        for _ in range(FIG["tries"]):
-            near = np.abs(now[1] - rng.uniform(0.0, 1.0) * now[0]) < rng.uniform(1, 6)
+        for k in range(FIG["tries"]):
+            near = np.abs(now[1] - rng.uniform(0.0, 1.0) * now[2]) < rng.uniform(1, 6)
             x = both((now[1] + near * rng.normal(0, rng.choice([0.1, 0.3, 0.6, 1.0]), n)).tolist())
-            if x[0] <= now[0] + 0.04:
+            if x[0] <= now[0] + 0.2 * (1.0 - k / FIG["tries"]) * rng.random():
                 now = x
             if x[0] < best[0]:
                 best = x
@@ -237,10 +239,14 @@ def rank_program(g, core, T, topo):
         scan(A(o, 0, at), A("MQ", 0, at), A(ps, 0, at), OP.add, OP.max)
         return lambda b0, b1, st=1: A(o, 4 * b0 + 3, 4 * b1, 4 * st)
 
+    def wide(ps, z, name, n):
+        toW(A(ps, 0, n // 16), z, name, 0, n)
+        return lambda b0, b1, st=1: A(ps, b0, b1, st)
+
     def dma(e, name, o, i, nbytes):
         n = node(e, [lambda: Q[e].dma_start(M(o), M(i))], [i, o], [], FIG["dma"], ("d" + name, 16), dict((m, 0.0) for m in fifo[0]))
         x = node("d", [], [], [], nbytes / FIG["rate"] + 8 * FIG["row"], None, dict([(n, FIG["load"])] + [(m, 0.0) for m in fifo[1]] + first))
-        node("l", [], [], [i, o], 0.0, ("d" + name, 16), {x: 0.0})
+        node("l", [], [], [i, o], 0.0, ("d" + name, 16), {x: LATE.get(name, 0.0)})
         fifo[0], fifo[1] = ([], []) if name[0] == "y" or name == "g4" else ([n], [x])
 
     def iota(o, pat, cm, base=0):
@@ -286,7 +292,9 @@ def rank_program(g, core, T, topo):
     iota(col("pi", 0), [[1, 1]], 1)
     iota(col("pi", 1), [[1, 1]], 4)
     iota(A("lo"), [[1, 256]], 0)
-    iota(A("io256"), [[256, VX]], 0)
+    iota(A("io256", 0, 512), [[256, 512]], 0)
+    ts(A("io256", 512, 1024), A("io256", 0, 512), 256.0 * 512, OP.add)
+    act(A("io256", 1024, V), A("io256", 0, 512), bias=256.0 * 1024)
     iota(A("Y"), [[4, 8], [0, 4], [1, 4]], 0)
     iota(A("hq"), [[0, 32], [1, 4]], 0)
     iota(A("TG"), [[1, 4 * L]], 0, -256)
@@ -317,13 +325,11 @@ def rank_program(g, core, T, topo):
     ts(col("cf", 21), col("M16", 0), -262144.0, OP.mult)
     tt(col("cf", 15), col("cf", 21), col("M16", 3), OP.subtract)
     act(col("cf", 16), col("cf", 13), bias=32768.0)
-    act(col("cf", 17), col("cf", 13), bias=256.0, scale=1.0 / 16)
+    act(col("cf", 17), col("cf", 13), bias=262143.5)
+    act(col("cf", 18), col("cf", 13), bias=262143.5, scale=-1.0)
     act(col("cf", 31), col("cf", 13), bias=-262144.0)
-    for t in range(R):
-        act(col("cf", 22 + t), col("cf", 13), bias=1.0 - 128 * t, scale=1.0 / 16)
-        if t < R - 1:
-            act(col("cf", 18 + t), col("cf", 13), bias=16.0 * (272 - 128 * t))
-            act(col("cf", 28 + t), col("cf", 13), bias=257.0 - 128 * t)
+    for t in range(R - 1):
+        act(col("cf", 28 + t), col("cf", 13), bias=257.0 - 128 * t)
     ts(A("hic"), A("lo", 0, 32), 256.0, OP.mult, col("M16", 7), OP.mult)
     for m in range(32):
         if m % 3 == 1:
@@ -351,16 +357,18 @@ def rank_program(g, core, T, topo):
     def xmask(ty, src):
         cp(IND(A("XM", 1024 * ty, 1024 * ty + 1024), A("xo")), src)
 
-    def keys(sU, sF):
+    def firsts(t, sU, sF):
         tt(A("keyR"), IND(A("io256"), sU), A("lo", 0, 128), OP.add)
-        act(A("kb", 8, 16), sF, bias=-0.5, scale=256.0)
-        tt(A("kb", 0, 8), A("kb", 8, 16), A("laneW", 0, 8), OP.add)
-
-    def counts(bs, whole=False):
-        for b in bs:
-            w = 128 if whole else 16 * b + 16
-            for j in (b + 8, b):
-                act(A("junk", 128 * j, 128 * j + w), A("keyR", 0, w), AF.Sign, bias=col("kb", j), scale=-1.0, accum=col("acc", j))
+        act(A("kb", 2, 4), sF, bias=-0.5, scale=256.0)
+        tt(A("kb", 0, 2), A("kb", 2, 4), A("laneW", 2 * r, 2 * r + 2), OP.add)
+        for j in range(4):
+            act(A("junk", 128 * j, 128 * j + 128), A("keyR"), AF.Sign, bias=col("kb", j), scale=-1.0, accum=col("acc", j))
+        act(A("nl", 0, 2), sF, AF.Abs, bias=-128.0 * t - 63.5)
+        act(A("nl", 2, 4), A("nl", 0, 2), AF.Relu, bias=64.0, scale=-1.0)
+        tt(A("ap", 0, 2), A("acc", 0, 2), A("nl", 2, 4), OP.add)
+        fs = lambda o: B("fst", 4 * t + o, S(0, 2))
+        tt(fs(r), A("ap", 0, 2), A("acc", 2, 4), OP.is_le)
+        send_all("f%d" % t, fs(r), [fs(r)] * 3, [fs(o) for o in others])
 
     def lists(t, src, c0, st, add=0.0):
         ts(A("WL", 32 * t, 32 * t + 16, 2), A(src, c0, c0 + 8 * st, st), add, OP.add)
@@ -368,10 +376,7 @@ def rank_program(g, core, T, topo):
         if t < 2:
             ts(A("WL", 32 * t + 16, 32 * t + 32 - 8 * t), A(src, c0 + 8 * st, c0 + (24 - 8 * t) * st, st), add, OP.add)
 
-    keys(A("sU", 0, 8), A("pF", 0, 8))
-    counts([2 * r, 2 * r + 1], True)
-    tt(A("fst", 4 * r, 4 * r + 2), A("acc", 2 * r, 2 * r + 2), A("acc", 8 + 2 * r, 10 + 2 * r), OP.is_equal)
-    send_all("f0", A("fst", 4 * r, 4 * r + 2), [A("fst", 4 * r, 4 * r + 2)] * 3, [A("fst", 4 * o, 4 * o + 2) for o in others])
+    firsts(0, A("sU", 0, 8), A("pF", 2 * r, 2 * r + 2))
     lists(0, "pF", 8, 1)
     cp(A("ps5"), A("btc", 0, 512))
     cp(A("ps6"), A("btc", 512, 1024))
@@ -391,7 +396,6 @@ def rank_program(g, core, T, topo):
             act(A(name, c0, c0 + VX // 2), A("io256", 0, VX // 2), bias=c, scale=0.0)
     act(A("DS"), A("io256", 0, 4 * LX), bias=col("cf", 15), scale=0.0)
     ms(A("Kc", 0, 16), 0.0)
-    act(A("lane16"), A("laneW", 0, 8), bias=16.0)
     for t in range(R - 1):
         ts(A("WL", 32 * t + 1, 32 * t + 16, 2), A("laneW", 8 * t + 8, 8 * t + 16), 0.0, OP.add)
     ts(A("XL", 0, 48, 2), A("laneW", 8, 32), 0.0, OP.add)
@@ -414,15 +418,17 @@ def rank_program(g, core, T, topo):
     ms(A("M18", 17, 19), 4 * BIG)
     ms(B("side", S(0, 4, 2), S(17, 19)), -16.0)
     ms(B("cutp", ALL, 0), float(C))
+    ms(A("d0s", 1, 40, 5), 1.0)
+    ms(A("d0s", 3, 40, 5), 1.0)
     ms(A("ones", 0, None, 7), 0.0)
     ms(A("ones", 1, None, 7), -1.0)
 
-    def terms(x, j0, n, code, bias, part):
+    def terms(x, j0, n, code, bias, part, fix=262143.5):
         at = lambda e, k: A(e + x, 7 * j0 + k, 7 * (j0 + n), 7)
         cp(at("e1", 0), code, "s")
         cp(at("e1", 1), part, "s")
         act(at("e0", 6), code, AF.Sign, bias=bias)
-        act(at("e1", 2), at("e0", 6), bias=262143.5, scale=262144.0)
+        act(at("e1", 2), at("e0", 6), bias=fix, scale=262144.0)
 
     def tally(x, j0, n, land, c0):
         for c in range(3):
@@ -437,8 +443,8 @@ def rank_program(g, core, T, topo):
             ts(at(d0), ps, 128.0 * t - 256.5, OP.is_lt)
             ts(at(d1), ps, 257.0 - 128 * t, OP.add, 0.0, OP.max)
         else:
-            act(at(d1), ps, AF.Relu, bias=col("cf", 28 + t))
-            act(at(d0), at(d1), AF.Relu, bias=1.0, scale=-1.0)
+            ts(at(d0), ps, col("cf", 28 + t), OP.add, 0.5, OP.is_lt)
+            ts(at(d1), ps, col("cf", 28 + t), OP.add, 0.0, OP.max)
 
     for t in range(R):
         last = t == R - 1
@@ -447,7 +453,7 @@ def rank_program(g, core, T, topo):
         nb, cc, halves = 8 * t + 8, 128.0 * t - 1, ((0, 64), (64, 96))
         nf, m = max(16 - 8 * t, 0), 18 + 2 * t
         sU = A("sU", 8 * t, nb)
-        sF = pF(0, 8) if t == 0 else A("sos", 2, 24, 3)
+        sF = pF(0, 8) if t == 0 else A("sos", 4, 40, 5)
         tags = A("TG", L * t, L * t + L)
         cp(A("cU"), IND(A("cds"), sU))
         cp(A("xsg"), IND(A("xs"), sU), "s")
@@ -473,19 +479,25 @@ def rank_program(g, core, T, topo):
             turn(B("TR", S(4 * c, 4 * c + 4)), A("ps%d" % c, 0, 128))
             ts(piece("SA", c), B("TR", S(4 * c, 4 * c + 4), S(0, 16)), 32768.0, OP.add)
             send("a%d%d" % (t, c), [([c], eng, piece("SA", c), [piece("LA", c)])], [piece("LA", c)], ne)
-        cp(A("Dg"), IND(A("dig"), A("cU", 32 * r, 32 * r + 32)), "s")
-        mms([(spot("ps3", 128, l), A("Dg", 16 * l, 16 * l + 16), A("Sel", 16, 32), True, True) for l in range(32)])
-        for e, l0, l1 in (("s", 0, 16), ("s", 16, 32)):
-            kg(3, e, l0, l1)
+        for l0, l1 in ((0, 16), (16, 32)):
+            cp(A("Dg", 16 * l0, 16 * l1), IND(A("dig"), A("cU", 32 * r + l0, 32 * r + l1)), "s")
+            mms([(spot("ps3", 128, l), A("Dg", 16 * l, 16 * l + 16), A("Sel", 16, 32), True, True) for l in range(l0, l1)])
+            kg(3, "s", l0, l1)
             mms([x for l in range(l0, l1) for x in (lane_mm("ps3", 32 * r + l, False), (spot("ps3", 0, l), A("Dg", 16 * l, 16 * l + 16), A("Sel", 0, 16), False, True))])
         turn(B("TO"), A("ps3", 0, 256))
         act(B("negc", ALL, S(1, 17)), B("TO", S(4, 8, 2), S(0, 16)), bias=-8388608.0)
         cp(B("cutp", ALL, S(1, 17)), B("TO", S(5, 8, 2), S(0, 16)), "s")
         tt(A("d1c"), B("cutp", ALL, S(0, 18)), B("cutp", ALL, S(1, 19)), OP.subtract)
-        for c in range(2):
-            ts(A("ps3", 256 + 64 * c, 320 + 64 * c), piece("LA", c), -32768.0, OP.add)
-        tt(A("r1"), B("TO", S(0, 4), S(0, 16)), A("ps3", 256, 320), OP.add)
-        tt(A("rest"), A("r1"), A("ps3", 320, 384), OP.add)
+        if t == 0:
+            ts(A("r1"), piece("LA", 0), -32768.0, OP.add)
+            ts(A("ps4", 320, 384), piece("LA", 1), -32768.0, OP.add)
+            tt(A("ps4", 256, 320), A("r1"), A("ps4", 320, 384), OP.add)
+            tt(A("rest"), B("TO", S(0, 4), S(0, 16)), A("ps4", 256, 320), OP.add)
+        else:
+            for c in range(2):
+                ts(A("ps3", 256 + 64 * c, 320 + 64 * c), piece("LA", c), -32768.0, OP.add)
+            tt(A("r1"), B("TO", S(0, 4), S(0, 16)), A("ps3", 256, 320), OP.add)
+            tt(A("rest"), A("r1"), A("ps3", 320, 384), OP.add)
         ts(A("ps3", 384, 448), piece("LA", 2), -1.0, OP.mult, 32768.0, OP.add)
         tt(B("side", ALL, S(1, 17)), A("rest"), A("ps3", 384, 448), OP.is_gt)
         tt(A("ne"), B("side", S(0, 4, 2), S(0, 18)), B("side", S(1, 4, 2), S(0, 18)), OP.not_equal)
@@ -500,56 +512,48 @@ def rank_program(g, core, T, topo):
         cp(dl(r), A("ps2", 0, 4))
         send_all("e%d" % t, dl(r), [dl(r)] * 3, [dl(o) for o in others])
         cond = A("cond", 9 * t + 1, 9 * t + 9)
-        act(A("nl", 0, 8), sF, AF.Abs, bias=-128.0 * t - 63.5)
         if t:
-            keys(sU, sF)
-            counts(range(8))
-            act(A("nl", 8, 16), A("nl", 0, 8), AF.Relu, bias=64.0, scale=-1.0)
-            tt(A("ap"), A("acc", 0, 8), A("nl", 8, 16), OP.add)
-            tt(A("o0", 1, 16, 2), A("ap"), A("acc", 8, 16), OP.is_le)
-        else:
-            ts(A("nl", 8, 16), A("nl", 0, 8), 64.0, OP.is_gt)
-            for h in range(2):
-                tt(A("o0", 1 + 2 * h, 16, 4), A("fst", h, 16, 4), A("nl", 8 + h, 16, 2), OP.mult)
+            firsts(t, sU, A("sos", 4 + 10 * r, 10 + 10 * r, 5))
+        may = B("fst", S(4 * t, 4 * t + 4), S(0, 2))
+        cp(A("o0", 1, 16, 2), may, "s")
         o1 = A("o1", 16 * t, 16 * t + 16)
         tt(A("o1", 16 * t, 16 * t + 16, 2), sF, A("o1", 16 * t + 1, 16 * t + 16, 2), OP.subtract)
         scan(A("og"), A("o0"), o1)
-        act(A("c18", 8 * t, nb), A("o0", 1, 16, 2), bias=BIG, scale=-BIG)
+        act(A("c18", 8 * t, nb), may, bias=BIG, scale=-BIG)
         offU = A("offU", 8 * t, nb)
         cp(offU, A("og", 1, 16, 2))
         cp(IND(A("who"), offU), tags)
-        cp(cond, A("o0", 1, 16, 2), "s")
+        cp(cond, may, "s")
         if not last:
             cp(A("Xsm"), IND(A("xs"), A("XL", 16 * t, 16 * t + 16)), "s")
             cp(A("RB", 0, 256 + 16 * nf), IND(A("who"), A("WL", 32 * t, 32 * t + 16 + nf)), "s")
-            sq = quad("sqL", "ps1", "Q", [("RB", 0, 256 + 16 * nf)])
-            ts(A("LL", 0, 16 + nf), sq(0, 16 + nf), col("cf", 18 + t), OP.add, 1.0 / 16, OP.mult)
-            act(A("Lf", 0, 16 + nf), sq(0, 16 + nf), bias=col("cf", 17), scale=1.0 / 16)
-            cp(A("d1s", 2, 24, 3), A("Lf", 1, 16, 2), "s")
-            tt(A("d1s", 1, 24, 3), A("Lf", 0, 16, 2), A("Lf", 1, 16, 2), OP.subtract)
-            tt(A("d1s", 0, 24, 3), pF(nb, nb + 8), A("Lf", 0, 16, 2), OP.subtract)
+            sq = wide("ps1", "Z", "RB", 256 + 16 * nf)
+            ts(A("LL", 0, 16 + nf), sq(0, 16 + nf), 16.0 * (272 - 128 * t), OP.add, 1.0 / 16, OP.mult)
+            cp(A("d1s", 0, 40, 5), pF(nb, nb + 8), "s")
+            for h in range(2):
+                act(A("d1s", 2 + 2 * h, 40, 5), sq(h, 16, 2), bias=256.0, scale=1.0 / 16)
+                act(A("d1s", 1 + 2 * h, 40, 5), A("d1s", 2 + 2 * h, 40, 5), scale=-1.0)
         if nf:
+            act(A("Lf", 16, 16 + nf), sq(16, 16 + nf), bias=256.0, scale=1.0 / 16)
             act(A("d1u", 1, 3 * nf, 3), A("Lf", 16, 16 + nf), bias=-cc)
             tt(A("d1u", 0, 3 * nf, 3), pF(32 - nf, 32), A("Lf", 16, 16 + nf), OP.subtract)
         ts(A("sbU"), sF, 1.0 / 16, OP.mult, -0.46875, OP.add)
         cp(A("mk"), IND(A("M16x"), sU), "s")
         tt(A("RU"), IND(pF(0, 96), A("sbU")), A("mk"), OP.mult)
-        sp = quad("sqP", "ps4", "Q", [("RU", 0, 128)])
-        ts(A("upU"), sp(0, 8), col("cf", 13), OP.add, 1.0 / 16, OP.mult)
+        sp = wide("ps4", "Z", "RU", 128)
+        ts(A("upU"), sp(0, 8), 1.0 / 16, OP.mult)
         cp(A("X3"), IND(A("xs"), A("upU")), "s")
         n, jl, l0, l1 = (96, 24, 0, 8) if last else (m, m - 2, 2 * r, 2 * r + 2)
-        act(A("upF", l0, l1), sp(l0, l1), bias=col("cf", 22 + t), scale=1.0 / 16)
-        cl = A("cl", 8 * t + l0, 8 * t + l1)
-        tt(cl, A("cond", 9 * t + 1 + l0, 9 * t + 1 + l1), A("lane16", l0, l1), OP.mult)
+        act(A("upF", l0, l1), sp(l0, l1), bias=-cc, scale=1.0 / 16)
+        if t:
+            act(A("lim", 14 + 2 * t, 16 + 2 * t), A("lim", 14 + 2 * t, 16 + 2 * t), scale=0.0)
+        act(A("lim", jl, jl + l1 - l0), A("cond", 9 * t + 1 + l0, 9 * t + 1 + l1), scale=BIG)
         ps = "ps1" if last else "ps7"
         thirds = ((0, 32, "s"), (32, 64, "s"), (64, 96, "v")) if last else ((0, n, "s"),)
         for b0, b1, e in thirds:
             cp(A("L1R", 16 * b0, 16 * b1), IND(A("who"), A("pN", b0, b1) if last else pS(r, m)), e)
         toW(A(ps, 256, 256 + n), "Z", "L1R", 0, 16 * n)
         ts(A("L1U", 0, n), A(ps, 256, 256 + n), 1.0 / 16, OP.mult, 272.0 - 128 * t, OP.add)
-        act(A("L1F", l0, l1), A(ps, 256 + jl, 256 + jl + l1 - l0), bias=272.0 - 128 * t, scale=1.0 / 16)
-        tt(A("val", l0, l1), A("L1F", l0, l1), cl, OP.subtract)
-        cp(A("L1U", jl, jl + l1 - l0), A("val", l0, l1))
         act(A("d1b", 1, 3 * n, 3), A(ps, 256, 256 + n), bias=256.0 - cc, scale=1.0 / 16)
         if last:
             act(A("ovt"), pF(0, 96), bias=-cc)
@@ -571,24 +575,24 @@ def rank_program(g, core, T, topo):
         DSw = A("DS", LX * t, LX * t + LX)
         if not last:
             cp(A("DJ", 0, 256), IND(DSw, A("LL", 0, 16)), "s")
-            st = quad("sqT", "ps0", "Q2", [("DJ", 0, 256)])
-            terms("s", 0, 16, st(0, 16), col("cf", 31), so(0, 16))
+            st = wide("ps0", "Z2", "DJ", 256)
+            terms("s", 0, 16, st(0, 16), -262144.0, so(0, 16), col("cf", 17))
             es = tally("s", 0, 16, "LS", 48 * t)
             for h in range(2):
-                ts(A("d0s", 1 + h, 24, 3), es(h, 16, 2), 0.0, OP.is_lt)
+                ts(A("d0s", 2 + 2 * h, 40, 5), es(h, 16, 2), 0.0, OP.is_lt)
             scan(A("sos"), A("d0s"), A("d1s"))
-            cp(A("sU", nb, nb + 8), A("sos", 2, 24, 3))
-            cp(pF(nb, nb + 8, t + 1), A("sos", 2, 24, 3), "s")
+            cp(A("sU", nb, nb + 8), A("sos", 4, 40, 5))
+            cp(pF(nb, nb + 8, t + 1), A("sos", 4, 40, 5), "s")
         nu = 8 + nf
         tt(A("Pu", 0, 128), A("Kc", 16, LX), A("X3"), OP.mult)
         if nf:
             tt(A("Pu", 128, 16 * nu), IND(A("Kc"), A("LL", 16, 16 + nf)), A("xs", 16 * (32 - nf), 512), OP.mult)
             cp(A("DJ", 256, 256 + 16 * nf), IND(DSw, A("LL", 16, 16 + nf)), "s")
-        su = quad("sqU", "ps4", "Q", [("Pu", 0, 16 * nu)])
-        ts(A("SU", 24 * t, 24 * t + nu), su(0, nu), col("cf", 16), OP.add)
+        su = wide("ps4", "Z", "Pu", 16 * nu)
+        ts(A("SU", 24 * t, 24 * t + nu), su(0, nu), 32768.0, OP.add)
         send_slots("u%d" % t, A("SU", 24 * t, 24 * t + nu), "LU", 72 * t, nu)
         sv = quad("sqV", "ps5", "Q2", [("DS", LX * t + 16, LX * t + LX)] + ([("DJ", 256, 256 + 16 * nf)] if nf else []))
-        terms("u", 0, nu, sv(0, nu), col("cf", 31), su(0, nu))
+        terms("u", 0, nu, sv(0, nu), col("cf", 31), su(0, nu), col("cf", 18))
         cp(IND(A("KS"), offU), A("Kc", 16, LX))
         if last:
             for h, (h0, h1) in enumerate(halves):
@@ -636,7 +640,7 @@ def rank_program(g, core, T, topo):
         for h, (b0, b1) in enumerate(halves if last else ((0, n),)):
             terms("b", b0, b1 - b0, A(pt, b0, b1), -262144.0, A("ps%d" % (6 + h), 0, b1 - b0) if last else A("ps6", m * r, m * r + m))
             eb = tally("b", b0, b1 - b0, *(("LF", 3 * b0) if last else ("LB", 72 * t)))
-            ts(A("d0b", 3 * b0 + 1, 3 * b1, 3), eb(b0, b1), 0.0, OP.is_lt)
+            tt(A("d0b", 3 * b0 + 1, 3 * b1, 3), eb(b0, b1), A("lim", b0, b1), OP.is_lt)
             scan(A("sob", 3 * b0, 3 * b1), A("d0b", 3 * b0, 3 * b1), A("d1b", 3 * b0, 3 * b1))
             if last:
                 ts(A("ypo", b0, b1), A("sob", 3 * b0 + 2, 3 * b1, 3), cc, OP.add)
@@ -645,14 +649,13 @@ def rank_program(g, core, T, topo):
             mine, slots = pS(r, m, t + 1), S(4 * t + 4, 4 * t + 8)
             ts(mine, A("sob", 2, 3 * m, 3), cc, OP.add)
             send_all("p%d" % t, mine, [mine] * 3, [pS(o, m, t + 1) for o in others])
-            cp(B("pG", ALL, S(0, m)), B("pS", slots, S(0, m)))
-            cp(pF(32, 96, t + 1), B("pG", ALL, S(0, 16)), "s")
+            cp(pF(32, 96, t + 1), B("pS", slots, S(0, 16)))
             for u in range(t + 1):
-                cp(pF(8 * u, 8 * u + 8, t + 1), B("pG", ALL, S(16 + 2 * u, 18 + 2 * u)), "s")
+                cp(pF(8 * u, 8 * u + 8, t + 1), B("pS", slots, S(16 + 2 * u, 18 + 2 * u)))
             if t == R - 2:
                 cp(A("pN"), pF(0, 96, t + 1))
             else:
-                cp(B("pS", slots, S(m, m + 2)), A("sos", 2, 24, 3), also=[pS(o, m, t + 1) for o in others])
+                cp(B("pS", slots, S(m, m + 2)), A("sos", 4, 40, 5), also=[pS(o, m, t + 1) for o in others])
     toW(A("ps5", 0, 36), "Z3", "DS", 0, 4 * LX)
     act(A("yc1"), A("ps5", 0, 36), bias=1.0)
     tt(B("ycq"), A("yc1"), A("cond"), OP.mult)

import numpy as np
from concourse.bass import DstId, RemoteDMATransfer
from concourse.mybir import AluOpType, ActivationFunctionType

V, C, L, R = 1536, 8192, 128, 4
BF, F32, F16, I32, U16 = "bfloat16", "float32", "float16", "int32", "uint16"
CX, VX, LX = C + 32, V + L, L + 16
BIG = 2.0 ** 22
WID = {
    "kcs": (CX, BF), "dig": (CX, BF), "xs": (V, BF), "xsP": ((4, 352), BF), "cds": (V, I32), "btc": (1024, I32), "dg5": (2560, BF),
    "pa32": (96, I32), "io256": (V, F32), "lo": (256, BF), "pi": (8, I32), "pj": (8, I32), "cf": (32, F32),
    "Z": (144, BF), "Z1": (144, BF), "Z2": (144, BF), "Z3": (144, BF), "Sel": (32, BF), "M16": (16, BF), "M16x": (V, BF),
    "Y": (128, BF), "Q": (512, BF), "Q1": (512, BF), "Q2": (512, BF), "hq": (128, F32), "hq2": (128, F32), "MQ": (128, F32), "TG": (4 * L, BF),
    "fst": ((16, 8), BF), "w0": (16, F32), "wg": (16, F32), "c18": (32, F32), "hic": (32, F32), "Perm": (128, F32),
    "laneW": (32, F32), "lane16": (8, F32),
    "XM": (2048, BF), "xo": (8, U16), "Kg": (2048, BF), "Dg": (512, BF), "xsg": (128, BF), "cU": (128, U16),
    "sU": (32, U16), "pS": ((16, 24), U16), "pG": ((4, 24), F32), "pN": (96, U16), "pF": (4 * 96, F32), "sqP": (32, F32), "sqW": (128, F32),
    "TR": ((12, 32), F32), "TO": ((8, 32), F32), "SA": (4 * 192, U16), "LA": (4 * 192, U16), "r1": (64, F32), "rest": (64, F32),
    "side": ((4, 19), F32), "cutp": ((2, 19), F32), "d1c": (36, F32), "d1e": (36, F32), "ne": (36, F32), "negc": ((2, 18), F32),
    "key": (36, F32), "pm": (36, F32), "M18": (36, F32), "nfl": (36, F32), "yq": (72, F32),
    "DL": ((16, 8), U16), "cx": (16, U16), "Kc": (LX, BF), "DS": (4 * LX, BF), "sgR": (128, BF),
    "WL": (96, U16), "XL": (48, U16), "RB": (512, BF), "sqL": (128, F32), "LL": (32, U16), "Lf": (32, F32), "Xsm": (256, BF),
    "Psm": (256, F16), "sqO": (64, F32), "sqT": (64, F32), "SS": (48, U16), "LS": (3 * 48, U16), "DJ": (512, BF),
    "e0s": (112, F32), "e1s": (112, F32), "es": (112, F32), "e0u": (168, F32), "e1u": (168, F32), "eu": (168, F32),
    "e0b": (672, F32), "e1b": (672, F32), "eb": (672, F32), "d0s": (40, F32), "d1s": (40, F32), "sos": (40, F32),
    "sbU": (8, U16), "mk": (128, BF), "RU": (128, F16), "upU": (8, U16), "upF": (8, F32), "X3": (128, BF), "Pu": (384, F16),
    "sqU": (96, F32), "sqV": (96, F32), "SU": (96, U16), "LU": (4 * 72, U16), "d0u": (48, F32), "d1u": (48, F32), "sou": (48, F32),
    "KS": (VX, BF), "who": (VX, BF), "ov": (VX, BF), "Pb": (V, F16), "L1R": (V, BF), "DB": (V, BF), "L1U": (96, U16), "L1F": (8, F32),
    "d0b": (288, F32), "d1b": (288, F32), "sob": (288, F32), "SB": (4 * 96, U16), "LB": (3 * 72, U16), "LF": (288, U16),
    "keyR": (128, F32), "kb": (16, F32), "junk": (2048, BF), "acc": (16, F32), "nl": (16, F32), "ap": (8, F32), "cond": (36, F32),
    "o0": (16, F32), "o1": (64, F32), "og": (16, F32), "lim": (96, F32), "offU": (32, U16), "offV": (8, U16),
    "ovt": (96, F32), "yc1": (36, F32), "ycq": ((4, 9), F32), "yco": (32, F32), "ypo": (96, F32),
}
SMALL = {}
ZERO, ONES = ["o0", "w0", "nfl", "M18", "d0s", "cond", "d0u", "e1s", "e1u", "d0b", "e1b", "lim"], ["e0s", "e0u", "e0b"]
for _n, _l in (("zero", ZERO), ("ones", ONES),
               ("small", [k for k, (w, d) in WID.items() if d == F32 and not isinstance(w, tuple) and w <= 128 and k not in ZERO + ONES + ["fst", "ypo", "yco"]])):
    _at = 0
    for _k in _l:
        SMALL[_k] = (_at, WID[_k][0], _n)
        _at += (WID.pop(_k)[0] + 7) // 8 * 8
    WID[_n] = (_at, F32)
SHAPE = dict((k, [128] + (list(w) if isinstance(w, tuple) else [w])) for k, (w, d) in WID.items())
SCRATCH = dict((k, ("sbuf", SHAPE[k], d)) for k, (w, d) in WID.items())
for _k in range(8):
    SCRATCH["ps%d" % _k] = ("psum", [128, 512], F32)
    SHAPE["ps%d" % _k] = [128, 512]
DMAS = ["pa", "bt", "co", "xv", "cd", "k0", "k1", "g0", "g1", "g2", "g3", "g4", "y0", "y1", "yc"]
SEMAPHORES = (["cv", "cs", "ct", "cg", "ls", "z0", "z1"] + ["d" + n for n in DMAS] + ["a%d%d" % (t, c) for t in range(R) for c in range(3)]
              + [n + "%d" % t for n in "euf" for t in range(R)] + [n + "%d" % t for n in "sbp" for t in range(R - 1)])
OP, AF = AluOpType, ActivationFunctionType
ALL = slice(None)
FIG = {"wake": 0.25, "same": 0.17, "gather": 1.45, "scatter": 3.4, "pe": 0.85, "call": 0.02, "issue": 0.2, "start": 0.7, "row": 0.029,
       "load": 0.7, "rate": 660e3, "dma": 0.25, "first": 2.8, "tries": 8000, "seed": 0}
LATE = {"pa": 1.0, "bt": 2.4, "co": 1.8, "xv": 1.8, "cd": 2.0}
CY = 0.00083


def A(name, c0=0, c1=None, st=1, p=ALL):
    if name in SMALL:
        at, w, buf = SMALL[name]
        return (buf, (p, slice(at + c0, at + (w if c1 is None else c1), st)))
    return (name, (p, slice(c0, c1, st)))


def B(name, i=ALL, j=ALL):
    return (name, (ALL, i, j))


def S(a, b=None, c=1):
    return slice(a, b, c)


def IND(win, off):
    return ("ind", win, off)


FOOT, PLAN = {}, []


def foot(a):
    k = repr(a)
    if k not in FOOT:
        sh = SHAPE[a[0]]
        cols = np.arange(int(np.prod(sh[1:]))).reshape(sh[1:])[a[1][1:]].reshape(-1)
        m = np.zeros(int(np.prod(sh[1:])), np.uint8)
        m[cols] = 1
        q = np.zeros(128, np.uint8)
        q[a[1][0]] = 1
        FOOT[k] = (int.from_bytes(np.packbits(q).tobytes(), "big"), int.from_bytes(np.packbits(m).tobytes(), "big"), len(cols))
    return FOOT[k]


def planned(ops):
    n = len(ops)
    que, dur = [o[0] for o in ops], [o[3] for o in ops]
    before, after = [list(o[2].items()) for o in ops], [[] for o in ops]
    for i in range(n):
        for m, lat in before[i]:
            after[m].append((i, lat))

    def place(urgency, links, ids):
        u = list(urgency)
        for i in ids:
            for m, _ in links[i]:
                if u[m] > u[i]:
                    u[i] = u[m]
        end, slots = [0.0] * n, dict((e, ([], [])) for e in que)
        for i in sorted(ids, key=lambda i: u[i]):
            s, d = 0.0, dur[i]
            for m, lat in links[i]:
                if end[m] + lat > s:
                    s = end[m] + lat
            if que[i] != "l":
                a, b = slots[que[i]]
                k = len(a)
                while k and b[k - 1] > s + 1e-12:
                    k -= 1
                while k < len(a) and s + d > a[k] + 1e-9:
                    s = b[k]
                    k += 1
                a.insert(k, s)
                b.insert(k, s + d)
            end[i] = s + d
        return end

    up, down = list(range(n)), list(range(n - 1, -1, -1))

    def both(urgency):
        end = place([-x for x in place([-x for x in place(urgency, before, up)], after, down)], before, up)
        return max(end) + 2.0 * sum(end[i] for i in marks) / len(marks), np.array(end) - dur, max(end)

    marks = [i for i in up if que[i] == "l"]
    if not PLAN:
        way = list(dur)
        for i in down:
            for m, lat in before[i]:
                way[m] = max(way[m], dur[m] + lat + way[i])
        best = now = both([-x for x in way])
        rng = np.random.default_rng(FIG["seed"])
        for k in range(FIG["tries"]):
            near = np.abs(now[1] - rng.uniform(0.0, 1.0) * now[2]) < rng.uniform(1, 6)
            x = both((now[1] + near * rng.normal(0, rng.choice([0.1, 0.3, 0.6, 1.0]), n)).tolist())
            if x[0] <= now[0] + 0.2 * (1.0 - k / FIG["tries"]) * rng.random():
                now = x
            if x[0] < best[0]:
                best = x
        PLAN.append(best[1].tolist())
    return [e - d for e, d in zip(place(PLAN[0], before, up), dur)]


def rank_program(g, core, T, topo):
    r = T.rank_of(core)
    if r is None:
        return
    N = len(T.cores)
    Q = {"v": g.vector, "s": g.scalar, "t": g.tensor, "g": g, "y": g.sync}
    CS = {"v": "cv", "s": "cs", "t": "ct", "g": "cg"}
    ops, acc, nloc, fifo, first = [], {}, [0], [[], []], []

    def M(a):
        if not isinstance(a, tuple):
            return a
        if a[0] == "ind":
            return M(a[1]).indirect(M(a[2]))
        return T[a[0]][a[1]]

    def flat(l):
        o = []
        for a in l:
            if isinstance(a, tuple):
                o += [a[1], a[2]] if a[0] == "ind" else [a]
        return o

    def node(eng, fns, rd, wr, dur, ev=None, after=None):
        n, deps = len(ops), dict(after or {})
        for w, l in ((False, flat(rd)), (True, flat(wr))):
            for a in l:
                p, c, _ = foot(a)
                keep = []
                for e in acc.get(a[0], []):
                    m, e2, w2, p2, c2 = e
                    if m != n and (((w or w2) and p & p2 and c & c2) or (a[0] not in WID and (e2 != eng or eng == "t"))):
                        deps.setdefault(m, FIG["wake"] if e2 != eng else 0.0 if eng == "t" else FIG["same"])
                    if not (w and m != n and p2 & ~p == 0 and c2 & ~c == 0 and (a[0] in WID or e2 == eng)):
                        keep.append(e)
                acc[a[0]] = keep + [(n, eng, w, p, c)]
        ops.append((eng, fns, deps, dur, ev))
        return n

    def two(l):
        return all(WID.get(a[0], (0, F32))[1] in (BF, F16, U16) for a in l)

    def vdur(o, ins, per=None):
        for a in [o] + ins:
            if a[0] == "ind":
                return 0.05 + 16 * foot(a[2])[2] * FIG["scatter" if a is o else "gather"] * CY
        return max(64, foot(o)[2] * (per or (0.5 if two([o] + ins) else 1))) * CY + FIG["call"]

    def cp(o, i, e="v", also=()):
        if e == "s":
            return act(o, i, AF.Copy)
        node("v", [lambda: g.vector.tensor_copy(M(o), M(i))], [i] + ([o[2]] if o[0] == "ind" else []) + list(also), [o[1] if o[0] == "ind" else o], vdur(o, [i]))

    def tt(o, a, b, f):
        node("v", [lambda: g.vector.tensor_tensor(M(o), M(a), M(b), f)], [a, b], [o], vdur(o, [a, b], 2 if a[0] in WID and b[0] in WID else 1))

    def ts(o, a, s1, f1, s2=None, f2=None):
        more = () if f2 is None else (f2,)
        node("v", [lambda: g.vector.tensor_scalar(M(o), M(a), M(s1), M(s2), f1, *more)], [a, s1, s2], [o], vdur(o, [a]))

    def ms(o, c):
        node("v", [lambda: g.vector.memset(M(o), c)], [], [o], vdur(o, []))

    def turn(o, a):
        node("v", [lambda: g.vector.transpose(M(o), M(a))], [a], [o], vdur(o, [a]))

    def scan(o, d0, d1, f0=OP.mult, f1=OP.add):
        node("v", [lambda: g.vector.tensor_tensor_scan(M(o), M(d0), M(d1), 0.0, f0, f1)], [d0, d1], [o], vdur(o, [d0, d1]))

    def act(o, i, f=AF.Identity, bias=None, scale=None, accum=None):
        kw = dict((k, v) for k, v in (("bias", bias), ("scale", scale), ("accum_out", accum)) if v is not None)
        node("s", [lambda: g.scalar.activation(M(o), M(i), f, **dict((k, M(v)) for k, v in kw.items()))], [i, bias, scale], [o, accum],
             0.065 + foot(o)[2] * CY * (FIG["gather"] if i[0] == "ind" else 1) + (0.02 if accum else 0))

    def mms(l):
        node("t", [(lambda x: lambda: g.tensor.matmul(M(x[0]), M(x[1]), M(x[2]), x[3], x[4]))(x) for x in l], [a for x in l for a in x[1:3]], [x[0] for x in l],
             sum(max(min(64, foot(x[1])[2]), foot(x[2])[2]) * (4 if WID[x[1][0]][1] == F32 else 1) for x in l) * CY * FIG["pe"])

    def toW(o, z, name, c0, c1):
        for a0 in range(0, 16, 4):
            mms([(o, A(z, 15 - a, 143 - a), A(name, c0 + a, c1, 16), a == 0, a == 15) for a in range(a0, a0 + 4)])

    def quad(o, ps, z, srcs):
        at = 0
        for name, c0, c1 in srcs:
            mms([(A(ps, at, at + (c1 - c0) // 4), A(z, 128 * a, 128 * a + 128), A(name, c0 + a, c1, 4), a == 0, a == 3) for a in range(4)])
            at += (c1 - c0) // 4
        scan(A(o, 0, at), A("MQ", 0, at), A(ps, 0, at), OP.add, OP.max)
        return lambda b0, b1, st=1: A(o, 4 * b0 + 3, 4 * b1, 4 * st)

    def wide(ps, z, name, n):
        toW(A(ps, 0, n // 16), z, name, 0, n)
        return lambda b0, b1, st=1: A(ps, b0, b1, st)

    def dma(e, name, o, i, nbytes):
        n = node(e, [lambda: Q[e].dma_start(M(o), M(i))], [i, o], [], FIG["dma"], ("d" + name, 16), dict((m, 0.0) for m in fifo[0]))
        x = node("d", [], [], [], nbytes / FIG["rate"] + 8 * FIG["row"], None, dict([(n, FIG["load"])] + [(m, 0.0) for m in fifo[1]] + first))
        node("l", [], [], [i, o], 0.0, ("d" + name, 16), {x: LATE.get(name, 0.0)})
        fifo[0], fifo[1] = ([], []) if name[0] == "y" or name == "g4" else ([n], [x])

    def iota(o, pat, cm, base=0):
        kw = {} if WID[o[0]][1] == I32 else {"allow_small_or_imprecise_dtypes": True}
        node("g", [lambda: g.iota(M(o), pat, base, cm, **kw)], [], [o], 0.13 + 2 * CY * foot(o)[2])

    peer = [T.cores[(r + 1 + c) % N] for c in range(N - 1)]
    did = [DstId(rid=topo.addr(p)[0], pnc=topo.addr(p)[1]) for p in peer]
    eng = [e for e in topo.engines(core, peer[0]) if all(e in topo.engines(core, p) for p in peer)]
    ne = len(eng)

    def mask_of(l):
        return sum(1 << e for e in l)

    def send(sem, trs, lands, count):
        nloc[0] += sum(len(x[1]) for x in trs)
        n = node("g", [lambda: g.remote_dma_fused([RemoteDMATransfer(dst_ids=[did[c] for c in x[0]], dma_engine_mask=mask_of(x[1]), remote_sem=T.sem[sem],
                                                                     srcs=[M(x[2])], dsts=[M(d) for d in x[3]]) for x in trs], local_sem=T.sem.ls)],
                 [x[2] for x in trs], [], FIG["issue"], "send")
        x = node("d", [], [], [], FIG["row"] * max(128 * len(x[0]) // len(x[1]) for x in trs), None,
                 dict([(n, FIG["start"] + (0.0 if first else FIG["first"]))] + first))
        node("l", [], [], lands, 0.0, (sem, count), {x: 0.0})
        if not first:
            first.append((x, 0.0))

    def send_all(sem, src, dsts, lands):
        send(sem, [([0, 1, 2], eng, src, dsts)], lands, ne * (N - 1))

    def send_slots(sem, src, name, c0, w):
        send_all(sem, src, [A(name, c0 + w * (2 - c), c0 + w * (3 - c)) for c in range(3)], [A(name, c0, c0 + 3 * w)])

    others = [(r + 1 + c) % N for c in range(3)]
    own = others + [r]
    col = lambda n, j: A(n, j, j + 1)

    dma("y", "pa", A("pa32"), T.pa[:], 49152)
    dma("s", "bt", A("btc", 0, 512), T.bt[:], 262144)
    dma("y", "co", A("btc", 512, 1024), T.co[:], 262144)
    dma("s", "xv", A("xs"), T.xv[:], 393216)
    dma("y", "cd", A("cds"), T.cd[:], 786432)
    dma("y", "k0", A("kcs", 0, C // 2), T.kc[:, 0:C // 2], 1048576)
    dma("s", "k1", A("kcs", C // 2, C), T.kc[:, C // 2:C], 1048576)
    iota(col("pi", 0), [[1, 1]], 1)
    iota(col("pi", 1), [[1, 1]], 4)
    iota(A("lo"), [[1, 256]], 0)
    iota(A("io256", 0, 512), [[256, 512]], 0)
    ts(A("io256", 512, 1024), A("io256", 0, 512), 256.0 * 512, OP.add)
    act(A("io256", 1024, V), A("io256", 0, 512), bias=256.0 * 1024)
    iota(A("Y"), [[4, 8], [0, 4], [1, 4]], 0)
    iota(A("hq"), [[0, 32], [1, 4]], 0)
    iota(A("TG"), [[1, 4 * L]], 0, -256)
    for h in range(3):
        iota(A("M16x", 512 * h, 512 * h + 512), [[0, 32], [1, 16]], 0)
    for name, step, c in (("XM", 512, 0), ("zero", 512, 0), ("ones", 476, 1)):
        for c0 in range(0, WID[name][0], step):
            c1 = min(c0 + step, WID[name][0])
            iota(A(name, c0, c1), [[0, c1 - c0]], 0, c)
    ts(col("pj", 0), col("pi", 0), 15, OP.bitwise_and)
    ts(col("pj", 1), col("pi", 0), 112, OP.bitwise_and)
    ts(col("pj", 2), col("pi", 0), 3, OP.logical_shift_right, 12, OP.bitwise_and)
    ts(col("pj", 3), col("pi", 1), 112, OP.bitwise_and)
    ts(col("pj", 4), col("pi", 0), 3, OP.bitwise_and)
    ts(col("pj", 5), col("pi", 0), 2, OP.logical_shift_right, 3, OP.bitwise_and)
    cp(A("cf", 0, 6), A("pj", 0, 6))
    ts(A("M16"), A("lo", 0, 16), col("cf", 0), OP.is_equal)
    ts(A("Z"), A("lo", 0, 144), -15.0, OP.add, col("cf", 1), OP.is_equal)
    for j, lim in enumerate((3.0, 6.0, 8.0)):
        ts(col("cf", 6 + j), col("cf", 0), lim, OP.is_lt)
    tt(A("cf", 9, 11), A("cf", 7, 9), A("cf", 6, 8), OP.subtract)
    cp(col("cf", 11), col("M16", 6), "s")
    ts(col("cf", 12), col("cf", 2), col("cf", 3), OP.add, col("cf", 4), OP.add)
    ts(col("cf", 13), col("cf", 5), 3.0, OP.is_lt, -BIG, OP.mult)
    act(col("cf", 14), col("cf", 1), scale=0.25)
    cp(col("cf", 26), col("M16", 0), "s")
    act(col("cf", 27), col("cf", 1), scale=8.0)
    ts(col("cf", 21), col("M16", 0), -262144.0, OP.mult)
    tt(col("cf", 15), col("cf", 21), col("M16", 3), OP.subtract)
    act(col("cf", 16), col("cf", 13), bias=32768.0)
    act(col("cf", 17), col("cf", 13), bias=262143.5)
    act(col("cf", 18), col("cf", 13), bias=262143.5, scale=-1.0)
    act(col("cf", 31), col("cf", 13), bias=-262144.0)
    for t in range(R - 1):
        act(col("cf", 28 + t), col("cf", 13), bias=257.0 - 128 * t)
    ts(A("hic"), A("lo", 0, 32), 256.0, OP.mult, col("M16", 7), OP.mult)
    for m in range(32):
        if m % 3 == 1:
            act(A("dig", 256 * m, 256 * m + 256), A("lo"), bias=col("hic", m), scale=col("cf", 11))
        else:
            ts(A("dig", 256 * m, 256 * m + 256), A("lo"), col("cf", 11), OP.mult, col("hic", m), OP.add)
    ms(A("dig", C, CX), 0.0)
    cp(col("dig", C), col("cf", 15))
    ts(col("dig", C + 17), col("M16", 2), 524288.0, OP.mult)
    ms(A("kcs", C, CX), 0.0)
    ts(A("laneW"), A("lo", 0, 32), 16.0, OP.mult, col("cf", 0), OP.add)
    cp(A("sU", 0, 8), A("pa32", 0, 8))
    cp(A("pF", 0, 96), A("pa32"))
    cp(B("pS", S(0, 4), S(0, 16)), A("pa32", 32, 96))
    cp(B("pS", S(0, 4), S(16, 18)), A("pa32", 0, 8))
    cp(B("xsP", ALL, S(0, 256)), A("xs", 512, V), "s")
    for t in range(R - 1):
        cp(B("xsP", ALL, S(256 + 32 * t, 288 + 32 * t)), A("xs", 128 * t, 128 * t + 128), "s")
    ts(A("Sel", 0, 8), A("Z", 15, 128, 16), col("cf", 6), OP.mult, -1.0, OP.mult)
    cp(A("Sel", 8, 16), A("Sel", 0, 8), "s")
    for j in range(2):
        ts(A("Sel", 16 + 8 * j, 24 + 8 * j), A("Z", 15, 128, 16), col("cf", 9 + j), OP.mult)
    ts(A("xo"), A("laneW", 0, 8), col("cf", 27), OP.add)

    def xmask(ty, src):
        cp(IND(A("XM", 1024 * ty, 1024 * ty + 1024), A("xo")), src)

    def firsts(t, sU, sF):
        tt(A("keyR"), IND(A("io256"), sU), A("lo", 0, 128), OP.add)
        act(A("kb", 2, 4), sF, bias=-0.5, scale=256.0)
        tt(A("kb", 0, 2), A("kb", 2, 4), A("laneW", 2 * r, 2 * r + 2), OP.add)
        for j in range(4):
            act(A("junk", 128 * j, 128 * j + 128), A("keyR"), AF.Sign, bias=col("kb", j), scale=-1.0, accum=col("acc", j))
        act(A("nl", 0, 2), sF, AF.Abs, bias=-128.0 * t - 63.5)
        act(A("nl", 2, 4), A("nl", 0, 2), AF.Relu, bias=64.0, scale=-1.0)
        tt(A("ap", 0, 2), A("acc", 0, 2), A("nl", 2, 4), OP.add)
        fs = lambda o: B("fst", 4 * t + o, S(0, 2))
        tt(fs(r), A("ap", 0, 2), A("acc", 2, 4), OP.is_le)
        send_all("f%d" % t, fs(r), [fs(r)] * 3, [fs(o) for o in others])

    def lists(t, src, c0, st, add=0.0):
        ts(A("WL", 32 * t, 32 * t + 16, 2), A(src, c0, c0 + 8 * st, st), add, OP.add)
        ts(A("XL", 16 * t + 1, 16 * t + 16, 2), A(src, c0, c0 + 8 * st, st), add, OP.add)
        if t < 2:
            ts(A("WL", 32 * t + 16, 32 * t + 32 - 8 * t), A(src, c0 + 8 * st, c0 + (24 - 8 * t) * st, st), add, OP.add)

    firsts(0, A("sU", 0, 8), A("pF", 2 * r, 2 * r + 2))
    lists(0, "pF", 8, 1)
    cp(A("ps5"), A("btc", 0, 512))
    cp(A("ps6"), A("btc", 512, 1024))
    cp(A("dg5", 0, 512), A("ps5"), "s")
    cp(A("dg5", 1024, 1536), A("ps6"), "s")
    tt(A("dg5", 512, 1024), A("ps5"), A("dg5", 0, 512), OP.subtract)
    tt(A("ps7"), A("ps6"), A("dg5", 1024, 1536), OP.subtract)
    cp(A("dg5", 1536, 2048), A("ps7"), "s")
    tt(A("dg5", 2048, 2560), A("ps7"), A("dg5", 1536, 2048), OP.subtract)
    for d, row in enumerate((0, 1, 3, 4, 5)):
        dma("y", "g%d" % d, A("dig", 0, C, 1, S(row, 128, 16)), A("dg5", 512 * d, 512 * d + 512), 131072)
    for t in range(R):
        mms([(A("ps%d" % t, 0, 256), A("lo", 0, 128), A("lo"), True, True)])
        act(A("o1", 16 * t + 1, 16 * t + 16, 2), A("laneW", 0, 8), bias=float(V))
    for name, c in (("who", -512.0), ("ov", -512.0), ("KS", 0.0)):
        for c0 in (0, VX // 2):
            act(A(name, c0, c0 + VX // 2), A("io256", 0, VX // 2), bias=c, scale=0.0)
    act(A("DS"), A("io256", 0, 4 * LX), bias=col("cf", 15), scale=0.0)
    ms(A("Kc", 0, 16), 0.0)
    for t in range(R - 1):
        ts(A("WL", 32 * t + 1, 32 * t + 16, 2), A("laneW", 8 * t + 8, 8 * t + 16), 0.0, OP.add)
    ts(A("XL", 0, 48, 2), A("laneW", 8, 32), 0.0, OP.add)
    ts(A("Perm"), A("lo", 0, 128), col("cf", 12), OP.is_equal)
    for z, c in (("Z1", col("cf", 26)), ("Z2", col("cf", 6)), ("Z3", col("cf", 9))):
        act(A(z), A("Z"), scale=c)
    for a in range(4):
        ts(A("Q", 128 * a, 128 * a + 128), A("Y"), -float(a), OP.add, col("cf", 14), OP.is_equal)
    act(A("Q1"), A("Q"), scale=col("cf", 26))
    act(A("Q2"), A("Q"), scale=col("cf", 6))
    ts(A("hq2"), A("hq"), -1.0, OP.add, col("cf", 5), OP.is_equal)
    ts(A("MQ"), A("hq"), col("cf", 5), OP.is_equal, -4.0, OP.mult)
    tt(A("hq"), A("hq2"), A("MQ"), OP.add)
    act(A("MQ"), A("hq"), scale=BIG)
    for h in range(3):
        ts(A("M16x", 512 * h, 512 * h + 512), A("M16x", 512 * h, 512 * h + 512), col("cf", 0), OP.is_equal, 16.0, OP.mult)
    for name in ("side", "cutp"):
        ms(B(name), 0.0)
    ms(B("negc"), 1.0)
    ms(A("M18", 17, 19), 4 * BIG)
    ms(B("side", S(0, 4, 2), S(17, 19)), -16.0)
    ms(B("cutp", ALL, 0), float(C))
    ms(A("d0s", 1, 40, 5), 1.0)
    ms(A("d0s", 3, 40, 5), 1.0)
    ms(A("ones", 0, None, 7), 0.0)
    ms(A("ones", 1, None, 7), -1.0)

    def terms(x, j0, n, code, bias, part, fix=262143.5):
        at = lambda e, k: A(e + x, 7 * j0 + k, 7 * (j0 + n), 7)
        cp(at("e1", 0), code, "s")
        cp(at("e1", 1), part, "s")
        act(at("e0", 6), code, AF.Sign, bias=bias)
        act(at("e1", 2), at("e0", 6), bias=fix, scale=262144.0)

    def tally(x, j0, n, land, c0):
        for c in range(3):
            ts(A("e1" + x, 7 * j0 + 3 + c, 7 * (j0 + n), 7), A(land, c0 + c * n, c0 + c * n + n), -32768.0, OP.add)
        scan(A("e" + x, 7 * j0, 7 * (j0 + n)), A("e0" + x, 7 * j0, 7 * (j0 + n)), A("e1" + x, 7 * j0, 7 * (j0 + n)))
        return lambda b0, b1, st=1: A("e" + x, 7 * b0 + 6, 7 * b1, 7 * st)

    def swaps(d0, d1, j0, ps, t):
        n = foot(ps)[2]
        at = lambda d: A(d, 3 * j0 + 2, 3 * (j0 + n), 3)
        if t == R - 1:
            ts(at(d0), ps, 128.0 * t - 256.5, OP.is_lt)
            ts(at(d1), ps, 257.0 - 128 * t, OP.add, 0.0, OP.max)
        else:
            ts(at(d0), ps, col("cf", 28 + t), OP.add, 0.5, OP.is_lt)
            ts(at(d1), ps, col("cf", 28 + t), OP.add, 0.0, OP.max)

    for t in range(R):
        last = t == R - 1
        pS = lambda o, n, u=t: B("pS", 4 * u + o, S(0, n))
        pF = lambda b0, b1, u=t: A("pF", 96 * u + b0, 96 * u + b1)
        nb, cc, halves = 8 * t + 8, 128.0 * t - 1, ((0, 64), (64, 96))
        nf, m = max(16 - 8 * t, 0), 18 + 2 * t
        sU = A("sU", 8 * t, nb)
        sF = pF(0, 8) if t == 0 else A("sos", 4, 40, 5)
        tags = A("TG", L * t, L * t + L)
        cp(A("cU"), IND(A("cds"), sU))
        cp(A("xsg"), IND(A("xs"), sU), "s")
        xmask(0, A("xs", 128 * t, 128 * t + 128))
        xmask(1, A("xsg"))

        def kg(c, e, l0=0, l1=32):
            o = own[c]
            cp(A("Kg", 512 * o + 16 * l0, 512 * o + 16 * l1), IND(A("kcs"), A("cU", 32 * o + l0, 32 * o + l1)), e)

        def spot(ps, c0, l):
            bb, q, b = l // 16, l % 16 // 4, l % 4
            return A(ps, c0 + 64 * bb + b, c0 + 64 * bb + 64, 4, S(32 * q, 32 * q + 16))

        def lane_mm(ps, l, stop=True):
            return (spot(ps, 0, l % 32), A("Kg", 16 * l, 16 * l + 16), A("XM", l, 2048, 128), True, stop)

        piece = lambda n, c: A(n, 192 * t + 64 * c, 192 * t + 64 * c + 64)
        for c, parts in enumerate(((("s", 0, 16), ("s", 16, 32)), (("v", 0, 32),), (("s", 0, 32),))):
            for e, l0, l1 in parts:
                kg(c, e, l0, l1)
                mms([lane_mm("ps%d" % c, 32 * own[c] + l) for l in range(l0, l1)])
            turn(B("TR", S(4 * c, 4 * c + 4)), A("ps%d" % c, 0, 128))
            ts(piece("SA", c), B("TR", S(4 * c, 4 * c + 4), S(0, 16)), 32768.0, OP.add)
            send("a%d%d" % (t, c), [([c], eng, piece("SA", c), [piece("LA", c)])], [piece("LA", c)], ne)
        for l0, l1 in ((0, 16), (16, 32)):
            cp(A("Dg", 16 * l0, 16 * l1), IND(A("dig"), A("cU", 32 * r + l0, 32 * r + l1)), "s")
            mms([(spot("ps3", 128, l), A("Dg", 16 * l, 16 * l + 16), A("Sel", 16, 32), True, True) for l in range(l0, l1)])
            kg(3, "s", l0, l1)
            mms([x for l in range(l0, l1) for x in (lane_mm("ps3", 32 * r + l, False), (spot("ps3", 0, l), A("Dg", 16 * l, 16 * l + 16), A("Sel", 0, 16), False, True))])
        turn(B("TO"), A("ps3", 0, 256))
        act(B("negc", ALL, S(1, 17)), B("TO", S(4, 8, 2), S(0, 16)), bias=-8388608.0)
        cp(B("cutp", ALL, S(1, 17)), B("TO", S(5, 8, 2), S(0, 16)), "s")
        tt(A("d1c"), B("cutp", ALL, S(0, 18)), B("cutp", ALL, S(1, 19)), OP.subtract)
        if t == 0:
            ts(A("r1"), piece("LA", 0), -32768.0, OP.add)
            ts(A("ps4", 320, 384), piece("LA", 1), -32768.0, OP.add)
            tt(A("ps4", 256, 320), A("r1"), A("ps4", 320, 384), OP.add)
            tt(A("rest"), B("TO", S(0, 4), S(0, 16)), A("ps4", 256, 320), OP.add)
        else:
            for c in range(2):
                ts(A("ps3", 256 + 64 * c, 320 + 64 * c), piece("LA", c), -32768.0, OP.add)
            tt(A("r1"), B("TO", S(0, 4), S(0, 16)), A("ps3", 256, 320), OP.add)
            tt(A("rest"), A("r1"), A("ps3", 320, 384), OP.add)
        ts(A("ps3", 384, 448), piece("LA", 2), -1.0, OP.mult, 32768.0, OP.add)
        tt(B("side", ALL, S(1, 17)), A("rest"), A("ps3", 384, 448), OP.is_gt)
        tt(A("ne"), B("side", S(0, 4, 2), S(0, 18)), B("side", S(1, 4, 2), S(0, 18)), OP.not_equal)
        tt(A("d1e"), B("side", S(0, 4, 2), S(0, 18)), B("side", S(0, 4, 2), S(1, 19)), OP.subtract)
        tt(A("key"), A("ne"), B("negc"), OP.mult)
        scan(A("pm"), A("M18"), A("key"), OP.add, OP.min)
        tt(A("nfl", 1, 36), A("key", 1, 36), A("pm", 0, 35), OP.is_ge)
        scan(A("yq", 0, 36), A("nfl"), A("d1c"))
        scan(A("yq", 36, 72), A("nfl"), A("d1e"))
        mms([(A("ps2", 0, 4), A("Perm"), A("yq", 17, 72, 18), True, True)])
        dl = lambda o, n=4: B("DL", 4 * t + o, S(0, n))
        cp(dl(r), A("ps2", 0, 4))
        send_all("e%d" % t, dl(r), [dl(r)] * 3, [dl(o) for o in others])
        cond = A("cond", 9 * t + 1, 9 * t + 9)
        if t:
            firsts(t, sU, A("sos", 4 + 10 * r, 10 + 10 * r, 5))
        may = B("fst", S(4 * t, 4 * t + 4), S(0, 2))
        cp(A("o0", 1, 16, 2), may, "s")
        o1 = A("o1", 16 * t, 16 * t + 16)
        tt(A("o1", 16 * t, 16 * t + 16, 2), sF, A("o1", 16 * t + 1, 16 * t + 16, 2), OP.subtract)
        scan(A("og"), A("o0"), o1)
        act(A("c18", 8 * t, nb), may, bias=BIG, scale=-BIG)
        offU = A("offU", 8 * t, nb)
        cp(offU, A("og", 1, 16, 2))
        cp(IND(A("who"), offU), tags)
        cp(cond, may, "s")
        if not last:
            cp(A("Xsm"), IND(A("xs"), A("XL", 16 * t, 16 * t + 16)), "s")
            cp(A("RB", 0, 256 + 16 * nf), IND(A("who"), A("WL", 32 * t, 32 * t + 16 + nf)), "s")
            sq = wide("ps1", "Z", "RB", 256 + 16 * nf)
            ts(A("LL", 0, 16 + nf), sq(0, 16 + nf), 16.0 * (272 - 128 * t), OP.add, 1.0 / 16, OP.mult)
            cp(A("d1s", 0, 40, 5), pF(nb, nb + 8), "s")
            for h in range(2):
                act(A("d1s", 2 + 2 * h, 40, 5), sq(h, 16, 2), bias=256.0, scale=1.0 / 16)
                act(A("d1s", 1 + 2 * h, 40, 5), A("d1s", 2 + 2 * h, 40, 5), scale=-1.0)
        if nf:
            act(A("Lf", 16, 16 + nf), sq(16, 16 + nf), bias=256.0, scale=1.0 / 16)
            act(A("d1u", 1, 3 * nf, 3), A("Lf", 16, 16 + nf), bias=-cc)
            tt(A("d1u", 0, 3 * nf, 3), pF(32 - nf, 32), A("Lf", 16, 16 + nf), OP.subtract)
        ts(A("sbU"), sF, 1.0 / 16, OP.mult, -0.46875, OP.add)
        cp(A("mk"), IND(A("M16x"), sU), "s")
        tt(A("RU"), IND(pF(0, 96), A("sbU")), A("mk"), OP.mult)
        sp = wide("ps4", "Z", "RU", 128)
        ts(A("upU"), sp(0, 8), 1.0 / 16, OP.mult)
        cp(A("X3"), IND(A("xs"), A("upU")), "s")
        n, jl, l0, l1 = (96, 24, 0, 8) if last else (m, m - 2, 2 * r, 2 * r + 2)
        act(A("upF", l0, l1), sp(l0, l1), bias=-cc, scale=1.0 / 16)
        if t:
            act(A("lim", 14 + 2 * t, 16 + 2 * t), A("lim", 14 + 2 * t, 16 + 2 * t), scale=0.0)
        act(A("lim", jl, jl + l1 - l0), A("cond", 9 * t + 1 + l0, 9 * t + 1 + l1), scale=BIG)
        ps = "ps1" if last else "ps7"
        thirds = ((0, 32, "s"), (32, 64, "s"), (64, 96, "v")) if last else ((0, n, "s"),)
        for b0, b1, e in thirds:
            cp(A("L1R", 16 * b0, 16 * b1), IND(A("who"), A("pN", b0, b1) if last else pS(r, m)), e)
        toW(A(ps, 256, 256 + n), "Z", "L1R", 0, 16 * n)
        ts(A("L1U", 0, n), A(ps, 256, 256 + n), 1.0 / 16, OP.mult, 272.0 - 128 * t, OP.add)
        act(A("d1b", 1, 3 * n, 3), A(ps, 256, 256 + n), bias=256.0 - cc, scale=1.0 / 16)
        if last:
            act(A("ovt"), pF(0, 96), bias=-cc)
        else:
            act(A("ovt", 0, jl), A("sob", 2, 3 * jl, 3) if t else pF(32 + 16 * r, 48 + 16 * r), bias=-128.0 if t else -cc)
            act(A("ovt", jl, n), pF(8 * t + l0, 8 * t + l1), bias=-cc)
        tt(A("d1b", 0, 3 * n, 3), A("ovt", 0, n), A("d1b", 1, 3 * n, 3), OP.subtract)
        for o, e in zip(own, "vvss"):
            cp(A("Kc", 16 + 32 * o, 48 + 32 * o), IND(A("kcs"), dl(o, 2)), e)
        if not last:
            tt(A("Psm"), IND(A("Kc"), A("LL", 0, 16)), A("Xsm"), OP.mult)
            so = quad("sqO", "ps2", "Q", [("Psm", 0, 256)])
            ts(A("SS", 16 * t, 16 * t + 16), so(0, 16), col("cf", 16), OP.add)
            send_slots("s%d" % t, A("SS", 16 * t, 16 * t + 16), "LS", 48 * t, 16)
        cp(A("cx", 0, 8), B("DL", S(4 * t, 4 * t + 4), S(0, 2)))
        cp(A("cx", 8, 16), B("DL", S(4 * t, 4 * t + 4), S(2, 4)))
        cp(A("sgR"), IND(A("dig", C, CX), A("cx", 8, 16)), "s")
        tt(A("DS", LX * t + 16, LX * t + LX), IND(A("dig"), A("cx", 0, 8)), A("sgR"), OP.add)
        DSw = A("DS", LX * t, LX * t + LX)
        if not last:
            cp(A("DJ", 0, 256), IND(DSw, A("LL", 0, 16)), "s")
            st = wide("ps0", "Z2", "DJ", 256)
            terms("s", 0, 16, st(0, 16), -262144.0, so(0, 16), col("cf", 17))
            es = tally("s", 0, 16, "LS", 48 * t)
            for h in range(2):
                ts(A("d0s", 2 + 2 * h, 40, 5), es(h, 16, 2), 0.0, OP.is_lt)
            scan(A("sos"), A("d0s"), A("d1s"))
            cp(A("sU", nb, nb + 8), A("sos", 4, 40, 5))
            cp(pF(nb, nb + 8, t + 1), A("sos", 4, 40, 5), "s")
        nu = 8 + nf
        tt(A("Pu", 0, 128), A("Kc", 16, LX), A("X3"), OP.mult)
        if nf:
            tt(A("Pu", 128, 16 * nu), IND(A("Kc"), A("LL", 16, 16 + nf)), A("xs", 16 * (32 - nf), 512), OP.mult)
            cp(A("DJ", 256, 256 + 16 * nf), IND(DSw, A("LL", 16, 16 + nf)), "s")
        su = wide("ps4", "Z", "Pu", 16 * nu)
        ts(A("SU", 24 * t, 24 * t + nu), su(0, nu), 32768.0, OP.add)
        send_slots("u%d" % t, A("SU", 24 * t, 24 * t + nu), "LU", 72 * t, nu)
        sv = quad("sqV", "ps5", "Q2", [("DS", LX * t + 16, LX * t + LX)] + ([("DJ", 256, 256 + 16 * nf)] if nf else []))
        terms("u", 0, nu, sv(0, nu), col("cf", 31), su(0, nu), col("cf", 18))
        cp(IND(A("KS"), offU), A("Kc", 16, LX))
        if last:
            for h, (h0, h1) in enumerate(halves):
                for b0 in range(h0, h1, 16):
                    tt(A("Pb", 16 * b0, 16 * b0 + 256), IND(A("KS"), A("pN", b0, b0 + 16)), A("xs", 16 * b0, 16 * b0 + 256), OP.mult)
                toW(A("ps%d" % (6 + h), 0, h1 - h0), "Z", "Pb", 16 * h0, 16 * h1)
                sb = A("SB", 96 * t + h0, 96 * t + h1)
                ts(sb, A("ps%d" % (6 + h), 0, h1 - h0), 32768.0, OP.add)
                send_slots("z%d" % h, sb, "LF", 3 * h0, h1 - h0)
        else:
            for o in range(N):
                tt(A("Pb", 16 * m * o, 16 * m * o + 16 * m), IND(A("KS"), pS(o, m)), B("xsP", o, S(0, 16 * m)), OP.mult)
            toW(A("ps6", 0, 4 * m), "Z", "Pb", 0, 64 * m)
            ts(A("SB", 96 * t, 96 * t + 4 * m), A("ps6", 0, 4 * m), 32768.0, OP.add)
            cuts = [0, ne // 4, ne // 2, ne]
            send("b%d" % t, [([c], eng[cuts[c]:cuts[c + 1]], A("SB", 96 * t + m * own[c], 96 * t + m * own[c] + m),
                              [A("LB", 72 * t + m * c, 72 * t + m * c + m)]) for c in range(3)], [A("LB", 72 * t, 72 * t + 3 * m)], ne)
        eu = tally("u", 0, nu, "LU", 72 * t)
        tt(A("w0", 1, 16, 2), eu(0, 8), A("c18", 8 * t, nb), OP.is_gt)
        scan(A("wg"), A("w0"), o1)
        cp(A("offV"), A("wg", 1, 16, 2))
        cp(IND(A("ov"), A("offV")), tags)
        if last:
            toW(A("ps2", 128, 224), "Z1", "ov", 0, V)
            swaps("d0b", "d1b", 0, A("ps2", 128, 152), t)
            swaps("d0b", "d1b", 32, A("ps2", 160, 224), t)
        else:
            past = [("ov", 128 * u + 32 * r, 128 * u + 32 * r + 32) for u in range(t)]
            sw = quad("sqW", "ps5", "Q1", [("ov", 512 + 256 * r, 768 + 256 * r)] + past + ([("ov", 512 - 16 * nf, 512)] if nf else []))
            swaps("d0b", "d1b", 0, sw(0, jl), t)
        if nf:
            swaps("d0u", "d1u", 0, sw(jl, jl + nf), t)
            ts(A("d0u", 1, 3 * nf, 3), eu(8, nu), 0.0, OP.is_lt)
            scan(A("sou", 0, 3 * nf), A("d0u", 0, 3 * nf), A("d1u", 0, 3 * nf))
            lists(t + 1, "sou", 2, 3, cc)
            act(pF(32 - nf, 32, t + 1), A("sou", 2, 3 * nf, 3), bias=cc)
        for b0, b1, e in thirds:
            cp(A("DB", 16 * b0, 16 * b1), IND(DSw, A("L1U", b0, b1)), e)
        pt = "ps0" if last else "ps7"
        toW(A(pt, 0, n), "Z2", "DB", 0, 16 * n)
        j0, j1 = 3 * jl + 2, 3 * (jl + l1 - l0)
        m3 = A("w0", 2 * l0 + 1, 2 * l1, 2)
        act(A("d0b", j0, j1, 3), m3, bias=1.0, scale=-1.0)
        tt(A("d1b", j0, j1, 3), A("upF", l0, l1), m3, OP.mult)
        for h, (b0, b1) in enumerate(halves if last else ((0, n),)):
            terms("b", b0, b1 - b0, A(pt, b0, b1), -262144.0, A("ps%d" % (6 + h), 0, b1 - b0) if last else A("ps6", m * r, m * r + m))
            eb = tally("b", b0, b1 - b0, *(("LF", 3 * b0) if last else ("LB", 72 * t)))
            tt(A("d0b", 3 * b0 + 1, 3 * b1, 3), eb(b0, b1), A("lim", b0, b1), OP.is_lt)
            scan(A("sob", 3 * b0, 3 * b1), A("d0b", 3 * b0, 3 * b1), A("d1b", 3 * b0, 3 * b1))
            if last:
                ts(A("ypo", b0, b1), A("sob", 3 * b0 + 2, 3 * b1, 3), cc, OP.add)
                dma("ys"[h], "y%d" % h, T.yp[:, b0:b1], A("ypo", b0, b1), 24576)
        if not last:
            mine, slots = pS(r, m, t + 1), S(4 * t + 4, 4 * t + 8)
            ts(mine, A("sob", 2, 3 * m, 3), cc, OP.add)
            send_all("p%d" % t, mine, [mine] * 3, [pS(o, m, t + 1) for o in others])
            cp(pF(32, 96, t + 1), B("pS", slots, S(0, 16)))
            for u in range(t + 1):
                cp(pF(8 * u, 8 * u + 8, t + 1), B("pS", slots, S(16 + 2 * u, 18 + 2 * u)))
            if t == R - 2:
                cp(A("pN"), pF(0, 96, t + 1))
            else:
                cp(B("pS", slots, S(m, m + 2)), A("sos", 4, 40, 5), also=[pS(o, m, t + 1) for o in others])
    toW(A("ps5", 0, 36), "Z3", "DS", 0, 4 * LX)
    act(A("yc1"), A("ps5", 0, 36), bias=1.0)
    tt(B("ycq"), A("yc1"), A("cond"), OP.mult)
    act(A("yco"), B("ycq", ALL, S(1, 9)), bias=-1.0)
    dma("y", "yc", T.yc[:], A("yco"), 16384)

    start = planned(ops)
    order = sorted(range(len(ops)), key=lambda i: (start[i], i))

    know, snap, cnt, plan = dict((e, {}) for e in Q), {}, dict((e, 0) for e in Q), []
    for pos, i in enumerate(order):
        e, fns, deps, _, ev = ops[i]
        if e == "l":
            snap[i] = (ev, {ev[0]: ev[1]}, pos)
        if e not in Q:
            continue
        waits = []
        for m in sorted([m for m in deps if m in snap and not (ops[m][0] == e == "t")], key=lambda m: -snap[m][2]):
            k, v = snap[m][0]
            if know[e].get(k, -1) < v:
                waits.append((k, v))
                for k2, v2 in snap[m][1].items():
                    know[e][k2] = max(know[e].get(k2, -1), v2)
        if ev is None:
            ev = (e, cnt[e])
            cnt[e] += 1
            snap[i] = (ev, dict(know[e], **{e: ev[1]}), pos)
        plan.append((e, fns, waits, ev))
    wanted = set(w for o in plan for w in o[2] if w[0] in CS)
    num, tot = {}, dict((e, 0) for e in CS)
    for e, fns, waits, ev in plan:
        if ev in wanted:
            tot[e] += 1
            num[ev] = tot[e]
    for e, fns, waits, ev in plan:
        for w in waits:
            Q[e].wait_ge(T.sem[CS[w[0]]] if w[0] in CS else T.sem[w[0]], num[w] if w[0] in CS else w[1])
        for fn in fns:
            ins = fn()
        if ev in wanted:
            ins.then_inc(T.sem[CS[e]], 1)
        elif ev != "send" and ev[0] not in CS:
            ins.then_inc(T.sem[ev[0]], 16)
    g.wait_ge(T.sem.ls, nloc[0])
    g.sync.wait_ge(T.sem.dy0, 16)
    g.scalar.wait_ge(T.sem.dy1, 16)
    g.sync.wait_ge(T.sem.dyc, 16)
